import numpy as np
import ml_dtypes


def mxq(x, axis, fmt="e4m3"):
    dtype, down = {"e4m3": (ml_dtypes.float8_e4m3fn, 7), "e5m2": (ml_dtypes.float8_e5m2, 14)}[fmt]
    v = np.moveaxis(np.asarray(x, np.float32).astype(ml_dtypes.bfloat16).astype(np.float64), axis, -1)
    blocks = v.reshape(v.shape[:-1] + (-1, 32))
    amax = np.abs(blocks).max(-1, keepdims=True)
    byte = np.maximum(np.where(amax > 0, np.frexp(amax)[1] - 1 + 127, 0) - down, 1)
    scale = np.exp2(byte - 127.0)
    codes = (blocks / scale).astype(np.float32).astype(dtype).astype(np.float64)
    return np.moveaxis((codes * scale).reshape(v.shape), -1, axis)


WIDE = False


def mx_kscale(k):
    if not WIDE:
        return np.ones(k)
    levels = np.array([10, -10, 5, -5, 0])
    if k % 512:
        return np.exp2(np.random.permutation(np.resize(levels, k // 32))).repeat(32)
    a = np.empty((k // 512, 16))
    for p in range(k // 512):
        a[p, :8] = np.random.permutation(np.resize(levels, 8))
        for g in range(8):
            far = levels[np.abs(levels - a[p, g]) >= 10]
            a[p, g + 8] = far[np.random.randint(len(far))]
    return np.exp2(a.ravel()).repeat(32)


def f64(x):
    return np.asarray(x).astype(np.float64)


def striped(idx):
    return np.tile(idx.reshape(-1, 16).T, (8, 1)).astype(np.uint16)


def unstriped(offs):
    return offs[:16].T.reshape(-1).astype(np.int64)


E2M1 = np.array([0.0, 0.5, 1.0, 1.5, 2.0, 3.0, 4.0, 6.0, -0.0, -0.5, -1.0, -1.5, -2.0, -3.0, -4.0, -6.0])


def pack_weight(w, fmt):
    k, n = w.shape
    w = f64(np.asarray(w, np.float32).astype(ml_dtypes.bfloat16)).reshape(k // 32, 32, n)
    amax = np.abs(w).max(1)
    if fmt == "e4m3":
        byte = np.frexp(amax)[1] - 1 + 127 - 7
    else:
        mant, ex = np.frexp(amax / 6.0)
        byte = np.where(mant > 0.5, ex, ex - 1) + 127
    byte = np.clip(np.where(amax > 0, byte, 1), 1, 254)
    scaled = (w * np.exp2(127.0 - byte)[:, None, :]).reshape(k, n).astype(np.float32)
    by_word = np.ascontiguousarray(scaled.reshape(k // 512, 128, 4, n).transpose(0, 1, 3, 2))
    if fmt == "e4m3":
        words = by_word.astype(ml_dtypes.float8_e4m3fn).view(np.uint8)
    else:
        c = by_word.astype(ml_dtypes.float4_e2m1fn).view(np.uint8) & 0xF
        words = (c[..., 0::2] | (c[..., 1::2] << 4)).reshape(k // 512, 128, 2 * n)
    return np.ascontiguousarray(words), np.ascontiguousarray(byte.astype(np.uint8).reshape(k // 512, 16, n))


def unpack_weight(words, scales, fmt):
    g, _, n = scales.shape
    words = np.ascontiguousarray(words).reshape(g, 128, n, -1)
    if fmt == "e4m3":
        vals = words.view(ml_dtypes.float8_e4m3fn).astype(np.float64)
    else:
        nib = np.empty((g, 128, n, 4), np.uint8)
        nib[..., 0::2] = words & 0xF
        nib[..., 1::2] = words >> 4
        vals = E2M1[nib]
    vals = vals * np.repeat(np.exp2(scales.astype(np.float64) - 127.0), 8, axis=1)[..., None]
    return vals.transpose(0, 1, 3, 2).reshape(g * 512, n)


def relu2(v):
    return np.maximum(v, 0.0) ** 2


def sigmoid(v):
    return 1.0 / (1.0 + np.exp(-np.maximum(v, -700.0)))


K, T, E, C, H, N, TOP = 512, 512, 16, 128, 512, 512, 4


def by_expert(wq, xq):
    return np.concatenate([wq[e].T @ xq[:, e * C:(e + 1) * C] for e in range(E)], axis=1)


def setup_inputs():
    n = np.random.standard_normal
    s = mx_kscale(K)
    u = mx_kscale(H)
    deal = np.repeat(np.arange(E), C).reshape(TOP, T)[:, np.random.permutation(T)]
    deal = np.take_along_axis(deal, np.argsort(np.random.rand(TOP, T), axis=0), axis=0)
    for _ in range(8):
        s_, t_ = np.random.permutation(T).reshape(2, -1); r = np.random.randint(TOP, size=T // 2); x, y = deal[r, s_].copy(), deal[r, t_].copy()
        ok = ~((deal[:, s_] == y).any(0) | (deal[:, t_] == x).any(0)); deal[r[ok], s_[ok]] = y[ok]; deal[r[ok], t_[ok]] = x[ok]
    order = np.argsort(deal.reshape(-1) + 0.5 * np.random.rand(TOP * T))
    slot_token = order % T; pos = np.empty(TOP * T, np.int64); pos[order] = np.arange(TOP * T); pos = pos.reshape(TOP, T)
    g = np.random.uniform(0.5, 1.5, (TOP, T)); g = g / g.sum(0)
    x = pack_weight(n((K, T)) * s[:, None], "e4m3")
    wg = pack_weight(n((K, N)) / np.sqrt(K) / s[:, None], "e2m1")
    w1 = [pack_weight(m, "e2m1") for m in n((E, K, H)) / np.sqrt(K) / s[None, :, None] * u]
    w2 = [pack_weight(m, "e2m1") for m in n((E, H, N)) / np.sqrt(H) / u[None, :, None] ** 2]
    return {
        "x_words": x[0],
        "x_scales": x[1],
        "wg_words": wg[0],
        "wg_scales": wg[1],
        "w1_words": np.stack([m[0] for m in w1]),
        "w1_scales": np.stack([m[1] for m in w1]),
        "w2_words": np.stack([m[0] for m in w2]),
        "w2_scales": np.stack([m[1] for m in w2]),
        "gate": np.stack([np.tile(r, (128, 1)) for r in g]).astype(np.float32),
        "offs": striped(slot_token),
        "pos1": striped(pos[0]),
        "pos2": striped(pos[1]),
        "pos3": striped(pos[2]),
        "pos4": striped(pos[3]),
    }


def reference(x_words, x_scales, wg_words, wg_scales, w1_words, w1_scales, w2_words, w2_scales, gate, offs, pos1, pos2, pos3, pos4):
    wg = unpack_weight(wg_words, wg_scales, "e2m1")
    w1 = np.stack([unpack_weight(w1_words[e], w1_scales[e], "e2m1") for e in range(E)])
    w2 = np.stack([unpack_weight(w2_words[e], w2_scales[e], "e2m1") for e in range(E)])
    idx = unstriped(offs)
    x = unpack_weight(x_words, x_scales, "e4m3")
    o = sigmoid(wg.T @ x)
    h = relu2(by_expert(w1, x[:, idx]))
    y = by_expert(w2, mxq(h, 0, "e4m3"))
    c = sum(f64(gate[r, :1]) * y[:, unstriped(p)] for r, p in enumerate((pos1, pos2, pos3, pos4)))
    return o * c

@@ -1,0 +1,250 @@
+from contextlib import ExitStack
+
+import concourse.mybir as mybir
+from concourse.masks import make_identity
+
+F32 = mybir.dt.float32
+BF16 = mybir.dt.bfloat16
+I32 = mybir.dt.int32
+U32 = mybir.dt.uint32
+U16 = mybir.dt.uint16
+U8 = mybir.dt.uint8
+FP8X4 = mybir.dt.float8_e4m3fn_x4
+FP4X4 = mybir.dt.float4_e2m1fn_x4
+ACT = mybir.ActivationFunctionType
+ALU = mybir.AluOpType
+
+P = 128
+T, E, C, H, N, TOP = 512, 16, 128, 512, 512, 4
+S = E * C
+NB = N // P
+FLOPS = 2415919104
+
+W1_GROUPS = ((0, 2), (2, 6), (6, 11), (11, 16))
+STREAM_BUFS = 6
+W1S_GROUPS = ((0, 2), (2, 8), (8, 16))
+GATHERS = ((0, 1), (1, 2), (2, 4), (4, 6), (6, 8), (8, 10), (10, 12), (12, 14), (14, 16))
+GATHER_BUFS = 4
+RELU_ON_VECTOR = (3, 5, 7, 9, 11, 12, 13, 14, 15)
+LAST = 128
+QUANT = [(0, 2), (2, 4), (4, 6), (6, 8), (8, 10), (10, 12), (12, 14), (14, 15), (15, 16)]
+FIRST_GROUPS = ((0, 4), (4, 8), (8, 12), (12, 15), (15, 16))
+GROUPS = ((0, 4), (4, 8), (8, 12), (12, 16))
+
+
+def tile_moe_ogt_relu2_sigmoid_kernel(
+    tc, x_words, x_scales, wg_words, wg_scales, w1_words, w1_scales, w2_words, w2_scales,
+    gate, offs, pos1, pos2, pos3, pos4, out,
+):
+    nc = tc.nc
+    with ExitStack() as ctx:
+        keep = ctx.enter_context(tc.tile_pool(name="keep", bufs=1))
+        work = ctx.enter_context(tc.tile_pool(name="work", bufs=1))
+        psum = ctx.enter_context(tc.psum_pool(name="psum", bufs=1))
+
+        def plane(name, cols, eng):
+            t = keep.tile([P, cols], U8, name=name, align_bytes=64)
+            eng.memset(t[:].bitcast(I32), 0)
+            return t
+
+        def load_scales(t, src):
+            ne, w = src.shape[0], src.shape[2]
+            rows = src.rearrange("e (q r) n -> r q e n", r=4)
+            dst = t[:].bitcast(I32).rearrange("p (e n) -> p e n", e=ne)
+            for r in range(4):
+                nc.sync.dma_start(out=dst[r:P:32, :, :], in_=rows[r])
+
+        def load_words(name, src):
+            ne, w = src.shape[0], src.shape[2]
+            t = work.tile([P, ne * w * 4], U8, name=name, tag="stream", bufs=STREAM_BUFS, align_bytes=64)
+            nc.sync.dma_start(out=t[:].bitcast(I32).rearrange("p (e n) -> p e n", e=ne), in_=src.rearrange("e p n -> p e n"))
+            return t
+
+        xs = plane("xs", T, nc.gpsimd)
+        w1s = [plane("w1s%d" % i, (b - a) * H, nc.vector) for i, (a, b) in enumerate(W1S_GROUPS)]
+        ident = keep.tile([P, P], F32, name="ident")
+        make_identity(nc, ident[:])
+        warm = keep.tile([P, 1], F32, name="warm")
+        nc.scalar.activation(warm[:], ident[:, 0:1], ACT.Sigmoid)
+        w2s = [plane("w2s%d" % i, E * 256, nc.gpsimd) for i in range(2)]
+        wgs = plane("wgs", N, nc.gpsimd)
+
+        w1w_d = w1_words.rearrange("e o p n -> (e o) p n").bitcast(I32)
+        w2w_d = w2_words.rearrange("e o p n -> (e o) p n").bitcast(I32)
+        w1s_d = w1_scales.rearrange("e o b n -> (e o) b n").bitcast(I32)
+        w2s_d = w2_scales.rearrange("e o b n -> (e o) b n").bitcast(I32)
+
+        offs_t = keep.tile([P, S // 16], U16, name="offs_t")
+        nc.sync.dma_start(offs_t[:], offs)
+        xw = keep.tile([P, T], I32, name="xw", align_bytes=64)
+        nc.sync.dma_start(out=xw[:], in_=x_words[0].rearrange("p t d -> p (t d)").bitcast(I32))
+        w1w = []
+        for g, (a, b) in enumerate(W1_GROUPS):
+            w1w.append(load_words("w1w%d" % g, w1w_d[a:b]))
+            if g == 0:
+                load_scales(xs, x_scales.bitcast(I32))
+                load_scales(w1s[0], w1s_d[0:2])
+            elif g < 3:
+                load_scales(w1s[g], w1s_d[W1S_GROUPS[g][0] : W1S_GROUPS[g][1]])
+        load_scales(w2s[0], w2s_d[:, :, 0:64])
+        w2w = [[load_words("w2w0_%d" % g, w2w_d[8 * g : 8 * g + 8, :, 0:128]) for g in range(2)]]
+        pos_t = []
+        for r, pos in enumerate((pos1, pos2, pos3, pos4)):
+            pt = keep.tile([P, T // 16], U16, name="pos_t%d" % r)
+            nc.sync.dma_start(pt[:], pos)
+            pos_t.append(pt)
+        load_scales(wgs, wg_scales.bitcast(I32))
+        load_scales(w2s[1], w2s_d[:, :, 64:128])
+
+        hq = keep.tile([P, S], U32, name="hq", align_bytes=64)
+        hs = keep.tile([P, S], U8, name="hs", align_bytes=64)
+        y = [keep.tile([P, S], F32, name="y%d" % nb) for nb in range(NB)]
+
+        xg, sg = {}, {}
+
+        def gather(i):
+            a, b = GATHERS[i]
+            o = offs_t[:, a * 8 : b * 8]
+            xg[i] = work.tile([P, (b - a) * C], U32, name="xg", tag="xg", bufs=GATHER_BUFS, align_bytes=64)
+            sg[i] = work.tile([P, (b - a) * C], U8, name="sg", tag="sg", bufs=GATHER_BUFS, align_bytes=64)
+            nc.vector.tensor_copy(sg[i][:], xs[:].indirect(o))
+            nc.vector.tensor_copy(xg[i][:], xw[:].bitcast(U32).indirect(o))
+
+        h = [keep.tile([P, (b - a) * C * 4], BF16, name="h%d" % a, align_bytes=64) for a, b in QUANT]
+
+        def find(groups, e):
+            for i, (a, b) in enumerate(groups):
+                if a <= e < b:
+                    return i, e - a
+
+        relu_t = {}
+
+        def layer1(e):
+            xi, xe = find(GATHERS, e)
+            sl = slice(xe * C, (xe + 1) * C)
+            gi, ge = find(W1_GROUPS, e)
+            si, se = find(W1S_GROUPS, e)
+            v = psum.tile([P, H], F32, name="v", tag="bankA", bufs=3)
+            nc.tensor.matmul_mx(
+                out=v[:], lhsT=xg[xi][:, sl].bitcast(FP8X4), lhsT_scale=sg[xi][:, sl],
+                rhs=w1w[gi][:, ge * 1024 : (ge + 1) * 1024].bitcast(FP4X4), rhs_scale=w1s[si][:, se * H : (se + 1) * H],
+                start=True, stop=True,
+            )
+            rl = work.tile([P, 4, P], F32, name="rl", tag="rl", bufs=3)
+            src = v[:].rearrange("p (m t) -> p t m", t=4)
+            if e not in RELU_ON_VECTOR:
+                nc.scalar.activation(rl[:], src, ACT.Relu)
+            else:
+                nc.vector.tensor_scalar(rl[:], src, 0.0, None, ALU.max)
+            relu_t[e] = rl
+
+        def turn(e):
+            rt = psum.tile([P, 4, C], F32, name="rt", tag="bankB", bufs=3)
+            for t in range(4):
+                nc.tensor.transpose(rt[:, t, :], relu_t[e][:, t, :], ident[:])
+            hi, he = find(QUANT, e)
+            nc.scalar.activation(h[hi][:, he * H : (he + 1) * H].rearrange("p (s t) -> p s t", t=4), rt[:].rearrange("p t s -> p s t"), ACT.Square)
+
+        def quantise(a, b):
+            sl = slice(a * C, b * C)
+            nc.vector.quantize_mx(out=hq[:, sl].bitcast(FP8X4), scales=hs[:, sl], in_=h[QUANT.index((a, b))][:])
+
+        def layer2(nb, a, b):
+            yb = psum.tile([P, (b - a) * C], F32, name="yb", tag="bankC", bufs=2)
+            half, sub = divmod(nb, 2)
+            for e in range(a, b):
+                j = e - a
+                sl = slice(e * C, (e + 1) * C)
+                w0 = (e % 8) * 512 + sub * 256
+                s0 = e * 256 + sub * P
+                nc.tensor.matmul_mx(
+                    out=yb[:, j * C : (j + 1) * C],
+                    lhsT=w2w[half][e // 8][:, w0 : w0 + 256].bitcast(FP4X4), lhsT_scale=w2s[half][:, s0 : s0 + P],
+                    rhs=hq[:, sl].bitcast(FP8X4), rhs_scale=hs[:, sl], start=True, stop=True,
+                )
+            nc.scalar.copy(y[nb][:, a * C : b * C], yb[:])
+
+        for i in range(GATHER_BUFS):
+            gather(i)
+        for step in range(E + 2):
+            for i, (a, b) in enumerate(GATHERS):
+                if b == step and i + GATHER_BUFS < len(GATHERS):
+                    gather(i + GATHER_BUFS)
+            if step < E:
+                layer1(step)
+            if 0 <= step - 1 < E:
+                turn(step - 1)
+            for a, b in QUANT:
+                if b - 1 == step - 2:
+                    quantise(a, b)
+            for a, b in FIRST_GROUPS:
+                if b - 1 == step - 2:
+                    layer2(0, a, b)
+
+        gate_t = []
+        for pair in range(2):
+            gt = work.tile([P, 2, T], F32, name="gt", tag="stream", bufs=STREAM_BUFS, align_bytes=64)
+            nc.sync.dma_start(out=gt[:], in_=gate[2 * pair : 2 * pair + 2].rearrange("r p t -> p r t"))
+            gate_t.extend([gt[:, 0, :], gt[:, 1, :]])
+        w2w.append([load_words("w2w1_0", w2w_d[0:8, :, 128:256])])
+        wgw = load_words("wgw", wg_words.bitcast(I32))
+        w2w[1].append(load_words("w2w1_1", w2w_d[8:16, :, 128:256]))
+
+        o_t = {}
+
+        def out_gate(nb):
+            z = psum.tile([P, T], F32, name="z", tag="bankC", bufs=2)
+            nc.tensor.matmul_mx(
+                out=z[:], lhsT=wgw[:, nb * 256 : (nb + 1) * 256].bitcast(FP4X4), lhsT_scale=wgs[:, nb * P : (nb + 1) * P],
+                rhs=xw[:].bitcast(FP8X4), rhs_scale=xs[:], start=True, stop=True,
+            )
+            o = work.tile([P, T], F32, name="o", tag="o", bufs=NB)
+            nc.scalar.activation(o[:], z[:], ACT.Sigmoid)
+            o_t[nb] = o
+
+        c_t = {}
+
+        def fetch(nb, t0, t1, r):
+            pr = work.tile([P, t1 - t0], F32, name="pr", tag="pr", bufs=8)
+            nc.vector.tensor_tensor(pr[:], y[nb][:].indirect(pos_t[r][:, t0 // 16 : t1 // 16]), gate_t[r][:, t0:t1], ALU.mult)
+            return pr
+
+        def combine(nb, t0, t1):
+            parts = [fetch(nb, t0, t1, r) for r in range(TOP)]
+            blocks = (t1 - t0) // P
+            ct = psum.tile([P, blocks, P], F32, name="ct", tag="bankA", bufs=3)
+            for tb in range(blocks):
+                for r in range(TOP):
+                    nc.tensor.matmul(ct[:, tb, :], parts[r][:, tb * P : (tb + 1) * P], ident[:], start=r == 0, stop=r == TOP - 1, is_transpose=True)
+            cs = work.tile([P, blocks, P], F32, name="cs", tag="cs", bufs=2)
+            nc.scalar.copy(cs[:], ct[:])
+            c = psum.tile([P, t1 - t0], F32, name="c", tag="bankB", bufs=3)
+            for tb in range(blocks):
+                nc.tensor.transpose(c[:, tb * P : (tb + 1) * P], cs[:, tb, :], ident[:])
+            c_t[nb, t0] = c
+
+        def finish(nb, t0, t1):
+            res = work.tile([P, t1 - t0], F32, name="res", tag="res", bufs=NB + 1)
+            nc.vector.tensor_tensor(res[:], c_t[nb, t0][:], o_t[nb][:, t0:t1], ALU.mult)
+            nc.sync.dma_start(out=out[nb * P : (nb + 1) * P, t0:t1], in_=res[:])
+
+        pieces = [(nb, 0, T) for nb in range(NB - 1)] + [(NB - 1, 0, T - LAST)]
+        for i, (nb, t0, t1) in enumerate(pieces):
+            if nb + 1 < NB:
+                for a, b in GROUPS:
+                    layer2(nb + 1, a, b)
+            out_gate(nb)
+            combine(nb, t0, t1)
+            if i > 0:
+                finish(*pieces[i - 1])
+
+        nb, t0 = NB - 1, T - LAST
+        parts = [fetch(nb, t0, T, r) for r in range(TOP)]
+        sums = work.tile([P, 3, LAST], F32, name="sums")
+        nc.vector.tensor_tensor(sums[:, 0, :], parts[0][:], parts[1][:], ALU.add)
+        nc.vector.tensor_tensor(sums[:, 1, :], parts[2][:], parts[3][:], ALU.add)
+        nc.vector.tensor_tensor(sums[:, 2, :], sums[:, 0, :], sums[:, 1, :], ALU.add)
+        res = work.tile([P, LAST], F32, name="res", tag="res", bufs=NB + 1)
+        nc.vector.tensor_tensor(res[:], sums[:, 2, :], o_t[nb][:, t0:T], ALU.mult)
+        nc.sync.dma_start(out=out[nb * P : (nb + 1) * P, t0:T], in_=res[:])
+        finish(*pieces[-1])

@@ -20,12 +20,18 @@ S = E * C
 NB = N // P
 FLOPS = 2415919104
 
-W1_GROUPS = ((0, 2), (2, 6), (6, 11), (11, 16))
-STREAM_BUFS = 6
-W1S_GROUPS = ((0, 2), (2, 8), (8, 16))
+W1_GROUPS = ((0, 2), (2, 5), (5, 10), (10, 16))
+
+W1S_GROUPS = ((0, 2), (2, 7), (7, 16))
 GATHERS = ((0, 1), (1, 2), (2, 4), (4, 6), (6, 8), (8, 10), (10, 12), (12, 14), (14, 16))
-GATHER_BUFS = 4
-RELU_ON_VECTOR = (3, 5, 7, 9, 11, 12, 13, 14, 15)
+GATHER_BUFS = 5
+RELU_FROM, RELU_ALL = 5, 8
+RELU_ON_VECTOR = [e for e in range(RELU_FROM, E) if e % 2 == 1 or e >= RELU_ALL]
+REPEATS = range(0, 0)
+V_BANKS = 3
+PR_SETS = 3
+EVAC_V = 8
+L2_AFTER = (9, 11, 13, 14, 15)
 LAST = 128
 QUANT = [(0, 2), (2, 4), (4, 6), (6, 8), (8, 10), (10, 12), (12, 14), (14, 15), (15, 16)]
 FIRST_GROUPS = ((0, 4), (4, 8), (8, 12), (12, 15), (15, 16))
@@ -56,7 +62,7 @@ def tile_moe_ogt_relu2_sigmoid_kernel(
 
         def load_words(name, src):
             ne, w = src.shape[0], src.shape[2]
-            t = work.tile([P, ne * w * 4], U8, name=name, tag="stream", bufs=STREAM_BUFS, align_bytes=64)
+            t = keep.tile([P, ne * w * 4], U8, name=name, align_bytes=64)
             nc.sync.dma_start(out=t[:].bitcast(I32).rearrange("p (e n) -> p e n", e=ne), in_=src.rearrange("e p n -> p e n"))
             return t
 
@@ -83,8 +89,7 @@ def tile_moe_ogt_relu2_sigmoid_kernel(
             w1w.append(load_words("w1w%d" % g, w1w_d[a:b]))
             if g == 0:
                 load_scales(xs, x_scales.bitcast(I32))
-                load_scales(w1s[0], w1s_d[0:2])
-            elif g < 3:
+            if g < len(W1S_GROUPS):
                 load_scales(w1s[g], w1s_d[W1S_GROUPS[g][0] : W1S_GROUPS[g][1]])
         load_scales(w2s[0], w2s_d[:, :, 0:64])
         w2w = [[load_words("w2w0_%d" % g, w2w_d[8 * g : 8 * g + 8, :, 0:128]) for g in range(2)]]
@@ -93,22 +98,40 @@ def tile_moe_ogt_relu2_sigmoid_kernel(
             pt = keep.tile([P, T // 16], U16, name="pos_t%d" % r)
             nc.sync.dma_start(pt[:], pos)
             pos_t.append(pt)
-        load_scales(wgs, wg_scales.bitcast(I32))
-        load_scales(w2s[1], w2s_d[:, :, 64:128])
 
         hq = keep.tile([P, S], U32, name="hq", align_bytes=64)
         hs = keep.tile([P, S], U8, name="hs", align_bytes=64)
         y = [keep.tile([P, S], F32, name="y%d" % nb) for nb in range(NB)]
 
+        gate_t = []
+        for pair in range(2):
+            gt = keep.tile([P, 2, T], F32, name="gt%d" % pair)
+            nc.sync.dma_start(out=gt[:], in_=gate[2 * pair : 2 * pair + 2].rearrange("r p t -> p r t"))
+            gate_t.extend([gt[:, 0, :], gt[:, 1, :]])
+        load_scales(w2s[1], w2s_d[:, :, 64:128])
+        w2w.append([load_words("w2w1_%d" % g, w2w_d[8 * g : 8 * g + 8, :, 128:256]) for g in (1, 0)][::-1])
+        load_scales(wgs, wg_scales.bitcast(I32))
+        wgw = load_words("wgw", wg_words.bitcast(I32))
+
+        banks = [psum.tile([P, 512], F32, name="bank%d" % b) for b in range(8)]
+        turns = []
+
+        def next_bank():
+            turns.append(0)
+            return banks[V_BANKS + (len(turns) - 1) % (8 - V_BANKS)]
+
+        xg_ring = [keep.tile([P, 3 * C], U32, name="xg%d" % i, align_bytes=64) for i in range(GATHER_BUFS)]
+        sg_ring = [keep.tile([P, 3 * C], U8, name="sg%d" % i, align_bytes=64) for i in range(GATHER_BUFS)]
+        rl_ring = [keep.tile([P, H], F32, name="rl%d" % i) for i in range(4)]
         xg, sg = {}, {}
 
         def gather(i):
             a, b = GATHERS[i]
             o = offs_t[:, a * 8 : b * 8]
-            xg[i] = work.tile([P, (b - a) * C], U32, name="xg", tag="xg", bufs=GATHER_BUFS, align_bytes=64)
-            sg[i] = work.tile([P, (b - a) * C], U8, name="sg", tag="sg", bufs=GATHER_BUFS, align_bytes=64)
-            nc.vector.tensor_copy(sg[i][:], xs[:].indirect(o))
-            nc.vector.tensor_copy(xg[i][:], xw[:].bitcast(U32).indirect(o))
+            xg[i] = xg_ring[i % GATHER_BUFS][:, 0 : (b - a) * C]
+            sg[i] = sg_ring[i % GATHER_BUFS][:, 0 : (b - a) * C]
+            nc.vector.tensor_copy(sg[i], xs[:].indirect(o))
+            nc.vector.tensor_copy(xg[i], xw[:].bitcast(U32).indirect(o))
 
         h = [keep.tile([P, (b - a) * C * 4], BF16, name="h%d" % a, align_bytes=64) for a, b in QUANT]
 
@@ -124,35 +147,36 @@ def tile_moe_ogt_relu2_sigmoid_kernel(
             sl = slice(xe * C, (xe + 1) * C)
             gi, ge = find(W1_GROUPS, e)
             si, se = find(W1S_GROUPS, e)
-            v = psum.tile([P, H], F32, name="v", tag="bankA", bufs=3)
-            nc.tensor.matmul_mx(
-                out=v[:], lhsT=xg[xi][:, sl].bitcast(FP8X4), lhsT_scale=sg[xi][:, sl],
-                rhs=w1w[gi][:, ge * 1024 : (ge + 1) * 1024].bitcast(FP4X4), rhs_scale=w1s[si][:, se * H : (se + 1) * H],
-                start=True, stop=True,
-            )
-            rl = work.tile([P, 4, P], F32, name="rl", tag="rl", bufs=3)
+            v = banks[e % V_BANKS]
+            for rep in range(2 if e in REPEATS else 1):
+                nc.tensor.matmul_mx(
+                    out=v[:], lhsT=xg[xi][:, sl].bitcast(FP8X4), lhsT_scale=sg[xi][:, sl],
+                    rhs=w1w[gi][:, ge * 1024 : (ge + 1) * 1024].bitcast(FP4X4), rhs_scale=w1s[si][:, se * H : (se + 1) * H],
+                    start=True, stop=True,
+                )
+            rl = rl_ring[e % 4][:].rearrange("p (t m) -> p t m", t=4)
             src = v[:].rearrange("p (m t) -> p t m", t=4)
             if e not in RELU_ON_VECTOR:
-                nc.scalar.activation(rl[:], src, ACT.Relu)
+                nc.scalar.activation(rl, src, ACT.Relu)
             else:
-                nc.vector.tensor_scalar(rl[:], src, 0.0, None, ALU.max)
+                nc.vector.tensor_scalar(rl, src, 0.0, None, ALU.max)
             relu_t[e] = rl
 
         def turn(e):
-            rt = psum.tile([P, 4, C], F32, name="rt", tag="bankB", bufs=3)
+            rt = next_bank()[:].rearrange("p (t s) -> p t s", t=4)
             for t in range(4):
                 nc.tensor.transpose(rt[:, t, :], relu_t[e][:, t, :], ident[:])
             hi, he = find(QUANT, e)
-            nc.scalar.activation(h[hi][:, he * H : (he + 1) * H].rearrange("p (s t) -> p s t", t=4), rt[:].rearrange("p t s -> p s t"), ACT.Square)
+            nc.scalar.activation(h[hi][:, he * H : (he + 1) * H].rearrange("p (s t) -> p s t", t=4), rt.rearrange("p t s -> p s t"), ACT.Square)
 
         def quantise(a, b):
             sl = slice(a * C, b * C)
             nc.vector.quantize_mx(out=hq[:, sl].bitcast(FP8X4), scales=hs[:, sl], in_=h[QUANT.index((a, b))][:])
 
-        def layer2(nb, a, b):
-            yb = psum.tile([P, (b - a) * C], F32, name="yb", tag="bankC", bufs=2)
+        def layer2(nb, a, b, bank, on_vector=False):
+            yb = bank[:, 0 : (b - a) * C]
             half, sub = divmod(nb, 2)
-            for e in range(a, b):
+            for e in reversed(range(a, b)) if nb else range(a, b):
                 j = e - a
                 sl = slice(e * C, (e + 1) * C)
                 w0 = (e % 8) * 512 + sub * 256
@@ -162,8 +186,12 @@ def tile_moe_ogt_relu2_sigmoid_kernel(
                     lhsT=w2w[half][e // 8][:, w0 : w0 + 256].bitcast(FP4X4), lhsT_scale=w2s[half][:, s0 : s0 + P],
                     rhs=hq[:, sl].bitcast(FP8X4), rhs_scale=hs[:, sl], start=True, stop=True,
                 )
-            nc.scalar.copy(y[nb][:, a * C : b * C], yb[:])
+            if on_vector:
+                nc.vector.tensor_copy(y[nb][:, a * C : b * C], yb)
+            else:
+                nc.scalar.copy(y[nb][:, a * C : b * C], yb)
 
+        first_banks = []
         for i in range(GATHER_BUFS):
             gather(i)
         for step in range(E + 2):
@@ -177,74 +205,63 @@ def tile_moe_ogt_relu2_sigmoid_kernel(
             for a, b in QUANT:
                 if b - 1 == step - 2:
                     quantise(a, b)
-            for a, b in FIRST_GROUPS:
-                if b - 1 == step - 2:
-                    layer2(0, a, b)
+            for (a, b), after in zip(FIRST_GROUPS, L2_AFTER):
+                if after == step - 2:
+                    first_banks.append(next_bank())
+                    layer2(0, a, b, first_banks[-1], a >= EVAC_V)
 
-        gate_t = []
-        for pair in range(2):
-            gt = work.tile([P, 2, T], F32, name="gt", tag="stream", bufs=STREAM_BUFS, align_bytes=64)
-            nc.sync.dma_start(out=gt[:], in_=gate[2 * pair : 2 * pair + 2].rearrange("r p t -> p r t"))
-            gate_t.extend([gt[:, 0, :], gt[:, 1, :]])
-        w2w.append([load_words("w2w1_0", w2w_d[0:8, :, 128:256])])
-        wgw = load_words("wgw", wg_words.bitcast(I32))
-        w2w[1].append(load_words("w2w1_1", w2w_d[8:16, :, 128:256]))
-
-        o_t = {}
+        o_t = [keep.tile([P, T], F32, name="o%d" % nb) for nb in range(NB)]
+        pr_ring = [keep.tile([P, T], F32, name="pr%d" % i) for i in range(PR_SETS * TOP)]
+        late_a, late_b = first_banks[-2], first_banks[-1]
+        free = [b for b in banks if b is not late_a and b is not late_b]
+        l2_banks = {1: (free[0], late_a, late_b, free[0]), 2: (free[1], late_b, free[0], free[1]), 3: (late_b, free[0], free[1], late_b)}
 
         def out_gate(nb):
-            z = psum.tile([P, T], F32, name="z", tag="bankC", bufs=2)
+            z = free[nb % 2]
             nc.tensor.matmul_mx(
                 out=z[:], lhsT=wgw[:, nb * 256 : (nb + 1) * 256].bitcast(FP4X4), lhsT_scale=wgs[:, nb * P : (nb + 1) * P],
                 rhs=xw[:].bitcast(FP8X4), rhs_scale=xs[:], start=True, stop=True,
             )
-            o = work.tile([P, T], F32, name="o", tag="o", bufs=NB)
-            nc.scalar.activation(o[:], z[:], ACT.Sigmoid)
-            o_t[nb] = o
+            nc.scalar.activation(o_t[nb][:], z[:], ACT.Sigmoid)
+
+        def fetch(i, nb, t0, t1, r):
+            pr = pr_ring[(i % PR_SETS) * TOP + r][:, 0 : t1 - t0]
+            nc.vector.tensor_tensor(pr, y[nb][:].indirect(pos_t[r][:, t0 // 16 : t1 // 16]), gate_t[r][:, t0:t1], ALU.mult)
+            return pr
 
         c_t = {}
 
-        def fetch(nb, t0, t1, r):
-            pr = work.tile([P, t1 - t0], F32, name="pr", tag="pr", bufs=8)
-            nc.vector.tensor_tensor(pr[:], y[nb][:].indirect(pos_t[r][:, t0 // 16 : t1 // 16]), gate_t[r][:, t0:t1], ALU.mult)
-            return pr
-
-        def combine(nb, t0, t1):
-            parts = [fetch(nb, t0, t1, r) for r in range(TOP)]
+        def combine(i, nb, t0, t1):
+            parts = [fetch(i, nb, t0, t1, r) for r in range(TOP)]
             blocks = (t1 - t0) // P
-            ct = psum.tile([P, blocks, P], F32, name="ct", tag="bankA", bufs=3)
+            ct = (late_a, late_b)[i % 2]
+            for r in range(TOP):
+                for tb in range(blocks):
+                    nc.tensor.matmul(
+                        ct[:, tb * P : (tb + 1) * P], parts[r][:, tb * P : (tb + 1) * P], ident[:],
+                        start=r == 0 and tb == 0, stop=r == TOP - 1 and tb == blocks - 1, is_transpose=True,
+                    )
+            cs = work.tile([P, t1 - t0], F32, name="cs", tag="cs", bufs=2)
+            nc.scalar.copy(cs[:], ct[:, 0 : t1 - t0])
+            c = free[2 + i % 4]
             for tb in range(blocks):
-                for r in range(TOP):
-                    nc.tensor.matmul(ct[:, tb, :], parts[r][:, tb * P : (tb + 1) * P], ident[:], start=r == 0, stop=r == TOP - 1, is_transpose=True)
-            cs = work.tile([P, blocks, P], F32, name="cs", tag="cs", bufs=2)
-            nc.scalar.copy(cs[:], ct[:])
-            c = psum.tile([P, t1 - t0], F32, name="c", tag="bankB", bufs=3)
-            for tb in range(blocks):
-                nc.tensor.transpose(c[:, tb * P : (tb + 1) * P], cs[:, tb, :], ident[:])
-            c_t[nb, t0] = c
+                nc.tensor.transpose(c[:, tb * P : (tb + 1) * P], cs[:, tb * P : (tb + 1) * P], ident[:])
+            c_t[i] = c[:, 0 : t1 - t0]
 
-        def finish(nb, t0, t1):
+        def finish(i, nb, t0, t1):
             res = work.tile([P, t1 - t0], F32, name="res", tag="res", bufs=NB + 1)
-            nc.vector.tensor_tensor(res[:], c_t[nb, t0][:], o_t[nb][:, t0:t1], ALU.mult)
+            nc.vector.tensor_tensor(res[:], c_t[i], o_t[nb][:, t0:t1], ALU.mult)
             nc.sync.dma_start(out=out[nb * P : (nb + 1) * P, t0:t1], in_=res[:])
 
-        pieces = [(nb, 0, T) for nb in range(NB - 1)] + [(NB - 1, 0, T - LAST)]
-        for i, (nb, t0, t1) in enumerate(pieces):
-            if nb + 1 < NB:
-                for a, b in GROUPS:
-                    layer2(nb + 1, a, b)
+        pieces = [(nb, 0, T) for nb in range(NB - 1)] + [(NB - 1, 0, T - LAST), (NB - 1, T - LAST, T)]
+        for nb in range(1, NB):
+            for (a, b), bank in zip(reversed(GROUPS), l2_banks[nb]):
+                layer2(nb, a, b, bank)
+        for nb in range(NB):
             out_gate(nb)
-            combine(nb, t0, t1)
+        for i, (nb, t0, t1) in enumerate(pieces):
+            combine(i, nb, t0, t1)
             if i > 0:
-                finish(*pieces[i - 1])
+                finish(i - 1, *pieces[i - 1])
 
-        nb, t0 = NB - 1, T - LAST
-        parts = [fetch(nb, t0, T, r) for r in range(TOP)]
-        sums = work.tile([P, 3, LAST], F32, name="sums")
-        nc.vector.tensor_tensor(sums[:, 0, :], parts[0][:], parts[1][:], ALU.add)
-        nc.vector.tensor_tensor(sums[:, 1, :], parts[2][:], parts[3][:], ALU.add)
-        nc.vector.tensor_tensor(sums[:, 2, :], sums[:, 0, :], sums[:, 1, :], ALU.add)
-        res = work.tile([P, LAST], F32, name="res", tag="res", bufs=NB + 1)
-        nc.vector.tensor_tensor(res[:], sums[:, 2, :], o_t[nb][:, t0:T], ALU.mult)
-        nc.sync.dma_start(out=out[nb * P : (nb + 1) * P, t0:T], in_=res[:])
-        finish(*pieces[-1])
+        finish(NB, *pieces[-1])

@@ -23,14 +23,17 @@ FLOPS = 2415919104
 W1_GROUPS = ((0, 2), (2, 5), (5, 10), (10, 16))
 
 W1S_GROUPS = ((0, 2), (2, 7), (7, 16))
-GATHERS = ((0, 1), (1, 2), (2, 4), (4, 6), (6, 8), (8, 10), (10, 12), (12, 14), (14, 16))
-GATHER_BUFS = 5
-RELU_FROM, RELU_ALL = 5, 8
+GATHERS = ((0, 2), (2, 4), (4, 7), (7, 10), (10, 13), (13, 16))
+GATHER_BUFS = 3
+RELU_FROM, RELU_ALL = 7, 7
 RELU_ON_VECTOR = [e for e in range(RELU_FROM, E) if e % 2 == 1 or e >= RELU_ALL]
 REPEATS = range(0, 0)
 V_BANKS = 3
+LAG = 3
+RL = 4
+AHEAD = 2
 PR_SETS = 3
-EVAC_V = 8
+EVAC_V = (8, 12, 15)
 L2_AFTER = (9, 11, 13, 14, 15)
 LAST = 128
 QUANT = [(0, 2), (2, 4), (4, 6), (6, 8), (8, 10), (10, 12), (12, 14), (14, 15), (15, 16)]
@@ -72,7 +75,7 @@ def tile_moe_ogt_relu2_sigmoid_kernel(
         make_identity(nc, ident[:])
         warm = keep.tile([P, 1], F32, name="warm")
         nc.scalar.activation(warm[:], ident[:, 0:1], ACT.Sigmoid)
-        w2s = [plane("w2s%d" % i, E * 256, nc.gpsimd) for i in range(2)]
+        w2s = [plane("w2s%d" % i, E * 256, nc.gpsimd if i else nc.vector) for i in range(2)]
         wgs = plane("wgs", N, nc.gpsimd)
 
         w1w_d = w1_words.rearrange("e o p n -> (e o) p n").bitcast(I32)
@@ -121,17 +124,20 @@ def tile_moe_ogt_relu2_sigmoid_kernel(
             return banks[V_BANKS + (len(turns) - 1) % (8 - V_BANKS)]
 
         xg_ring = [keep.tile([P, 3 * C], U32, name="xg%d" % i, align_bytes=64) for i in range(GATHER_BUFS)]
-        sg_ring = [keep.tile([P, 3 * C], U8, name="sg%d" % i, align_bytes=64) for i in range(GATHER_BUFS)]
-        rl_ring = [keep.tile([P, H], F32, name="rl%d" % i) for i in range(4)]
+        sg_ring = [keep.tile([P, 3 * C], U8, name="sg%d" % i, align_bytes=64) for i in range(len(GATHERS))]
+        rl_ring = [keep.tile([P, H], F32, name="rl%d" % i) for i in range(RL)]
         xg, sg = {}, {}
 
         def gather(i):
             a, b = GATHERS[i]
             o = offs_t[:, a * 8 : b * 8]
             xg[i] = xg_ring[i % GATHER_BUFS][:, 0 : (b - a) * C]
-            sg[i] = sg_ring[i % GATHER_BUFS][:, 0 : (b - a) * C]
-            nc.vector.tensor_copy(sg[i], xs[:].indirect(o))
             nc.vector.tensor_copy(xg[i], xw[:].bitcast(U32).indirect(o))
+
+        def gather_scales(i):
+            a, b = GATHERS[i]
+            sg[i] = sg_ring[i][:, 0 : (b - a) * C]
+            nc.vector.tensor_copy(sg[i], xs[:].indirect(offs_t[:, a * 8 : b * 8]))
 
         h = [keep.tile([P, (b - a) * C * 4], BF16, name="h%d" % a, align_bytes=64) for a, b in QUANT]
 
@@ -154,12 +160,13 @@ def tile_moe_ogt_relu2_sigmoid_kernel(
                     rhs=w1w[gi][:, ge * 1024 : (ge + 1) * 1024].bitcast(FP4X4), rhs_scale=w1s[si][:, se * H : (se + 1) * H],
                     start=True, stop=True,
                 )
-            rl = rl_ring[e % 4][:].rearrange("p (t m) -> p t m", t=4)
-            src = v[:].rearrange("p (m t) -> p t m", t=4)
+            rl = rl_ring[e % RL][:].rearrange("p (t m) -> p t m", t=4)
+            dst = rl_ring[e % RL][:].rearrange("p (u d m) -> p u m d", u=2, d=2)
+            src = v[:].rearrange("p (m u d) -> p u m d", u=2, d=2)
             if e not in RELU_ON_VECTOR:
-                nc.scalar.activation(rl, src, ACT.Relu)
+                nc.scalar.activation(dst, src, ACT.Relu)
             else:
-                nc.vector.tensor_scalar(rl, src, 0.0, None, ALU.max)
+                nc.vector.tensor_scalar(dst, src, 0.0, None, ALU.max)
             relu_t[e] = rl
 
         def turn(e):
@@ -194,12 +201,17 @@ def tile_moe_ogt_relu2_sigmoid_kernel(
         first_banks = []
         for i in range(GATHER_BUFS):
             gather(i)
+        for i in range(len(GATHERS)):
+            gather_scales(i)
         for step in range(E + 2):
             for i, (a, b) in enumerate(GATHERS):
-                if b == step and i + GATHER_BUFS < len(GATHERS):
+                if b == step + AHEAD - 1 and i + GATHER_BUFS < len(GATHERS):
                     gather(i + GATHER_BUFS)
-            if step < E:
-                layer1(step)
+            if step == 0:
+                for e in range(AHEAD - 1):
+                    layer1(e)
+            if step + AHEAD - 1 < E:
+                layer1(step + AHEAD - 1)
             if 0 <= step - 1 < E:
                 turn(step - 1)
             for a, b in QUANT:
@@ -208,16 +220,16 @@ def tile_moe_ogt_relu2_sigmoid_kernel(
             for (a, b), after in zip(FIRST_GROUPS, L2_AFTER):
                 if after == step - 2:
                     first_banks.append(next_bank())
-                    layer2(0, a, b, first_banks[-1], a >= EVAC_V)
+                    layer2(0, a, b, first_banks[-1], a in EVAC_V)
 
         o_t = [keep.tile([P, T], F32, name="o%d" % nb) for nb in range(NB)]
         pr_ring = [keep.tile([P, T], F32, name="pr%d" % i) for i in range(PR_SETS * TOP)]
         late_a, late_b = first_banks[-2], first_banks[-1]
         free = [b for b in banks if b is not late_a and b is not late_b]
-        l2_banks = {1: (free[0], late_a, late_b, free[0]), 2: (free[1], late_b, free[0], free[1]), 3: (late_b, free[0], free[1], late_b)}
+        l2_banks = {1: (free[0], late_a, late_b, free[0]), 2: (late_a, late_b, free[0], late_a), 3: (late_b, free[0], late_a, late_b)}
 
         def out_gate(nb):
-            z = free[nb % 2]
+            z = (free[0], late_a, late_b, free[0])[nb]
             nc.tensor.matmul_mx(
                 out=z[:], lhsT=wgw[:, nb * 256 : (nb + 1) * 256].bitcast(FP4X4), lhsT_scale=wgs[:, nb * P : (nb + 1) * P],
                 rhs=xw[:].bitcast(FP8X4), rhs_scale=xs[:], start=True, stop=True,
@@ -243,7 +255,7 @@ def tile_moe_ogt_relu2_sigmoid_kernel(
                     )
             cs = work.tile([P, t1 - t0], F32, name="cs", tag="cs", bufs=2)
             nc.scalar.copy(cs[:], ct[:, 0 : t1 - t0])
-            c = free[2 + i % 4]
+            c = free[1 + i]
             for tb in range(blocks):
                 nc.tensor.transpose(c[:, tb * P : (tb + 1) * P], cs[:, tb * P : (tb + 1) * P], ident[:])
             c_t[i] = c[:, 0 : t1 - t0]
@@ -261,7 +273,7 @@ def tile_moe_ogt_relu2_sigmoid_kernel(
             out_gate(nb)
         for i, (nb, t0, t1) in enumerate(pieces):
             combine(i, nb, t0, t1)
-            if i > 0:
-                finish(i - 1, *pieces[i - 1])
-
-        finish(NB, *pieces[-1])
+            if i >= LAG:
+                finish(i - LAG, *pieces[i - LAG])
+        for i in range(len(pieces) - LAG, len(pieces)):
+            finish(i, *pieces[i])

@@ -16,29 +16,30 @@ ALU = mybir.AluOpType
 
 P = 128
 T, E, C, H, N, TOP = 512, 16, 128, 512, 512, 4
-S = E * C
-NB = N // P
-FLOPS = 2415919104
+SLOTS = E * C
+ROW_BLOCKS = N // P
+HALF = N // 2
+LIST_COLS = C // 16
+FLOPS = 2 * 512 * N * T + 2 * (512 * H + H * N) * SLOTS
 
-W1_GROUPS = ((0, 2), (2, 5), (5, 10), (10, 16))
+W1_LOADS = [(0, 2), (2, 4)] + [(a, a + 4) for a in range(4, E, 4)]
+GATHERS = [(0, 2), (2, 4)] + [(a, a + 3) for a in range(4, E, 3)]
+QUANTISE = [(a, a + 2) for a in range(0, E - 2, 2)] + [(E - 2, E - 1), (E - 1, E)]
+FOURS = [(a, a + 4) for a in range(0, E, 4)]
+FIRST_BLOCK = FOURS[:-1] + [(E - 4, E - 1), (E - 1, E)]
 
-W1S_GROUPS = ((0, 2), (2, 7), (7, 16))
-GATHERS = ((0, 2), (2, 4), (4, 7), (7, 10), (10, 13), (13, 16))
-GATHER_BUFS = 3
-RELU_FROM, RELU_ALL = 7, 7
-RELU_ON_VECTOR = [e for e in range(RELU_FROM, E) if e % 2 == 1 or e >= RELU_ALL]
-REPEATS = range(0, 0)
-V_BANKS = 3
-LAG = 3
-RL = 4
-AHEAD = 2
-PR_SETS = 3
-EVAC_V = (8, 12, 15)
-L2_AFTER = (9, 11, 13, 14, 15)
-LAST = 128
-QUANT = [(0, 2), (2, 4), (4, 6), (6, 8), (8, 10), (10, 12), (12, 14), (14, 15), (15, 16)]
-FIRST_GROUPS = ((0, 4), (4, 8), (8, 12), (12, 15), (15, 16))
-GROUPS = ((0, 4), (4, 8), (8, 12), (12, 16))
+RELU_ON_SCALAR = 7
+FIRST_BLOCK_ON_SCALAR = 2
+WORD_TILES = 3
+RELU_TILES = 4
+PRODUCT_BANKS = 3
+PART_SETS = 3
+FINISH_LAG = 3
+STREAM_TILES = 8
+
+
+def locate(ranges, e):
+    return [(i, e - a) for i, (a, b) in enumerate(ranges) if a <= e < b][0]
 
 
 def tile_moe_ogt_relu2_sigmoid_kernel(
@@ -51,229 +52,226 @@ def tile_moe_ogt_relu2_sigmoid_kernel(
         work = ctx.enter_context(tc.tile_pool(name="work", bufs=1))
         psum = ctx.enter_context(tc.psum_pool(name="psum", bufs=1))
 
-        def plane(name, cols, eng):
-            t = keep.tile([P, cols], U8, name=name, align_bytes=64)
-            eng.memset(t[:].bitcast(I32), 0)
-            return t
+        def zeroed_plane(name, cols, engine):
+            plane = keep.tile([P, cols], U8, name=name, align_bytes=64)
+            engine.memset(plane[:].bitcast(I32), 0)
+            return plane
 
-        def load_scales(t, src):
-            ne, w = src.shape[0], src.shape[2]
-            rows = src.rearrange("e (q r) n -> r q e n", r=4)
-            dst = t[:].bitcast(I32).rearrange("p (e n) -> p e n", e=ne)
-            for r in range(4):
-                nc.sync.dma_start(out=dst[r:P:32, :, :], in_=rows[r])
-
-        def load_words(name, src):
-            ne, w = src.shape[0], src.shape[2]
-            t = keep.tile([P, ne * w * 4], U8, name=name, align_bytes=64)
-            nc.sync.dma_start(out=t[:].bitcast(I32).rearrange("p (e n) -> p e n", e=ne), in_=src.rearrange("e p n -> p e n"))
-            return t
-
-        xs = plane("xs", T, nc.gpsimd)
-        w1s = [plane("w1s%d" % i, (b - a) * H, nc.vector) for i, (a, b) in enumerate(W1S_GROUPS)]
+        x_plane = zeroed_plane("x_plane", T, nc.gpsimd)
+        w1_planes = [
+            zeroed_plane("w1_plane%d" % i, (b - a) * H, nc.vector if b <= E // 2 else nc.gpsimd)
+            for i, (a, b) in enumerate(W1_LOADS)
+        ]
+        w2_planes = [zeroed_plane("w2_plane0", E * HALF, nc.vector)]
         ident = keep.tile([P, P], F32, name="ident")
         make_identity(nc, ident[:])
-        warm = keep.tile([P, 1], F32, name="warm")
-        nc.scalar.activation(warm[:], ident[:, 0:1], ACT.Sigmoid)
-        w2s = [plane("w2s%d" % i, E * 256, nc.gpsimd if i else nc.vector) for i in range(2)]
-        wgs = plane("wgs", N, nc.gpsimd)
+        wg_plane = zeroed_plane("wg_plane", N, nc.gpsimd)
+        w2_planes.append(zeroed_plane("w2_plane1", E * HALF, nc.gpsimd))
 
-        w1w_d = w1_words.rearrange("e o p n -> (e o) p n").bitcast(I32)
-        w2w_d = w2_words.rearrange("e o p n -> (e o) p n").bitcast(I32)
-        w1s_d = w1_scales.rearrange("e o b n -> (e o) b n").bitcast(I32)
-        w2s_d = w2_scales.rearrange("e o b n -> (e o) b n").bitcast(I32)
+        def load_scales(plane, rows):
+            src = rows.rearrange("e (q r) n -> r q e n", r=4)
+            dst = plane[:].bitcast(I32).rearrange("p (e n) -> p e n", e=rows.shape[0])
+            for r in range(4):
+                nc.sync.dma_start(out=dst[r:P:32, :, :], in_=src[r])
 
-        offs_t = keep.tile([P, S // 16], U16, name="offs_t")
-        nc.sync.dma_start(offs_t[:], offs)
-        xw = keep.tile([P, T], I32, name="xw", align_bytes=64)
-        nc.sync.dma_start(out=xw[:], in_=x_words[0].rearrange("p t d -> p (t d)").bitcast(I32))
-        w1w = []
-        for g, (a, b) in enumerate(W1_GROUPS):
-            w1w.append(load_words("w1w%d" % g, w1w_d[a:b]))
-            if g == 0:
-                load_scales(xs, x_scales.bitcast(I32))
-            if g < len(W1S_GROUPS):
-                load_scales(w1s[g], w1s_d[W1S_GROUPS[g][0] : W1S_GROUPS[g][1]])
-        load_scales(w2s[0], w2s_d[:, :, 0:64])
-        w2w = [[load_words("w2w0_%d" % g, w2w_d[8 * g : 8 * g + 8, :, 0:128]) for g in range(2)]]
-        pos_t = []
+        def load_words(tile, words):
+            dst = tile[:].bitcast(I32).rearrange("p (e n) -> p e n", e=words.shape[0])
+            nc.sync.dma_start(out=dst, in_=words.rearrange("e p n -> p e n"))
+            return tile
+
+        def stream_tile(name, shape, dtype):
+            return work.tile(shape, dtype, name=name, tag="stream", bufs=STREAM_TILES, align_bytes=64)
+
+        w1_words32 = w1_words.rearrange("e o p n -> (e o) p n").bitcast(I32)
+        w2_words32 = w2_words.rearrange("e o p n -> (e o) p n").bitcast(I32)
+        w1_scales32 = w1_scales.rearrange("e o b n -> (e o) b n").bitcast(I32)
+        w2_scales32 = w2_scales.rearrange("e o b n -> (e o) b n").bitcast(I32)
+
+        def load_w2(half, eight):
+            tile = stream_tile("w2_%d_%d" % (half, eight), [P, 8 * 2 * HALF], U8)
+            return load_words(tile, w2_words32[8 * eight : 8 * eight + 8, :, half * HALF // 2 : (half + 1) * HALF // 2])
+
+        def load_w2_scales(half):
+            load_scales(w2_planes[half], w2_scales32[:, :, half * HALF // 4 : (half + 1) * HALF // 4])
+
+        def load_gates(pair):
+            tile = stream_tile("gates%d" % pair, [P, 2, T], F32)
+            nc.sync.dma_start(out=tile[:], in_=gate[2 * pair : 2 * pair + 2].rearrange("r p t -> p r t"))
+            return [tile[:, 0, :], tile[:, 1, :]]
+
+        offs_tile = keep.tile([P, SLOTS // 16], U16, name="offs_tile")
+        nc.sync.dma_start(offs_tile[:], offs)
+        x_tile = keep.tile([P, T], I32, name="x_tile", align_bytes=64)
+        nc.sync.dma_start(out=x_tile[:], in_=x_words[0].rearrange("p t d -> p (t d)").bitcast(I32))
+        w1_tiles = []
+        for i, (a, b) in enumerate(W1_LOADS):
+            w1_tiles.append(load_words(stream_tile("w1_%d" % i, [P, (b - a) * 2 * H], U8), w1_words32[a:b]))
+            if i == 0:
+                load_scales(x_plane, x_scales.bitcast(I32))
+            load_scales(w1_planes[i], w1_scales32[a:b])
+        load_w2_scales(0)
+        w2_tiles = {(0, eight): load_w2(0, eight) for eight in range(2)}
+        load_scales(wg_plane, wg_scales.bitcast(I32))
+        wg_tile = load_words(keep.tile([P, 2 * N], U8, name="wg_tile", align_bytes=64), wg_words.bitcast(I32))
+        gates = load_gates(0)
+        pos_tiles = []
         for r, pos in enumerate((pos1, pos2, pos3, pos4)):
-            pt = keep.tile([P, T // 16], U16, name="pos_t%d" % r)
-            nc.sync.dma_start(pt[:], pos)
-            pos_t.append(pt)
+            pos_tiles.append(keep.tile([P, T // 16], U16, name="pos_tile%d" % r))
+            nc.sync.dma_start(pos_tiles[r][:], pos)
+        gates = gates + load_gates(1)
+        load_w2_scales(1)
+        for eight in (1, 0):
+            w2_tiles[1, eight] = load_w2(1, eight)
 
-        hq = keep.tile([P, S], U32, name="hq", align_bytes=64)
-        hs = keep.tile([P, S], U8, name="hs", align_bytes=64)
-        y = [keep.tile([P, S], F32, name="y%d" % nb) for nb in range(NB)]
-
-        gate_t = []
-        for pair in range(2):
-            gt = keep.tile([P, 2, T], F32, name="gt%d" % pair)
-            nc.sync.dma_start(out=gt[:], in_=gate[2 * pair : 2 * pair + 2].rearrange("r p t -> p r t"))
-            gate_t.extend([gt[:, 0, :], gt[:, 1, :]])
-        load_scales(w2s[1], w2s_d[:, :, 64:128])
-        w2w.append([load_words("w2w1_%d" % g, w2w_d[8 * g : 8 * g + 8, :, 128:256]) for g in (1, 0)][::-1])
-        load_scales(wgs, wg_scales.bitcast(I32))
-        wgw = load_words("wgw", wg_words.bitcast(I32))
-
+        h_words = keep.tile([P, SLOTS], U32, name="h_words", align_bytes=64)
+        h_plane = keep.tile([P, SLOTS], U8, name="h_plane", align_bytes=64)
+        y = [keep.tile([P, SLOTS], F32, name="y%d" % nb) for nb in range(ROW_BLOCKS)]
         banks = [psum.tile([P, 512], F32, name="bank%d" % b) for b in range(8)]
-        turns = []
+        slot_words = [keep.tile([P, 3 * C], U32, name="slot_words%d" % i, align_bytes=64) for i in range(WORD_TILES)]
+        slot_planes = [keep.tile([P, 3 * C], U8, name="slot_plane%d" % i, align_bytes=64) for i in range(len(GATHERS))]
+        relu_tiles = [keep.tile([P, H], F32, name="relu%d" % i) for i in range(RELU_TILES)]
+        h_tiles = [keep.tile([P, (b - a) * H], BF16, name="h%d" % a, align_bytes=64) for a, b in QUANTISE]
+        handed_out = []
 
         def next_bank():
-            turns.append(0)
-            return banks[V_BANKS + (len(turns) - 1) % (8 - V_BANKS)]
+            handed_out.append(banks[PRODUCT_BANKS + len(handed_out) % (len(banks) - PRODUCT_BANKS)])
+            return handed_out[-1]
 
-        xg_ring = [keep.tile([P, 3 * C], U32, name="xg%d" % i, align_bytes=64) for i in range(GATHER_BUFS)]
-        sg_ring = [keep.tile([P, 3 * C], U8, name="sg%d" % i, align_bytes=64) for i in range(len(GATHERS))]
-        rl_ring = [keep.tile([P, H], F32, name="rl%d" % i) for i in range(RL)]
-        xg, sg = {}, {}
+        def gather_words(g):
+            a, b = GATHERS[g]
+            entries = offs_tile[:, a * LIST_COLS : b * LIST_COLS]
+            nc.vector.tensor_copy(slot_words[g % WORD_TILES][:, 0 : (b - a) * C], x_tile[:].bitcast(U32).indirect(entries))
 
-        def gather(i):
-            a, b = GATHERS[i]
-            o = offs_t[:, a * 8 : b * 8]
-            xg[i] = xg_ring[i % GATHER_BUFS][:, 0 : (b - a) * C]
-            nc.vector.tensor_copy(xg[i], xw[:].bitcast(U32).indirect(o))
+        def gather_scales(g):
+            a, b = GATHERS[g]
+            entries = offs_tile[:, a * LIST_COLS : b * LIST_COLS]
+            nc.vector.tensor_copy(slot_planes[g][:, 0 : (b - a) * C], x_plane[:].indirect(entries))
 
-        def gather_scales(i):
-            a, b = GATHERS[i]
-            sg[i] = sg_ring[i][:, 0 : (b - a) * C]
-            nc.vector.tensor_copy(sg[i], xs[:].indirect(offs_t[:, a * 8 : b * 8]))
-
-        h = [keep.tile([P, (b - a) * C * 4], BF16, name="h%d" % a, align_bytes=64) for a, b in QUANT]
-
-        def find(groups, e):
-            for i, (a, b) in enumerate(groups):
-                if a <= e < b:
-                    return i, e - a
-
-        relu_t = {}
-
-        def layer1(e):
-            xi, xe = find(GATHERS, e)
-            sl = slice(xe * C, (xe + 1) * C)
-            gi, ge = find(W1_GROUPS, e)
-            si, se = find(W1S_GROUPS, e)
-            v = banks[e % V_BANKS]
-            for rep in range(2 if e in REPEATS else 1):
-                nc.tensor.matmul_mx(
-                    out=v[:], lhsT=xg[xi][:, sl].bitcast(FP8X4), lhsT_scale=sg[xi][:, sl],
-                    rhs=w1w[gi][:, ge * 1024 : (ge + 1) * 1024].bitcast(FP4X4), rhs_scale=w1s[si][:, se * H : (se + 1) * H],
-                    start=True, stop=True,
-                )
-            rl = rl_ring[e % RL][:].rearrange("p (t m) -> p t m", t=4)
-            dst = rl_ring[e % RL][:].rearrange("p (u d m) -> p u m d", u=2, d=2)
-            src = v[:].rearrange("p (m u d) -> p u m d", u=2, d=2)
-            if e not in RELU_ON_VECTOR:
+        def first_product(e):
+            g, in_gather = locate(GATHERS, e)
+            load, in_load = locate(W1_LOADS, e)
+            slots = slice(in_gather * C, (in_gather + 1) * C)
+            bank = banks[e % PRODUCT_BANKS]
+            nc.tensor.matmul_mx(
+                out=bank[:],
+                lhsT=slot_words[g % WORD_TILES][:, slots].bitcast(FP8X4),
+                lhsT_scale=slot_planes[g][:, slots],
+                rhs=w1_tiles[load][:, in_load * 2 * H : (in_load + 1) * 2 * H].bitcast(FP4X4),
+                rhs_scale=w1_planes[load][:, in_load * H : (in_load + 1) * H],
+                start=True, stop=True,
+            )
+            src = bank[:].rearrange("p (m u v) -> p u m v", u=2, v=2)
+            dst = relu_tiles[e % RELU_TILES][:].rearrange("p (u v m) -> p u m v", u=2, v=2)
+            if e < RELU_ON_SCALAR:
                 nc.scalar.activation(dst, src, ACT.Relu)
             else:
                 nc.vector.tensor_scalar(dst, src, 0.0, None, ALU.max)
-            relu_t[e] = rl
 
-        def turn(e):
-            rt = next_bank()[:].rearrange("p (t s) -> p t s", t=4)
-            for t in range(4):
-                nc.tensor.transpose(rt[:, t, :], relu_t[e][:, t, :], ident[:])
-            hi, he = find(QUANT, e)
-            nc.scalar.activation(h[hi][:, he * H : (he + 1) * H].rearrange("p (s t) -> p s t", t=4), rt.rearrange("p t s -> p s t"), ACT.Square)
+        def turn_and_square(e):
+            bank = next_bank()
+            for d in range(4):
+                nc.tensor.transpose(bank[:, d * C : (d + 1) * C], relu_tiles[e % RELU_TILES][:, d * P : (d + 1) * P], ident[:])
+            q, in_tile = locate(QUANTISE, e)
+            dst = h_tiles[q][:, in_tile * H : (in_tile + 1) * H].rearrange("p (s d) -> p s d", d=4)
+            nc.scalar.activation(dst, bank[:].rearrange("p (d s) -> p s d", d=4), ACT.Square)
+            return bank
 
-        def quantise(a, b):
-            sl = slice(a * C, b * C)
-            nc.vector.quantize_mx(out=hq[:, sl].bitcast(FP8X4), scales=hs[:, sl], in_=h[QUANT.index((a, b))][:])
+        def quantise(q):
+            a, b = QUANTISE[q]
+            nc.vector.quantize_mx(out=h_words[:, a * C : b * C].bitcast(FP8X4), scales=h_plane[:, a * C : b * C], in_=h_tiles[q][:])
 
-        def layer2(nb, a, b, bank, on_vector=False):
-            yb = bank[:, 0 : (b - a) * C]
-            half, sub = divmod(nb, 2)
-            for e in reversed(range(a, b)) if nb else range(a, b):
-                j = e - a
-                sl = slice(e * C, (e + 1) * C)
-                w0 = (e % 8) * 512 + sub * 256
-                s0 = e * 256 + sub * P
+        def second_product(nb, experts, bank, copy_out):
+            half, col = divmod(nb * P, HALF)
+            first = min(experts)
+            for e in experts:
+                word_col, scale_col = (e % 8) * HALF + col, e * HALF + col
                 nc.tensor.matmul_mx(
-                    out=yb[:, j * C : (j + 1) * C],
-                    lhsT=w2w[half][e // 8][:, w0 : w0 + 256].bitcast(FP4X4), lhsT_scale=w2s[half][:, s0 : s0 + P],
-                    rhs=hq[:, sl].bitcast(FP8X4), rhs_scale=hs[:, sl], start=True, stop=True,
+                    out=bank[:, (e - first) * C : (e - first + 1) * C],
+                    lhsT=w2_tiles[half, e // 8][:, 2 * word_col : 2 * (word_col + P)].bitcast(FP4X4),
+                    lhsT_scale=w2_planes[half][:, scale_col : scale_col + P],
+                    rhs=h_words[:, e * C : (e + 1) * C].bitcast(FP8X4),
+                    rhs_scale=h_plane[:, e * C : (e + 1) * C],
+                    start=True, stop=True,
                 )
-            if on_vector:
-                nc.vector.tensor_copy(y[nb][:, a * C : b * C], yb)
-            else:
-                nc.scalar.copy(y[nb][:, a * C : b * C], yb)
+            copy_out(y[nb][:, first * C : (first + len(experts)) * C], bank[:, 0 : len(experts) * C])
 
-        first_banks = []
-        for i in range(GATHER_BUFS):
-            gather(i)
-        for i in range(len(GATHERS)):
-            gather_scales(i)
+        for g in range(WORD_TILES):
+            gather_words(g)
+        for g in range(len(GATHERS)):
+            gather_scales(g)
+        turn_banks, block_banks = [], []
         for step in range(E + 2):
-            for i, (a, b) in enumerate(GATHERS):
-                if b == step + AHEAD - 1 and i + GATHER_BUFS < len(GATHERS):
-                    gather(i + GATHER_BUFS)
+            for g in range(len(GATHERS) - WORD_TILES):
+                if GATHERS[g][1] == step + 1:
+                    gather_words(g + WORD_TILES)
             if step == 0:
-                for e in range(AHEAD - 1):
-                    layer1(e)
-            if step + AHEAD - 1 < E:
-                layer1(step + AHEAD - 1)
-            if 0 <= step - 1 < E:
-                turn(step - 1)
-            for a, b in QUANT:
-                if b - 1 == step - 2:
-                    quantise(a, b)
-            for (a, b), after in zip(FIRST_GROUPS, L2_AFTER):
-                if after == step - 2:
-                    first_banks.append(next_bank())
-                    layer2(0, a, b, first_banks[-1], a in EVAC_V)
+                first_product(0)
+            if step + 1 < E:
+                first_product(step + 1)
+            if 1 <= step <= E:
+                turn_banks.append(turn_and_square(step - 1))
+            for q in range(len(QUANTISE)):
+                if QUANTISE[q][1] == step - 1:
+                    quantise(q)
+            j = step - (E + 2 - len(FIRST_BLOCK))
+            if j >= 0:
+                block_banks.append(next_bank())
+                copy_out = nc.scalar.copy if j < FIRST_BLOCK_ON_SCALAR else nc.vector.tensor_copy
+                second_product(0, range(*FIRST_BLOCK[j]), block_banks[j], copy_out)
 
-        o_t = [keep.tile([P, T], F32, name="o%d" % nb) for nb in range(NB)]
-        pr_ring = [keep.tile([P, T], F32, name="pr%d" % i) for i in range(PR_SETS * TOP)]
-        late_a, late_b = first_banks[-2], first_banks[-1]
-        free = [b for b in banks if b is not late_a and b is not late_b]
-        l2_banks = {1: (free[0], late_a, late_b, free[0]), 2: (late_a, late_b, free[0], late_a), 3: (late_b, free[0], late_a, late_b)}
+        ring = [banks[0], block_banks[-2], block_banks[-1]]
+        gate_banks = [turn_banks[E - 2], ring[0], ring[2], ring[0]]
+        sum_banks = [ring[1], ring[2]]
+        result_banks = [banks[1], banks[2], turn_banks[E - 1], block_banks[-3], turn_banks[E - 2]]
+        out_gates = [keep.tile([P, T], F32, name="out_gate%d" % nb) for nb in range(ROW_BLOCKS)]
+        part_tiles = [keep.tile([P, T], F32, name="part%d" % i) for i in range(PART_SETS * TOP)]
+        pieces = [(nb, 0, T) for nb in range(ROW_BLOCKS - 1)] + [(ROW_BLOCKS - 1, 0, T - P), (ROW_BLOCKS - 1, T - P, T)]
 
-        def out_gate(nb):
-            z = (free[0], late_a, late_b, free[0])[nb]
+        def output_gate(nb):
             nc.tensor.matmul_mx(
-                out=z[:], lhsT=wgw[:, nb * 256 : (nb + 1) * 256].bitcast(FP4X4), lhsT_scale=wgs[:, nb * P : (nb + 1) * P],
-                rhs=xw[:].bitcast(FP8X4), rhs_scale=xs[:], start=True, stop=True,
+                out=gate_banks[nb][:],
+                lhsT=wg_tile[:, 2 * nb * P : 2 * (nb + 1) * P].bitcast(FP4X4),
+                lhsT_scale=wg_plane[:, nb * P : (nb + 1) * P],
+                rhs=x_tile[:].bitcast(FP8X4),
+                rhs_scale=x_plane[:],
+                start=True, stop=True,
             )
-            nc.scalar.activation(o_t[nb][:], z[:], ACT.Sigmoid)
+            nc.scalar.activation(out_gates[nb][:], gate_banks[nb][:], ACT.Sigmoid)
 
-        def fetch(i, nb, t0, t1, r):
-            pr = pr_ring[(i % PR_SETS) * TOP + r][:, 0 : t1 - t0]
-            nc.vector.tensor_tensor(pr, y[nb][:].indirect(pos_t[r][:, t0 // 16 : t1 // 16]), gate_t[r][:, t0:t1], ALU.mult)
-            return pr
-
-        c_t = {}
-
-        def combine(i, nb, t0, t1):
-            parts = [fetch(i, nb, t0, t1, r) for r in range(TOP)]
-            blocks = (t1 - t0) // P
-            ct = (late_a, late_b)[i % 2]
+        def combine(i):
+            nb, t0, t1 = pieces[i]
+            width = t1 - t0
+            blocks = [slice(c, c + P) for c in range(0, width, P)]
+            parts = [part_tiles[(i % PART_SETS) * TOP + r] for r in range(TOP)]
             for r in range(TOP):
-                for tb in range(blocks):
+                looked_up = y[nb][:].indirect(pos_tiles[r][:, t0 // 16 : t1 // 16])
+                nc.vector.tensor_tensor(parts[r][:, 0:width], looked_up, gates[r][:, t0:t1], ALU.mult)
+            sums = sum_banks[i % 2]
+            for r in range(TOP):
+                for cols in blocks:
                     nc.tensor.matmul(
-                        ct[:, tb * P : (tb + 1) * P], parts[r][:, tb * P : (tb + 1) * P], ident[:],
-                        start=r == 0 and tb == 0, stop=r == TOP - 1 and tb == blocks - 1, is_transpose=True,
+                        sums[:, cols], parts[r][:, cols], ident[:], is_transpose=True,
+                        start=r == 0 and cols == blocks[0], stop=r == TOP - 1 and cols == blocks[-1],
                     )
-            cs = work.tile([P, t1 - t0], F32, name="cs", tag="cs", bufs=2)
-            nc.scalar.copy(cs[:], ct[:, 0 : t1 - t0])
-            c = free[1 + i]
-            for tb in range(blocks):
-                nc.tensor.transpose(c[:, tb * P : (tb + 1) * P], cs[:, tb * P : (tb + 1) * P], ident[:])
-            c_t[i] = c[:, 0 : t1 - t0]
+            turned = work.tile([P, width], F32, name="turned", tag="turned", bufs=2)
+            nc.scalar.copy(turned[:], sums[:, 0:width])
+            for cols in blocks:
+                nc.tensor.transpose(result_banks[i][:, cols], turned[:, cols], ident[:])
 
-        def finish(i, nb, t0, t1):
-            res = work.tile([P, t1 - t0], F32, name="res", tag="res", bufs=NB + 1)
-            nc.vector.tensor_tensor(res[:], c_t[i], o_t[nb][:, t0:t1], ALU.mult)
-            nc.sync.dma_start(out=out[nb * P : (nb + 1) * P, t0:t1], in_=res[:])
+        def finish(i):
+            nb, t0, t1 = pieces[i]
+            result = work.tile([P, t1 - t0], F32, name="result", tag="result", bufs=len(pieces))
+            nc.vector.tensor_tensor(result[:], result_banks[i][:, 0 : t1 - t0], out_gates[nb][:, t0:t1], ALU.mult)
+            nc.sync.dma_start(out=out[nb * P : (nb + 1) * P, t0:t1], in_=result[:])
 
-        pieces = [(nb, 0, T) for nb in range(NB - 1)] + [(NB - 1, 0, T - LAST), (NB - 1, T - LAST, T)]
-        for nb in range(1, NB):
-            for (a, b), bank in zip(reversed(GROUPS), l2_banks[nb]):
-                layer2(nb, a, b, bank)
-        for nb in range(NB):
-            out_gate(nb)
-        for i, (nb, t0, t1) in enumerate(pieces):
-            combine(i, nb, t0, t1)
-            if i >= LAG:
-                finish(i - LAG, *pieces[i - LAG])
-        for i in range(len(pieces) - LAG, len(pieces)):
-            finish(i, *pieces[i])
+        output_gate(0)
+        for nb in range(1, ROW_BLOCKS):
+            for j, (a, b) in enumerate(reversed(FOURS)):
+                second_product(nb, range(b - 1, a - 1, -1), ring[((nb - 1) * len(FOURS) + j) % len(ring)], nc.scalar.copy)
+        for nb in range(1, ROW_BLOCKS):
+            output_gate(nb)
+        for i in range(len(pieces) + FINISH_LAG):
+            if i < len(pieces):
+                combine(i)
+            if i >= FINISH_LAG:
+                finish(i - FINISH_LAG)

@@ -22,7 +22,8 @@ HALF = N // 2
 LIST_COLS = C // 16
 FLOPS = 2 * 512 * N * T + 2 * (512 * H + H * N) * SLOTS
 
-W1_LOADS = [(0, 2), (2, 4)] + [(a, a + 4) for a in range(4, E, 4)]
+W1_LOADS = [(0, 2), (2, 5), (5, 10), (10, E)]
+W1_SCALE_LOADS = [(0, 2), (2, 7), (7, E)]
 GATHERS = [(0, 2), (2, 4)] + [(a, a + 3) for a in range(4, E, 3)]
 QUANTISE = [(a, a + 2) for a in range(0, E - 2, 2)] + [(E - 2, E - 1), (E - 1, E)]
 FOURS = [(a, a + 4) for a in range(0, E, 4)]
@@ -35,7 +36,7 @@ RELU_TILES = 4
 PRODUCT_BANKS = 3
 PART_SETS = 3
 FINISH_LAG = 3
-STREAM_TILES = 8
+FIRST_BLOCK_STEP = 11
 
 
 def locate(ranges, e):
@@ -58,15 +59,13 @@ def tile_moe_ogt_relu2_sigmoid_kernel(
             return plane
 
         x_plane = zeroed_plane("x_plane", T, nc.gpsimd)
-        w1_planes = [
-            zeroed_plane("w1_plane%d" % i, (b - a) * H, nc.vector if b <= E // 2 else nc.gpsimd)
-            for i, (a, b) in enumerate(W1_LOADS)
-        ]
-        w2_planes = [zeroed_plane("w2_plane0", E * HALF, nc.vector)]
+        w1_planes = [zeroed_plane("w1_plane%d" % i, (b - a) * H, nc.vector) for i, (a, b) in enumerate(W1_SCALE_LOADS)]
+        w2_planes = [zeroed_plane("w2_plane%d" % half, E * HALF, nc.vector) for half in range(2)]
+        wg_plane = zeroed_plane("wg_plane", N, nc.vector)
         ident = keep.tile([P, P], F32, name="ident")
         make_identity(nc, ident[:])
-        wg_plane = zeroed_plane("wg_plane", N, nc.gpsimd)
-        w2_planes.append(zeroed_plane("w2_plane1", E * HALF, nc.gpsimd))
+        preload = keep.tile([P, 1], F32, name="preload")
+        nc.scalar.activation(preload[:], ident[:, 0:1], ACT.Sigmoid)
 
         def load_scales(plane, rows):
             src = rows.rearrange("e (q r) n -> r q e n", r=4)
@@ -74,13 +73,11 @@ def tile_moe_ogt_relu2_sigmoid_kernel(
             for r in range(4):
                 nc.sync.dma_start(out=dst[r:P:32, :, :], in_=src[r])
 
-        def load_words(tile, words):
+        def load_words(name, words):
+            tile = keep.tile([P, 4 * words.shape[0] * words.shape[2]], U8, name=name, align_bytes=64)
             dst = tile[:].bitcast(I32).rearrange("p (e n) -> p e n", e=words.shape[0])
             nc.sync.dma_start(out=dst, in_=words.rearrange("e p n -> p e n"))
             return tile
-
-        def stream_tile(name, shape, dtype):
-            return work.tile(shape, dtype, name=name, tag="stream", bufs=STREAM_TILES, align_bytes=64)
 
         w1_words32 = w1_words.rearrange("e o p n -> (e o) p n").bitcast(I32)
         w2_words32 = w2_words.rearrange("e o p n -> (e o) p n").bitcast(I32)
@@ -88,14 +85,14 @@ def tile_moe_ogt_relu2_sigmoid_kernel(
         w2_scales32 = w2_scales.rearrange("e o b n -> (e o) b n").bitcast(I32)
 
         def load_w2(half, eight):
-            tile = stream_tile("w2_%d_%d" % (half, eight), [P, 8 * 2 * HALF], U8)
-            return load_words(tile, w2_words32[8 * eight : 8 * eight + 8, :, half * HALF // 2 : (half + 1) * HALF // 2])
+            words = w2_words32[8 * eight : 8 * eight + 8, :, half * HALF // 2 : (half + 1) * HALF // 2]
+            return load_words("w2_%d_%d" % (half, eight), words)
 
         def load_w2_scales(half):
             load_scales(w2_planes[half], w2_scales32[:, :, half * HALF // 4 : (half + 1) * HALF // 4])
 
         def load_gates(pair):
-            tile = stream_tile("gates%d" % pair, [P, 2, T], F32)
+            tile = keep.tile([P, 2, T], F32, name="gates%d" % pair)
             nc.sync.dma_start(out=tile[:], in_=gate[2 * pair : 2 * pair + 2].rearrange("r p t -> p r t"))
             return [tile[:, 0, :], tile[:, 1, :]]
 
@@ -105,23 +102,23 @@ def tile_moe_ogt_relu2_sigmoid_kernel(
         nc.sync.dma_start(out=x_tile[:], in_=x_words[0].rearrange("p t d -> p (t d)").bitcast(I32))
         w1_tiles = []
         for i, (a, b) in enumerate(W1_LOADS):
-            w1_tiles.append(load_words(stream_tile("w1_%d" % i, [P, (b - a) * 2 * H], U8), w1_words32[a:b]))
+            w1_tiles.append(load_words("w1_%d" % i, w1_words32[a:b]))
             if i == 0:
                 load_scales(x_plane, x_scales.bitcast(I32))
-            load_scales(w1_planes[i], w1_scales32[a:b])
+            if i < len(W1_SCALE_LOADS):
+                load_scales(w1_planes[i], w1_scales32[slice(*W1_SCALE_LOADS[i])])
         load_w2_scales(0)
         w2_tiles = {(0, eight): load_w2(0, eight) for eight in range(2)}
-        load_scales(wg_plane, wg_scales.bitcast(I32))
-        wg_tile = load_words(keep.tile([P, 2 * N], U8, name="wg_tile", align_bytes=64), wg_words.bitcast(I32))
-        gates = load_gates(0)
         pos_tiles = []
         for r, pos in enumerate((pos1, pos2, pos3, pos4)):
             pos_tiles.append(keep.tile([P, T // 16], U16, name="pos_tile%d" % r))
             nc.sync.dma_start(pos_tiles[r][:], pos)
-        gates = gates + load_gates(1)
+        gates = load_gates(0) + load_gates(1)
         load_w2_scales(1)
         for eight in (1, 0):
             w2_tiles[1, eight] = load_w2(1, eight)
+        load_scales(wg_plane, wg_scales.bitcast(I32))
+        wg_tile = load_words("wg_tile", wg_words.bitcast(I32))
 
         h_words = keep.tile([P, SLOTS], U32, name="h_words", align_bytes=64)
         h_plane = keep.tile([P, SLOTS], U8, name="h_plane", align_bytes=64)
@@ -150,6 +147,7 @@ def tile_moe_ogt_relu2_sigmoid_kernel(
         def first_product(e):
             g, in_gather = locate(GATHERS, e)
             load, in_load = locate(W1_LOADS, e)
+            plane, in_plane = locate(W1_SCALE_LOADS, e)
             slots = slice(in_gather * C, (in_gather + 1) * C)
             bank = banks[e % PRODUCT_BANKS]
             nc.tensor.matmul_mx(
@@ -157,7 +155,7 @@ def tile_moe_ogt_relu2_sigmoid_kernel(
                 lhsT=slot_words[g % WORD_TILES][:, slots].bitcast(FP8X4),
                 lhsT_scale=slot_planes[g][:, slots],
                 rhs=w1_tiles[load][:, in_load * 2 * H : (in_load + 1) * 2 * H].bitcast(FP4X4),
-                rhs_scale=w1_planes[load][:, in_load * H : (in_load + 1) * H],
+                rhs_scale=w1_planes[plane][:, in_plane * H : (in_plane + 1) * H],
                 start=True, stop=True,
             )
             src = bank[:].rearrange("p (m u v) -> p u m v", u=2, v=2)
@@ -174,7 +172,6 @@ def tile_moe_ogt_relu2_sigmoid_kernel(
             q, in_tile = locate(QUANTISE, e)
             dst = h_tiles[q][:, in_tile * H : (in_tile + 1) * H].rearrange("p (s d) -> p s d", d=4)
             nc.scalar.activation(dst, bank[:].rearrange("p (d s) -> p s d", d=4), ACT.Square)
-            return bank
 
         def quantise(q):
             a, b = QUANTISE[q]
@@ -195,11 +192,14 @@ def tile_moe_ogt_relu2_sigmoid_kernel(
                 )
             copy_out(y[nb][:, first * C : (first + len(experts)) * C], bank[:, 0 : len(experts) * C])
 
-        for g in range(WORD_TILES):
-            gather_words(g)
-        for g in range(len(GATHERS)):
+        for gather in (gather_words, gather_scales):
+            gather(0)
+            gather(1)
+        gather_words(2)
+        for g in range(2, len(GATHERS)):
             gather_scales(g)
-        turn_banks, block_banks = [], []
+        block_steps = [FIRST_BLOCK_STEP + 2 * j for j in range(3)] + [E, E + 1]
+        block_banks = []
         for step in range(E + 2):
             for g in range(len(GATHERS) - WORD_TILES):
                 if GATHERS[g][1] == step + 1:
@@ -209,34 +209,33 @@ def tile_moe_ogt_relu2_sigmoid_kernel(
             if step + 1 < E:
                 first_product(step + 1)
             if 1 <= step <= E:
-                turn_banks.append(turn_and_square(step - 1))
+                turn_and_square(step - 1)
             for q in range(len(QUANTISE)):
                 if QUANTISE[q][1] == step - 1:
                     quantise(q)
-            j = step - (E + 2 - len(FIRST_BLOCK))
-            if j >= 0:
+            if step in block_steps:
+                j = block_steps.index(step)
                 block_banks.append(next_bank())
                 copy_out = nc.scalar.copy if j < FIRST_BLOCK_ON_SCALAR else nc.vector.tensor_copy
                 second_product(0, range(*FIRST_BLOCK[j]), block_banks[j], copy_out)
 
         ring = [banks[0], block_banks[-2], block_banks[-1]]
-        gate_banks = [turn_banks[E - 2], ring[0], ring[2], ring[0]]
-        sum_banks = [ring[1], ring[2]]
-        result_banks = [banks[1], banks[2], turn_banks[E - 1], block_banks[-3], turn_banks[E - 2]]
+        sum_banks = ring[1:]
+        result_banks = [bank for bank in banks if all(bank is not used for used in ring)]
         out_gates = [keep.tile([P, T], F32, name="out_gate%d" % nb) for nb in range(ROW_BLOCKS)]
         part_tiles = [keep.tile([P, T], F32, name="part%d" % i) for i in range(PART_SETS * TOP)]
         pieces = [(nb, 0, T) for nb in range(ROW_BLOCKS - 1)] + [(ROW_BLOCKS - 1, 0, T - P), (ROW_BLOCKS - 1, T - P, T)]
 
         def output_gate(nb):
             nc.tensor.matmul_mx(
-                out=gate_banks[nb][:],
+                out=ring[nb % len(ring)][:],
                 lhsT=wg_tile[:, 2 * nb * P : 2 * (nb + 1) * P].bitcast(FP4X4),
                 lhsT_scale=wg_plane[:, nb * P : (nb + 1) * P],
                 rhs=x_tile[:].bitcast(FP8X4),
                 rhs_scale=x_plane[:],
                 start=True, stop=True,
             )
-            nc.scalar.activation(out_gates[nb][:], gate_banks[nb][:], ACT.Sigmoid)
+            nc.scalar.activation(out_gates[nb][:], ring[nb % len(ring)][:], ACT.Sigmoid)
 
         def combine(i):
             nb, t0, t1 = pieces[i]
@@ -264,11 +263,10 @@ def tile_moe_ogt_relu2_sigmoid_kernel(
             nc.vector.tensor_tensor(result[:], result_banks[i][:, 0 : t1 - t0], out_gates[nb][:, t0:t1], ALU.mult)
             nc.sync.dma_start(out=out[nb * P : (nb + 1) * P, t0:t1], in_=result[:])
 
-        output_gate(0)
         for nb in range(1, ROW_BLOCKS):
             for j, (a, b) in enumerate(reversed(FOURS)):
                 second_product(nb, range(b - 1, a - 1, -1), ring[((nb - 1) * len(FOURS) + j) % len(ring)], nc.scalar.copy)
-        for nb in range(1, ROW_BLOCKS):
+        for nb in range(ROW_BLOCKS):
             output_gate(nb)
         for i in range(len(pieces) + FINISH_LAG):
             if i < len(pieces):

@@ -22,21 +22,20 @@ HALF = N // 2
 LIST_COLS = C // 16
 FLOPS = 2 * 512 * N * T + 2 * (512 * H + H * N) * SLOTS
 
-W1_LOADS = [(0, 2), (2, 5), (5, 10), (10, E)]
-W1_SCALE_LOADS = [(0, 2), (2, 7), (7, E)]
-GATHERS = [(0, 2), (2, 4)] + [(a, a + 3) for a in range(4, E, 3)]
+W1_LOADS = [(0, 2), (2, 4), (4, 8), (8, 12), (12, E)]
+W1_SCALE_LOADS = [(0, 4), (4, E)]
+GATHERS = [(a, a + 2) for a in range(0, E, 2)]
 QUANTISE = [(a, a + 2) for a in range(0, E - 2, 2)] + [(E - 2, E - 1), (E - 1, E)]
 FOURS = [(a, a + 4) for a in range(0, E, 4)]
 FIRST_BLOCK = FOURS[:-1] + [(E - 4, E - 1), (E - 1, E)]
 
-RELU_ON_SCALAR = 7
-FIRST_BLOCK_ON_SCALAR = 2
-WORD_TILES = 3
+PAIRS = E // 2
+FIRST_BLOCK_ON_SCALAR = 3
+WORD_TILES = 2
 RELU_TILES = 4
 PRODUCT_BANKS = 3
 PART_SETS = 3
 FINISH_LAG = 3
-FIRST_BLOCK_STEP = 11
 
 
 def locate(ranges, e):
@@ -59,17 +58,18 @@ def tile_moe_ogt_relu2_sigmoid_kernel(
             return plane
 
         x_plane = zeroed_plane("x_plane", T, nc.gpsimd)
-        w1_planes = [zeroed_plane("w1_plane%d" % i, (b - a) * H, nc.vector) for i, (a, b) in enumerate(W1_SCALE_LOADS)]
-        w2_planes = [zeroed_plane("w2_plane%d" % half, E * HALF, nc.vector) for half in range(2)]
-        wg_plane = zeroed_plane("wg_plane", N, nc.vector)
+        w1_planes = [keep.tile([P, (b - a) * H], U8, name="w1_plane%d" % a, align_bytes=64) for a, b in W1_SCALE_LOADS]
+        nc.vector.memset(w1_planes[0][:].bitcast(I32), 0)
+        share = (E - W1_SCALE_LOADS[1][0]) * H // 2
+        nc.vector.memset(w1_planes[1][:, 0:share].bitcast(I32), 0)
+        nc.gpsimd.memset(w1_planes[1][:, share : 2 * share].bitcast(I32), 0)
+        wg_plane = zeroed_plane("wg_plane", N, nc.gpsimd)
         ident = keep.tile([P, P], F32, name="ident")
         make_identity(nc, ident[:])
-        preload = keep.tile([P, 1], F32, name="preload")
-        nc.scalar.activation(preload[:], ident[:, 0:1], ACT.Sigmoid)
 
         def load_scales(plane, rows):
             src = rows.rearrange("e (q r) n -> r q e n", r=4)
-            dst = plane[:].bitcast(I32).rearrange("p (e n) -> p e n", e=rows.shape[0])
+            dst = plane.bitcast(I32).rearrange("p (e n) -> p e n", e=rows.shape[0])
             for r in range(4):
                 nc.sync.dma_start(out=dst[r:P:32, :, :], in_=src[r])
 
@@ -78,6 +78,8 @@ def tile_moe_ogt_relu2_sigmoid_kernel(
             dst = tile[:].bitcast(I32).rearrange("p (e n) -> p e n", e=words.shape[0])
             nc.sync.dma_start(out=dst, in_=words.rearrange("e p n -> p e n"))
             return tile
+
+        W2_PLANE_BLOCKS = [(0, 1), (1, 2), (2, 4)]
 
         w1_words32 = w1_words.rearrange("e o p n -> (e o) p n").bitcast(I32)
         w2_words32 = w2_words.rearrange("e o p n -> (e o) p n").bitcast(I32)
@@ -88,8 +90,9 @@ def tile_moe_ogt_relu2_sigmoid_kernel(
             words = w2_words32[8 * eight : 8 * eight + 8, :, half * HALF // 2 : (half + 1) * HALF // 2]
             return load_words("w2_%d_%d" % (half, eight), words)
 
-        def load_w2_scales(half):
-            load_scales(w2_planes[half], w2_scales32[:, :, half * HALF // 4 : (half + 1) * HALF // 4])
+        def load_w2_scales(i):
+            a, b = W2_PLANE_BLOCKS[i]
+            load_scales(w1_tiles[i][:], w2_scales32[:, :, a * P // 4 : b * P // 4])
 
         def load_gates(pair):
             tile = keep.tile([P, 2, T], F32, name="gates%d" % pair)
@@ -98,34 +101,31 @@ def tile_moe_ogt_relu2_sigmoid_kernel(
 
         offs_tile = keep.tile([P, SLOTS // 16], U16, name="offs_tile")
         nc.sync.dma_start(offs_tile[:], offs)
+        load_scales(x_plane[:], x_scales.bitcast(I32))
         x_tile = keep.tile([P, T], I32, name="x_tile", align_bytes=64)
         nc.sync.dma_start(out=x_tile[:], in_=x_words[0].rearrange("p t d -> p (t d)").bitcast(I32))
         w1_tiles = []
         for i, (a, b) in enumerate(W1_LOADS):
             w1_tiles.append(load_words("w1_%d" % i, w1_words32[a:b]))
-            if i == 0:
-                load_scales(x_plane, x_scales.bitcast(I32))
             if i < len(W1_SCALE_LOADS):
-                load_scales(w1_planes[i], w1_scales32[slice(*W1_SCALE_LOADS[i])])
-        load_w2_scales(0)
+                load_scales(w1_planes[i][:], w1_scales32[slice(*W1_SCALE_LOADS[i])])
         w2_tiles = {(0, eight): load_w2(0, eight) for eight in range(2)}
         pos_tiles = []
         for r, pos in enumerate((pos1, pos2, pos3, pos4)):
             pos_tiles.append(keep.tile([P, T // 16], U16, name="pos_tile%d" % r))
             nc.sync.dma_start(pos_tiles[r][:], pos)
         gates = load_gates(0) + load_gates(1)
-        load_w2_scales(1)
         for eight in (1, 0):
             w2_tiles[1, eight] = load_w2(1, eight)
-        load_scales(wg_plane, wg_scales.bitcast(I32))
+        load_scales(wg_plane[:], wg_scales.bitcast(I32))
         wg_tile = load_words("wg_tile", wg_words.bitcast(I32))
 
         h_words = keep.tile([P, SLOTS], U32, name="h_words", align_bytes=64)
         h_plane = keep.tile([P, SLOTS], U8, name="h_plane", align_bytes=64)
         y = [keep.tile([P, SLOTS], F32, name="y%d" % nb) for nb in range(ROW_BLOCKS)]
         banks = [psum.tile([P, 512], F32, name="bank%d" % b) for b in range(8)]
-        slot_words = [keep.tile([P, 3 * C], U32, name="slot_words%d" % i, align_bytes=64) for i in range(WORD_TILES)]
-        slot_planes = [keep.tile([P, 3 * C], U8, name="slot_plane%d" % i, align_bytes=64) for i in range(len(GATHERS))]
+        slot_words = [keep.tile([P, 2 * C], U32, name="slot_words%d" % i, align_bytes=64) for i in range(WORD_TILES)]
+        slot_planes = [keep.tile([P, 2 * C], U8, name="slot_plane%d" % i, align_bytes=64) for i in range(WORD_TILES)]
         relu_tiles = [keep.tile([P, H], F32, name="relu%d" % i) for i in range(RELU_TILES)]
         h_tiles = [keep.tile([P, (b - a) * H], BF16, name="h%d" % a, align_bytes=64) for a, b in QUANTISE]
         handed_out = []
@@ -142,7 +142,7 @@ def tile_moe_ogt_relu2_sigmoid_kernel(
         def gather_scales(g):
             a, b = GATHERS[g]
             entries = offs_tile[:, a * LIST_COLS : b * LIST_COLS]
-            nc.vector.tensor_copy(slot_planes[g][:, 0 : (b - a) * C], x_plane[:].indirect(entries))
+            nc.vector.tensor_copy(slot_planes[g % WORD_TILES][:, 0 : (b - a) * C], x_plane[:].indirect(entries))
 
         def first_product(e):
             g, in_gather = locate(GATHERS, e)
@@ -153,14 +153,17 @@ def tile_moe_ogt_relu2_sigmoid_kernel(
             nc.tensor.matmul_mx(
                 out=bank[:],
                 lhsT=slot_words[g % WORD_TILES][:, slots].bitcast(FP8X4),
-                lhsT_scale=slot_planes[g][:, slots],
+                lhsT_scale=slot_planes[g % WORD_TILES][:, slots],
                 rhs=w1_tiles[load][:, in_load * 2 * H : (in_load + 1) * 2 * H].bitcast(FP4X4),
                 rhs_scale=w1_planes[plane][:, in_plane * H : (in_plane + 1) * H],
                 start=True, stop=True,
             )
+
+        def relu(e):
+            bank = banks[e % PRODUCT_BANKS]
             src = bank[:].rearrange("p (m u v) -> p u m v", u=2, v=2)
             dst = relu_tiles[e % RELU_TILES][:].rearrange("p (u v m) -> p u m v", u=2, v=2)
-            if e < RELU_ON_SCALAR:
+            if e < 2 or (e % 2 == 0 and e < E - 4):
                 nc.scalar.activation(dst, src, ACT.Relu)
             else:
                 nc.vector.tensor_scalar(dst, src, 0.0, None, ALU.max)
@@ -181,43 +184,50 @@ def tile_moe_ogt_relu2_sigmoid_kernel(
             half, col = divmod(nb * P, HALF)
             first = min(experts)
             for e in experts:
-                word_col, scale_col = (e % 8) * HALF + col, e * HALF + col
+                plane, in_plane = locate(W2_PLANE_BLOCKS, nb)
+                blocks = W2_PLANE_BLOCKS[plane][1] - W2_PLANE_BLOCKS[plane][0]
+                word_col, scale_col = (e % 8) * HALF + col, (e * blocks + in_plane) * P
                 nc.tensor.matmul_mx(
                     out=bank[:, (e - first) * C : (e - first + 1) * C],
                     lhsT=w2_tiles[half, e // 8][:, 2 * word_col : 2 * (word_col + P)].bitcast(FP4X4),
-                    lhsT_scale=w2_planes[half][:, scale_col : scale_col + P],
+                    lhsT_scale=w1_tiles[plane][:, scale_col : scale_col + P],
                     rhs=h_words[:, e * C : (e + 1) * C].bitcast(FP8X4),
                     rhs_scale=h_plane[:, e * C : (e + 1) * C],
                     start=True, stop=True,
                 )
             copy_out(y[nb][:, first * C : (first + len(experts)) * C], bank[:, 0 : len(experts) * C])
 
-        for gather in (gather_words, gather_scales):
-            gather(0)
-            gather(1)
-        gather_words(2)
-        for g in range(2, len(GATHERS)):
-            gather_scales(g)
-        block_steps = [FIRST_BLOCK_STEP + 2 * j for j in range(3)] + [E, E + 1]
         block_banks = []
-        for step in range(E + 2):
-            for g in range(len(GATHERS) - WORD_TILES):
-                if GATHERS[g][1] == step + 1:
-                    gather_words(g + WORD_TILES)
-            if step == 0:
-                first_product(0)
-            if step + 1 < E:
-                first_product(step + 1)
-            if 1 <= step <= E:
-                turn_and_square(step - 1)
-            for q in range(len(QUANTISE)):
-                if QUANTISE[q][1] == step - 1:
-                    quantise(q)
-            if step in block_steps:
-                j = block_steps.index(step)
-                block_banks.append(next_bank())
-                copy_out = nc.scalar.copy if j < FIRST_BLOCK_ON_SCALAR else nc.vector.tensor_copy
-                second_product(0, range(*FIRST_BLOCK[j]), block_banks[j], copy_out)
+
+        def first_block(j):
+            block_banks.append(next_bank())
+            copy_out = nc.scalar.copy if j < FIRST_BLOCK_ON_SCALAR else nc.vector.tensor_copy
+            second_product(0, range(*FIRST_BLOCK[j]), block_banks[j], copy_out)
+
+        for g in range(WORD_TILES):
+            gather_scales(g)
+            gather_words(g)
+        for step in range(PAIRS + 1):
+            if step < PAIRS:
+                for e in range(*GATHERS[step]):
+                    first_product(e)
+                    relu(e)
+                for i in range(len(W2_PLANE_BLOCKS)):
+                    if W1_LOADS[i][1] == GATHERS[step][1]:
+                        load_w2_scales(i)
+            if step + WORD_TILES < PAIRS:
+                gather_words(step + WORD_TILES)
+                gather_scales(step + WORD_TILES)
+            if step >= 2:
+                quantise(step - 2)
+            if step >= PAIRS - 2:
+                first_block(step - (PAIRS - 2))
+            if step >= 1:
+                for e in range(*GATHERS[step - 1]):
+                    turn_and_square(e)
+        for j in (0, 1):
+            quantise(PAIRS - 1 + j)
+            first_block(len(FOURS) - 1 + j)
 
         ring = [banks[0], block_banks[-2], block_banks[-1]]
         sum_banks = ring[1:]

@@ -23,13 +23,14 @@ LIST_COLS = C // 16
 FLOPS = 2 * 512 * N * T + 2 * (512 * H + H * N) * SLOTS
 
 W1_LOADS = [(0, 2), (2, 4), (4, 8), (8, 12), (12, E)]
-W1_SCALE_LOADS = [(0, 4), (4, E)]
+W1_SCALE_LOADS = [(0, 2), (2, 8), (8, E)]
 GATHERS = [(a, a + 2) for a in range(0, E, 2)]
 QUANTISE = [(a, a + 2) for a in range(0, E - 2, 2)] + [(E - 2, E - 1), (E - 1, E)]
 FOURS = [(a, a + 4) for a in range(0, E, 4)]
 FIRST_BLOCK = FOURS[:-1] + [(E - 4, E - 1), (E - 1, E)]
 
 PAIRS = E // 2
+GATE_TILE_EXPERT = 4
 FIRST_BLOCK_ON_SCALAR = 3
 WORD_TILES = 2
 RELU_TILES = 4
@@ -59,11 +60,8 @@ def tile_moe_ogt_relu2_sigmoid_kernel(
 
         x_plane = zeroed_plane("x_plane", T, nc.gpsimd)
         w1_planes = [keep.tile([P, (b - a) * H], U8, name="w1_plane%d" % a, align_bytes=64) for a, b in W1_SCALE_LOADS]
-        nc.vector.memset(w1_planes[0][:].bitcast(I32), 0)
-        share = (E - W1_SCALE_LOADS[1][0]) * H // 2
-        nc.vector.memset(w1_planes[1][:, 0:share].bitcast(I32), 0)
-        nc.gpsimd.memset(w1_planes[1][:, share : 2 * share].bitcast(I32), 0)
-        wg_plane = zeroed_plane("wg_plane", N, nc.gpsimd)
+        for plane, engine in zip(w1_planes, (nc.vector, nc.vector, nc.gpsimd)):
+            engine.memset(plane[:].bitcast(I32), 0)
         ident = keep.tile([P, P], F32, name="ident")
         make_identity(nc, ident[:])
 
@@ -73,11 +71,9 @@ def tile_moe_ogt_relu2_sigmoid_kernel(
             for r in range(4):
                 nc.sync.dma_start(out=dst[r:P:32, :, :], in_=src[r])
 
-        def load_words(name, words):
-            tile = keep.tile([P, 4 * words.shape[0] * words.shape[2]], U8, name=name, align_bytes=64)
-            dst = tile[:].bitcast(I32).rearrange("p (e n) -> p e n", e=words.shape[0])
+        def load_words(tile, words):
+            dst = tile.bitcast(I32).rearrange("p (e n) -> p e n", e=words.shape[0])
             nc.sync.dma_start(out=dst, in_=words.rearrange("e p n -> p e n"))
-            return tile
 
         W2_PLANE_BLOCKS = [(0, 1), (1, 2), (2, 4)]
 
@@ -86,39 +82,39 @@ def tile_moe_ogt_relu2_sigmoid_kernel(
         w1_scales32 = w1_scales.rearrange("e o b n -> (e o) b n").bitcast(I32)
         w2_scales32 = w2_scales.rearrange("e o b n -> (e o) b n").bitcast(I32)
 
+        w1_tiles = [keep.tile([P, (b - a) * 2 * H], U8, name="w1_%d" % a, align_bytes=64) for a, b in W1_LOADS]
+        w2_tiles = {(0, eight): keep.tile([P, 8 * 2 * HALF], U8, name="w2_%d" % eight, align_bytes=64) for eight in range(2)}
+        w2_tiles[1, 1], w2_tiles[1, 0] = w1_tiles[3], w1_tiles[4]
+        gate_pairs = [keep.tile([P, 2, T], F32, name="gates%d" % pair) for pair in range(TOP // 2)]
+        gates = [gate_pairs[r // 2][:, r % 2, :] for r in range(TOP)]
+
         def load_w2(half, eight):
             words = w2_words32[8 * eight : 8 * eight + 8, :, half * HALF // 2 : (half + 1) * HALF // 2]
-            return load_words("w2_%d_%d" % (half, eight), words)
+            load_words(w2_tiles[half, eight][:], words)
 
         def load_w2_scales(i):
             a, b = W2_PLANE_BLOCKS[i]
             load_scales(w1_tiles[i][:], w2_scales32[:, :, a * P // 4 : b * P // 4])
 
         def load_gates(pair):
-            tile = keep.tile([P, 2, T], F32, name="gates%d" % pair)
-            nc.sync.dma_start(out=tile[:], in_=gate[2 * pair : 2 * pair + 2].rearrange("r p t -> p r t"))
-            return [tile[:, 0, :], tile[:, 1, :]]
+            nc.sync.dma_start(out=gate_pairs[pair][:], in_=gate[2 * pair : 2 * pair + 2].rearrange("r p t -> p r t"))
 
         offs_tile = keep.tile([P, SLOTS // 16], U16, name="offs_tile")
         nc.sync.dma_start(offs_tile[:], offs)
         load_scales(x_plane[:], x_scales.bitcast(I32))
         x_tile = keep.tile([P, T], I32, name="x_tile", align_bytes=64)
         nc.sync.dma_start(out=x_tile[:], in_=x_words[0].rearrange("p t d -> p (t d)").bitcast(I32))
-        w1_tiles = []
         for i, (a, b) in enumerate(W1_LOADS):
-            w1_tiles.append(load_words("w1_%d" % i, w1_words32[a:b]))
-            if i < len(W1_SCALE_LOADS):
-                load_scales(w1_planes[i][:], w1_scales32[slice(*W1_SCALE_LOADS[i])])
-        w2_tiles = {(0, eight): load_w2(0, eight) for eight in range(2)}
+            load_words(w1_tiles[i][:], w1_words32[a:b])
+            for j, (c, d) in enumerate(W1_SCALE_LOADS):
+                if c == a:
+                    load_scales(w1_planes[j][:], w1_scales32[c:d])
+        for eight in range(2):
+            load_w2(0, eight)
         pos_tiles = []
         for r, pos in enumerate((pos1, pos2, pos3, pos4)):
             pos_tiles.append(keep.tile([P, T // 16], U16, name="pos_tile%d" % r))
             nc.sync.dma_start(pos_tiles[r][:], pos)
-        gates = load_gates(0) + load_gates(1)
-        for eight in (1, 0):
-            w2_tiles[1, eight] = load_w2(1, eight)
-        load_scales(wg_plane[:], wg_scales.bitcast(I32))
-        wg_tile = load_words("wg_tile", wg_words.bitcast(I32))
 
         h_words = keep.tile([P, SLOTS], U32, name="h_words", align_bytes=64)
         h_plane = keep.tile([P, SLOTS], U8, name="h_plane", align_bytes=64)
@@ -129,6 +125,9 @@ def tile_moe_ogt_relu2_sigmoid_kernel(
         relu_tiles = [keep.tile([P, H], F32, name="relu%d" % i) for i in range(RELU_TILES)]
         h_tiles = [keep.tile([P, (b - a) * H], BF16, name="h%d" % a, align_bytes=64) for a, b in QUANTISE]
         handed_out = []
+
+        def relu_tile(e):
+            return gates[e - GATE_TILE_EXPERT] if 0 <= e - GATE_TILE_EXPERT < TOP else relu_tiles[e % RELU_TILES][:]
 
         def next_bank():
             handed_out.append(banks[PRODUCT_BANKS + len(handed_out) % (len(banks) - PRODUCT_BANKS)])
@@ -162,7 +161,7 @@ def tile_moe_ogt_relu2_sigmoid_kernel(
         def relu(e):
             bank = banks[e % PRODUCT_BANKS]
             src = bank[:].rearrange("p (m u v) -> p u m v", u=2, v=2)
-            dst = relu_tiles[e % RELU_TILES][:].rearrange("p (u v m) -> p u m v", u=2, v=2)
+            dst = relu_tile(e).rearrange("p (u v m) -> p u m v", u=2, v=2)
             if e < 2 or (e % 2 == 0 and e < E - 4):
                 nc.scalar.activation(dst, src, ACT.Relu)
             else:
@@ -171,7 +170,7 @@ def tile_moe_ogt_relu2_sigmoid_kernel(
         def turn_and_square(e):
             bank = next_bank()
             for d in range(4):
-                nc.tensor.transpose(bank[:, d * C : (d + 1) * C], relu_tiles[e % RELU_TILES][:, d * P : (d + 1) * P], ident[:])
+                nc.tensor.transpose(bank[:, d * C : (d + 1) * C], relu_tile(e)[:, d * P : (d + 1) * P], ident[:])
             q, in_tile = locate(QUANTISE, e)
             dst = h_tiles[q][:, in_tile * H : (in_tile + 1) * H].rearrange("p (s d) -> p s d", d=4)
             nc.scalar.activation(dst, bank[:].rearrange("p (d s) -> p s d", d=4), ACT.Square)
@@ -215,37 +214,43 @@ def tile_moe_ogt_relu2_sigmoid_kernel(
                 for i in range(len(W2_PLANE_BLOCKS)):
                     if W1_LOADS[i][1] == GATHERS[step][1]:
                         load_w2_scales(i)
+                for eight in range(2):
+                    if W1_LOADS[4 - eight][1] == GATHERS[step][1]:
+                        load_w2(1, eight)
             if step + WORD_TILES < PAIRS:
                 gather_words(step + WORD_TILES)
                 gather_scales(step + WORD_TILES)
             if step >= 2:
                 quantise(step - 2)
-            if step >= PAIRS - 2:
-                first_block(step - (PAIRS - 2))
+            if step >= 4 and step % 2 == 0:
+                first_block(step // 2 - 2)
             if step >= 1:
                 for e in range(*GATHERS[step - 1]):
                     turn_and_square(e)
+                if 0 <= step - 1 - GATE_TILE_EXPERT // 2 < TOP // 2:
+                    load_gates(step - 1 - GATE_TILE_EXPERT // 2)
         for j in (0, 1):
             quantise(PAIRS - 1 + j)
             first_block(len(FOURS) - 1 + j)
 
         ring = [banks[0], block_banks[-2], block_banks[-1]]
-        sum_banks = ring[1:]
         result_banks = [bank for bank in banks if all(bank is not used for used in ring)]
+        wg_tile = w2_tiles[0, 1][:, 0 : 2 * N]
+        wg_plane = w2_tiles[0, 1][:, 2 * N : 3 * N]
         out_gates = [keep.tile([P, T], F32, name="out_gate%d" % nb) for nb in range(ROW_BLOCKS)]
         part_tiles = [keep.tile([P, T], F32, name="part%d" % i) for i in range(PART_SETS * TOP)]
         pieces = [(nb, 0, T) for nb in range(ROW_BLOCKS - 1)] + [(ROW_BLOCKS - 1, 0, T - P), (ROW_BLOCKS - 1, T - P, T)]
 
         def output_gate(nb):
             nc.tensor.matmul_mx(
-                out=ring[nb % len(ring)][:],
+                out=result_banks[nb][:],
                 lhsT=wg_tile[:, 2 * nb * P : 2 * (nb + 1) * P].bitcast(FP4X4),
                 lhsT_scale=wg_plane[:, nb * P : (nb + 1) * P],
                 rhs=x_tile[:].bitcast(FP8X4),
                 rhs_scale=x_plane[:],
                 start=True, stop=True,
             )
-            nc.scalar.activation(out_gates[nb][:], ring[nb % len(ring)][:], ACT.Sigmoid)
+            nc.scalar.activation(out_gates[nb][:], result_banks[nb][:], ACT.Sigmoid)
 
         def combine(i):
             nb, t0, t1 = pieces[i]
@@ -255,7 +260,7 @@ def tile_moe_ogt_relu2_sigmoid_kernel(
             for r in range(TOP):
                 looked_up = y[nb][:].indirect(pos_tiles[r][:, t0 // 16 : t1 // 16])
                 nc.vector.tensor_tensor(parts[r][:, 0:width], looked_up, gates[r][:, t0:t1], ALU.mult)
-            sums = sum_banks[i % 2]
+            sums = ring[i % len(ring)]
             for r in range(TOP):
                 for cols in blocks:
                     nc.tensor.matmul(
@@ -276,6 +281,9 @@ def tile_moe_ogt_relu2_sigmoid_kernel(
         for nb in range(1, ROW_BLOCKS):
             for j, (a, b) in enumerate(reversed(FOURS)):
                 second_product(nb, range(b - 1, a - 1, -1), ring[((nb - 1) * len(FOURS) + j) % len(ring)], nc.scalar.copy)
+            if nb == 1:
+                load_words(wg_tile, wg_words.bitcast(I32))
+                load_scales(wg_plane, wg_scales.bitcast(I32))
         for nb in range(ROW_BLOCKS):
             output_gate(nb)
         for i in range(len(pieces) + FINISH_LAG):

@@ -24,19 +24,19 @@ FLOPS = 2 * 512 * N * T + 2 * (512 * H + H * N) * SLOTS
 
 W1_LOADS = [(0, 2), (2, 4), (4, 8), (8, 12), (12, E)]
 W1_SCALE_LOADS = [(0, 2), (2, 8), (8, E)]
-GATHERS = [(a, a + 2) for a in range(0, E, 2)]
+W2_PLANE_BLOCKS = [(0, 1), (1, 2), (2, 4)]
+GATHERS = [(0, 2), (2, 4)] + [(a, a + 3) for a in range(4, E, 3)]
 QUANTISE = [(a, a + 2) for a in range(0, E - 2, 2)] + [(E - 2, E - 1), (E - 1, E)]
 FOURS = [(a, a + 4) for a in range(0, E, 4)]
 FIRST_BLOCK = FOURS[:-1] + [(E - 4, E - 1), (E - 1, E)]
 
-PAIRS = E // 2
-GATE_TILE_EXPERT = 4
-FIRST_BLOCK_ON_SCALAR = 3
-WORD_TILES = 2
-RELU_TILES = 4
+RELU_ON_SCALAR = 8
+FIRST_BLOCK_STEPS = (6, 7, 8)
+GATE_TILE_PAIR = 2
+FIRST_BLOCK_ON_SCALAR = (0, 1)
+RELU_TILES = 2
 PRODUCT_BANKS = 3
 PART_SETS = 3
-FINISH_LAG = 3
 
 
 def locate(ranges, e):
@@ -62,6 +62,7 @@ def tile_moe_ogt_relu2_sigmoid_kernel(
         w1_planes = [keep.tile([P, (b - a) * H], U8, name="w1_plane%d" % a, align_bytes=64) for a, b in W1_SCALE_LOADS]
         for plane, engine in zip(w1_planes, (nc.vector, nc.vector, nc.gpsimd)):
             engine.memset(plane[:].bitcast(I32), 0)
+        first_w2_plane = zeroed_plane("first_w2_plane", E * P, nc.gpsimd)
         ident = keep.tile([P, P], F32, name="ident")
         make_identity(nc, ident[:])
 
@@ -75,7 +76,6 @@ def tile_moe_ogt_relu2_sigmoid_kernel(
             dst = tile.bitcast(I32).rearrange("p (e n) -> p e n", e=words.shape[0])
             nc.sync.dma_start(out=dst, in_=words.rearrange("e p n -> p e n"))
 
-        W2_PLANE_BLOCKS = [(0, 1), (1, 2), (2, 4)]
 
         w1_words32 = w1_words.rearrange("e o p n -> (e o) p n").bitcast(I32)
         w2_words32 = w2_words.rearrange("e o p n -> (e o) p n").bitcast(I32)
@@ -85,6 +85,7 @@ def tile_moe_ogt_relu2_sigmoid_kernel(
         w1_tiles = [keep.tile([P, (b - a) * 2 * H], U8, name="w1_%d" % a, align_bytes=64) for a, b in W1_LOADS]
         w2_tiles = {(0, eight): keep.tile([P, 8 * 2 * HALF], U8, name="w2_%d" % eight, align_bytes=64) for eight in range(2)}
         w2_tiles[1, 1], w2_tiles[1, 0] = w1_tiles[3], w1_tiles[4]
+        w2_planes = [first_w2_plane, w1_tiles[1], w1_tiles[2]]
         gate_pairs = [keep.tile([P, 2, T], F32, name="gates%d" % pair) for pair in range(TOP // 2)]
         gates = [gate_pairs[r // 2][:, r % 2, :] for r in range(TOP)]
 
@@ -94,7 +95,7 @@ def tile_moe_ogt_relu2_sigmoid_kernel(
 
         def load_w2_scales(i):
             a, b = W2_PLANE_BLOCKS[i]
-            load_scales(w1_tiles[i][:], w2_scales32[:, :, a * P // 4 : b * P // 4])
+            load_scales(w2_planes[i][:], w2_scales32[:, :, a * P // 4 : b * P // 4])
 
         def load_gates(pair):
             nc.sync.dma_start(out=gate_pairs[pair][:], in_=gate[2 * pair : 2 * pair + 2].rearrange("r p t -> p r t"))
@@ -109,8 +110,10 @@ def tile_moe_ogt_relu2_sigmoid_kernel(
             for j, (c, d) in enumerate(W1_SCALE_LOADS):
                 if c == a:
                     load_scales(w1_planes[j][:], w1_scales32[c:d])
-        for eight in range(2):
-            load_w2(0, eight)
+            if i == 2:
+                load_w2_scales(0)
+                load_w2(0, 0)
+        load_w2(0, 1)
         pos_tiles = []
         for r, pos in enumerate((pos1, pos2, pos3, pos4)):
             pos_tiles.append(keep.tile([P, T // 16], U16, name="pos_tile%d" % r))
@@ -120,49 +123,56 @@ def tile_moe_ogt_relu2_sigmoid_kernel(
         h_plane = keep.tile([P, SLOTS], U8, name="h_plane", align_bytes=64)
         y = [keep.tile([P, SLOTS], F32, name="y%d" % nb) for nb in range(ROW_BLOCKS)]
         banks = [psum.tile([P, 512], F32, name="bank%d" % b) for b in range(8)]
-        slot_words = [keep.tile([P, 2 * C], U32, name="slot_words%d" % i, align_bytes=64) for i in range(WORD_TILES)]
-        slot_planes = [keep.tile([P, 2 * C], U8, name="slot_plane%d" % i, align_bytes=64) for i in range(WORD_TILES)]
-        relu_tiles = [keep.tile([P, H], F32, name="relu%d" % i) for i in range(RELU_TILES)]
+        slot_words = [keep.tile([P, 6 * C], U32, name="slot_words%d" % i, align_bytes=64) for i in range(2)]
+        slot_planes = [keep.tile([P, 6 * C], U8, name="slot_plane%d" % i, align_bytes=64) for i in range(2)]
+        relu_tiles = [keep.tile([P, 2, H], F32, name="relu%d" % i) for i in range(RELU_TILES)]
         h_tiles = [keep.tile([P, (b - a) * H], BF16, name="h%d" % a, align_bytes=64) for a, b in QUANTISE]
         handed_out = []
 
-        def relu_tile(e):
-            return gates[e - GATE_TILE_EXPERT] if 0 <= e - GATE_TILE_EXPERT < TOP else relu_tiles[e % RELU_TILES][:]
+        def relu_tile(pair):
+            return gate_pairs[pair - GATE_TILE_PAIR] if 0 <= pair - GATE_TILE_PAIR < TOP // 2 else relu_tiles[pair % RELU_TILES]
 
         def next_bank():
             handed_out.append(banks[PRODUCT_BANKS + len(handed_out) % (len(banks) - PRODUCT_BANKS)])
             return handed_out[-1]
 
+        def slot_columns(g):
+            a, b = GATHERS[g]
+            tile, first = (g, 2) if g < 2 else ((g - 2) // 2, 3 * (g % 2))
+            return tile, first * C, (first + b - a) * C
+
         def gather_words(g):
             a, b = GATHERS[g]
             entries = offs_tile[:, a * LIST_COLS : b * LIST_COLS]
-            nc.vector.tensor_copy(slot_words[g % WORD_TILES][:, 0 : (b - a) * C], x_tile[:].bitcast(U32).indirect(entries))
+            tile, c0, c1 = slot_columns(g)
+            nc.vector.tensor_copy(slot_words[tile][:, c0:c1], x_tile[:].bitcast(U32).indirect(entries))
 
         def gather_scales(g):
             a, b = GATHERS[g]
             entries = offs_tile[:, a * LIST_COLS : b * LIST_COLS]
-            nc.vector.tensor_copy(slot_planes[g % WORD_TILES][:, 0 : (b - a) * C], x_plane[:].indirect(entries))
+            tile, c0, c1 = slot_columns(g)
+            nc.vector.tensor_copy(slot_planes[tile][:, c0:c1], x_plane[:].indirect(entries))
 
-        def first_product(e):
-            g, in_gather = locate(GATHERS, e)
-            load, in_load = locate(W1_LOADS, e)
-            plane, in_plane = locate(W1_SCALE_LOADS, e)
-            slots = slice(in_gather * C, (in_gather + 1) * C)
-            bank = banks[e % PRODUCT_BANKS]
-            nc.tensor.matmul_mx(
-                out=bank[:],
-                lhsT=slot_words[g % WORD_TILES][:, slots].bitcast(FP8X4),
-                lhsT_scale=slot_planes[g % WORD_TILES][:, slots],
-                rhs=w1_tiles[load][:, in_load * 2 * H : (in_load + 1) * 2 * H].bitcast(FP4X4),
-                rhs_scale=w1_planes[plane][:, in_plane * H : (in_plane + 1) * H],
-                start=True, stop=True,
-            )
-
-        def relu(e):
-            bank = banks[e % PRODUCT_BANKS]
-            src = bank[:].rearrange("p (m u v) -> p u m v", u=2, v=2)
-            dst = relu_tile(e).rearrange("p (u v m) -> p u m v", u=2, v=2)
-            if e < 2 or (e % 2 == 0 and e < E - 4):
+        def first_product(pair, half):
+            bank = banks[(2 * pair + half) % PRODUCT_BANKS]
+            for e in (2 * pair, 2 * pair + 1):
+                g, in_gather = locate(GATHERS, e)
+                load, in_load = locate(W1_LOADS, e)
+                plane, in_plane = locate(W1_SCALE_LOADS, e)
+                tile, c0, c1 = slot_columns(g)
+                slots = slice(c0 + in_gather * C, c0 + (in_gather + 1) * C)
+                word_col, scale_col = in_load * H + half * H // 2, in_plane * H + half * H // 2
+                nc.tensor.matmul_mx(
+                    out=bank[:, e % 2 * H // 2 : (e % 2 + 1) * H // 2],
+                    lhsT=slot_words[tile][:, slots].bitcast(FP8X4),
+                    lhsT_scale=slot_planes[tile][:, slots],
+                    rhs=w1_tiles[load][:, 2 * word_col : 2 * word_col + H].bitcast(FP4X4),
+                    rhs_scale=w1_planes[plane][:, scale_col : scale_col + H // 2],
+                    start=True, stop=True,
+                )
+            src = bank[:].rearrange("p (e m d) -> p e d m", e=2, d=4)
+            dst = relu_tile(pair)[:].rearrange("p e (d h m) -> p h e d m", d=4, h=2)[:, half]
+            if 2 * pair + half < RELU_ON_SCALAR:
                 nc.scalar.activation(dst, src, ACT.Relu)
             else:
                 nc.vector.tensor_scalar(dst, src, 0.0, None, ALU.max)
@@ -170,7 +180,7 @@ def tile_moe_ogt_relu2_sigmoid_kernel(
         def turn_and_square(e):
             bank = next_bank()
             for d in range(4):
-                nc.tensor.transpose(bank[:, d * C : (d + 1) * C], relu_tile(e)[:, d * P : (d + 1) * P], ident[:])
+                nc.tensor.transpose(bank[:, d * C : (d + 1) * C], relu_tile(e // 2)[:, e % 2, d * P : (d + 1) * P], ident[:])
             q, in_tile = locate(QUANTISE, e)
             dst = h_tiles[q][:, in_tile * H : (in_tile + 1) * H].rearrange("p (s d) -> p s d", d=4)
             nc.scalar.activation(dst, bank[:].rearrange("p (d s) -> p s d", d=4), ACT.Square)
@@ -189,7 +199,7 @@ def tile_moe_ogt_relu2_sigmoid_kernel(
                 nc.tensor.matmul_mx(
                     out=bank[:, (e - first) * C : (e - first + 1) * C],
                     lhsT=w2_tiles[half, e // 8][:, 2 * word_col : 2 * (word_col + P)].bitcast(FP4X4),
-                    lhsT_scale=w1_tiles[plane][:, scale_col : scale_col + P],
+                    lhsT_scale=w2_planes[plane][:, scale_col : scale_col + P],
                     rhs=h_words[:, e * C : (e + 1) * C].bitcast(FP8X4),
                     rhs_scale=h_plane[:, e * C : (e + 1) * C],
                     start=True, stop=True,
@@ -200,38 +210,38 @@ def tile_moe_ogt_relu2_sigmoid_kernel(
 
         def first_block(j):
             block_banks.append(next_bank())
-            copy_out = nc.scalar.copy if j < FIRST_BLOCK_ON_SCALAR else nc.vector.tensor_copy
+            copy_out = nc.scalar.copy if j in FIRST_BLOCK_ON_SCALAR else nc.vector.tensor_copy
             second_product(0, range(*FIRST_BLOCK[j]), block_banks[j], copy_out)
 
-        for g in range(WORD_TILES):
+        for g in range(2):
             gather_scales(g)
             gather_words(g)
-        for step in range(PAIRS + 1):
-            if step < PAIRS:
-                for e in range(*GATHERS[step]):
-                    first_product(e)
-                    relu(e)
-                for i in range(len(W2_PLANE_BLOCKS)):
-                    if W1_LOADS[i][1] == GATHERS[step][1]:
-                        load_w2_scales(i)
-                for eight in range(2):
-                    if W1_LOADS[4 - eight][1] == GATHERS[step][1]:
-                        load_w2(1, eight)
-            if step + WORD_TILES < PAIRS:
-                gather_words(step + WORD_TILES)
-                gather_scales(step + WORD_TILES)
+        for step in range(E // 2 + 1):
+            if step < E // 2:
+                for half in range(2):
+                    first_product(step, half)
+            if step < 2:
+                for g in (2 * step + 2, 2 * step + 3):
+                    gather_words(g)
+                    gather_scales(g)
+            for i in range(1, len(W2_PLANE_BLOCKS)):
+                if W1_LOADS[i][1] == 2 * step + 2:
+                    load_w2_scales(i)
+            for eight in range(2):
+                if W1_LOADS[4 - eight][1] == 2 * step + 2:
+                    load_w2(1, eight)
             if step >= 2:
                 quantise(step - 2)
-            if step >= 4 and step % 2 == 0:
-                first_block(step // 2 - 2)
+            if step in FIRST_BLOCK_STEPS:
+                first_block(FIRST_BLOCK_STEPS.index(step))
             if step >= 1:
-                for e in range(*GATHERS[step - 1]):
+                for e in (2 * step - 2, 2 * step - 1):
                     turn_and_square(e)
-                if 0 <= step - 1 - GATE_TILE_EXPERT // 2 < TOP // 2:
-                    load_gates(step - 1 - GATE_TILE_EXPERT // 2)
-        for j in (0, 1):
-            quantise(PAIRS - 1 + j)
-            first_block(len(FOURS) - 1 + j)
+            if 0 <= step - 1 - GATE_TILE_PAIR < TOP // 2:
+                load_gates(step - 1 - GATE_TILE_PAIR)
+        for j in range(2):
+            quantise(len(QUANTISE) - 2 + j)
+            first_block(len(FIRST_BLOCK) - 2 + j)
 
         ring = [banks[0], block_banks[-2], block_banks[-1]]
         result_banks = [bank for bank in banks if all(bank is not used for used in ring)]
@@ -240,6 +250,8 @@ def tile_moe_ogt_relu2_sigmoid_kernel(
         out_gates = [keep.tile([P, T], F32, name="out_gate%d" % nb) for nb in range(ROW_BLOCKS)]
         part_tiles = [keep.tile([P, T], F32, name="part%d" % i) for i in range(PART_SETS * TOP)]
         pieces = [(nb, 0, T) for nb in range(ROW_BLOCKS - 1)] + [(ROW_BLOCKS - 1, 0, T - P), (ROW_BLOCKS - 1, T - P, T)]
+
+        first_result = keep.tile([P, T], F32, name="first_result")
 
         def output_gate(nb):
             nc.tensor.matmul_mx(
@@ -274,9 +286,9 @@ def tile_moe_ogt_relu2_sigmoid_kernel(
 
         def finish(i):
             nb, t0, t1 = pieces[i]
-            result = work.tile([P, t1 - t0], F32, name="result", tag="result", bufs=len(pieces))
-            nc.vector.tensor_tensor(result[:], result_banks[i][:, 0 : t1 - t0], out_gates[nb][:, t0:t1], ALU.mult)
-            nc.sync.dma_start(out=out[nb * P : (nb + 1) * P, t0:t1], in_=result[:])
+            result = (gates[i - 1] if i else first_result)[:, 0 : t1 - t0]
+            nc.vector.tensor_tensor(result, result_banks[i][:, 0 : t1 - t0], out_gates[nb][:, t0:t1], ALU.mult)
+            nc.sync.dma_start(out=out[nb * P : (nb + 1) * P, t0:t1], in_=result)
 
         for nb in range(1, ROW_BLOCKS):
             for j, (a, b) in enumerate(reversed(FOURS)):
@@ -286,8 +298,7 @@ def tile_moe_ogt_relu2_sigmoid_kernel(
                 load_scales(wg_plane, wg_scales.bitcast(I32))
         for nb in range(ROW_BLOCKS):
             output_gate(nb)
-        for i in range(len(pieces) + FINISH_LAG):
-            if i < len(pieces):
-                combine(i)
-            if i >= FINISH_LAG:
-                finish(i - FINISH_LAG)
+        for i in range(len(pieces)):
+            combine(i)
+        for i in range(len(pieces)):
+            finish(i)

@@ -23,17 +23,18 @@ LIST_COLS = C // 16
 FLOPS = 2 * 512 * N * T + 2 * (512 * H + H * N) * SLOTS
 
 W1_LOADS = [(0, 2), (2, 4), (4, 8), (8, 12), (12, E)]
-W1_SCALE_LOADS = [(0, 2), (2, 8), (8, E)]
+W1_SCALE_LOADS = [(0, 4), (4, E)]
 W2_PLANE_BLOCKS = [(0, 1), (1, 2), (2, 4)]
 GATHERS = [(0, 2), (2, 4)] + [(a, a + 3) for a in range(4, E, 3)]
 QUANTISE = [(a, a + 2) for a in range(0, E - 2, 2)] + [(E - 2, E - 1), (E - 1, E)]
 FOURS = [(a, a + 4) for a in range(0, E, 4)]
 FIRST_BLOCK = FOURS[:-1] + [(E - 4, E - 1), (E - 1, E)]
 
-RELU_ON_SCALAR = 8
+BOTH_ON_SCALAR = 4
+ONE_ON_SCALAR = 6
 FIRST_BLOCK_STEPS = (6, 7, 8)
 GATE_TILE_PAIR = 2
-FIRST_BLOCK_ON_SCALAR = (0, 1)
+FIRST_BLOCK_ON_SCALAR = (0,)
 RELU_TILES = 2
 PRODUCT_BANKS = 3
 PART_SETS = 3
@@ -60,8 +61,10 @@ def tile_moe_ogt_relu2_sigmoid_kernel(
 
         x_plane = zeroed_plane("x_plane", T, nc.gpsimd)
         w1_planes = [keep.tile([P, (b - a) * H], U8, name="w1_plane%d" % a, align_bytes=64) for a, b in W1_SCALE_LOADS]
-        for plane, engine in zip(w1_planes, (nc.vector, nc.vector, nc.gpsimd)):
-            engine.memset(plane[:].bitcast(I32), 0)
+        nc.vector.memset(w1_planes[0][:].bitcast(I32), 0)
+        share = (E - W1_SCALE_LOADS[1][0]) * H // 2
+        nc.vector.memset(w1_planes[1][:, 0:share].bitcast(I32), 0)
+        nc.gpsimd.memset(w1_planes[1][:, share : 2 * share].bitcast(I32), 0)
         first_w2_plane = zeroed_plane("first_w2_plane", E * P, nc.gpsimd)
         ident = keep.tile([P, P], F32, name="ident")
         make_identity(nc, ident[:])
@@ -110,7 +113,7 @@ def tile_moe_ogt_relu2_sigmoid_kernel(
             for j, (c, d) in enumerate(W1_SCALE_LOADS):
                 if c == a:
                     load_scales(w1_planes[j][:], w1_scales32[c:d])
-            if i == 2:
+            if i == 3:
                 load_w2_scales(0)
                 load_w2(0, 0)
         load_w2(0, 1)
@@ -172,7 +175,7 @@ def tile_moe_ogt_relu2_sigmoid_kernel(
                 )
             src = bank[:].rearrange("p (e m d) -> p e d m", e=2, d=4)
             dst = relu_tile(pair)[:].rearrange("p e (d h m) -> p h e d m", d=4, h=2)[:, half]
-            if 2 * pair + half < RELU_ON_SCALAR:
+            if pair < BOTH_ON_SCALAR or (half == 0 and pair < ONE_ON_SCALAR):
                 nc.scalar.activation(dst, src, ACT.Relu)
             else:
                 nc.vector.tensor_scalar(dst, src, 0.0, None, ALU.max)

@@ -18,7 +18,6 @@ P = 128
 T, E, C, H, N, TOP = 512, 16, 128, 512, 512, 4
 SLOTS = E * C
 ROW_BLOCKS = N // P
-HALF = N // 2
 LIST_COLS = C // 16
 FLOPS = 2 * 512 * N * T + 2 * (512 * H + H * N) * SLOTS
 
@@ -31,10 +30,9 @@ FOURS = [(a, a + 4) for a in range(0, E, 4)]
 FIRST_BLOCK = FOURS[:-1] + [(E - 4, E - 1), (E - 1, E)]
 
 BOTH_ON_SCALAR = 4
-ONE_ON_SCALAR = 6
-FIRST_BLOCK_STEPS = (6, 7, 8)
+ONE_ON_SCALAR = 5
 GATE_TILE_PAIR = 2
-FIRST_BLOCK_ON_SCALAR = (0,)
+FIRST_BLOCK_ON_SCALAR = (2, 3)
 RELU_TILES = 2
 PRODUCT_BANKS = 3
 PART_SETS = 3
@@ -86,15 +84,11 @@ def tile_moe_ogt_relu2_sigmoid_kernel(
         w2_scales32 = w2_scales.rearrange("e o b n -> (e o) b n").bitcast(I32)
 
         w1_tiles = [keep.tile([P, (b - a) * 2 * H], U8, name="w1_%d" % a, align_bytes=64) for a, b in W1_LOADS]
-        w2_tiles = {(0, eight): keep.tile([P, 8 * 2 * HALF], U8, name="w2_%d" % eight, align_bytes=64) for eight in range(2)}
-        w2_tiles[1, 1], w2_tiles[1, 0] = w1_tiles[3], w1_tiles[4]
+        w2_first = keep.tile([P, E * 2 * P], U8, name="w2_first", align_bytes=64)
+        w2_rest = [keep.tile([P, 8 * 2 * (N - P)], U8, name="w2_rest%d" % eight, align_bytes=64) for eight in range(2)]
         w2_planes = [first_w2_plane, w1_tiles[1], w1_tiles[2]]
         gate_pairs = [keep.tile([P, 2, T], F32, name="gates%d" % pair) for pair in range(TOP // 2)]
         gates = [gate_pairs[r // 2][:, r % 2, :] for r in range(TOP)]
-
-        def load_w2(half, eight):
-            words = w2_words32[8 * eight : 8 * eight + 8, :, half * HALF // 2 : (half + 1) * HALF // 2]
-            load_words(w2_tiles[half, eight][:], words)
 
         def load_w2_scales(i):
             a, b = W2_PLANE_BLOCKS[i]
@@ -113,14 +107,14 @@ def tile_moe_ogt_relu2_sigmoid_kernel(
             for j, (c, d) in enumerate(W1_SCALE_LOADS):
                 if c == a:
                     load_scales(w1_planes[j][:], w1_scales32[c:d])
-            if i == 3:
-                load_w2_scales(0)
-                load_w2(0, 0)
-        load_w2(0, 1)
+        load_w2_scales(0)
+        load_words(w2_first[:], w2_words32[:, :, 0 : P // 2])
         pos_tiles = []
         for r, pos in enumerate((pos1, pos2, pos3, pos4)):
             pos_tiles.append(keep.tile([P, T // 16], U16, name="pos_tile%d" % r))
             nc.sync.dma_start(pos_tiles[r][:], pos)
+        for eight in (1, 0):
+            load_words(w2_rest[eight][:], w2_words32[8 * eight : 8 * eight + 8, :, P // 2 : N // 2])
 
         h_words = keep.tile([P, SLOTS], U32, name="h_words", align_bytes=64)
         h_plane = keep.tile([P, SLOTS], U8, name="h_plane", align_bytes=64)
@@ -193,15 +187,15 @@ def tile_moe_ogt_relu2_sigmoid_kernel(
             nc.vector.quantize_mx(out=h_words[:, a * C : b * C].bitcast(FP8X4), scales=h_plane[:, a * C : b * C], in_=h_tiles[q][:])
 
         def second_product(nb, experts, bank, copy_out):
-            half, col = divmod(nb * P, HALF)
             first = min(experts)
             for e in experts:
                 plane, in_plane = locate(W2_PLANE_BLOCKS, nb)
                 blocks = W2_PLANE_BLOCKS[plane][1] - W2_PLANE_BLOCKS[plane][0]
-                word_col, scale_col = (e % 8) * HALF + col, (e * blocks + in_plane) * P
+                words, word_col = (w2_rest[e // 8], e % 8 * (N - P) + (nb - 1) * P) if nb else (w2_first, e * P)
+                scale_col = (e * blocks + in_plane) * P
                 nc.tensor.matmul_mx(
                     out=bank[:, (e - first) * C : (e - first + 1) * C],
-                    lhsT=w2_tiles[half, e // 8][:, 2 * word_col : 2 * (word_col + P)].bitcast(FP4X4),
+                    lhsT=words[:, 2 * word_col : 2 * (word_col + P)].bitcast(FP4X4),
                     lhsT_scale=w2_planes[plane][:, scale_col : scale_col + P],
                     rhs=h_words[:, e * C : (e + 1) * C].bitcast(FP8X4),
                     rhs_scale=h_plane[:, e * C : (e + 1) * C],
@@ -212,9 +206,8 @@ def tile_moe_ogt_relu2_sigmoid_kernel(
         block_banks = []
 
         def first_block(j):
-            block_banks.append(next_bank())
-            copy_out = nc.scalar.copy if j in FIRST_BLOCK_ON_SCALAR else nc.vector.tensor_copy
-            second_product(0, range(*FIRST_BLOCK[j]), block_banks[j], copy_out)
+            block_banks.append(banks[(E - PRODUCT_BANKS + j) % PRODUCT_BANKS] if j < PRODUCT_BANKS else next_bank())
+            second_product(0, range(*FIRST_BLOCK[j]), block_banks[j], nc.scalar.copy if j in FIRST_BLOCK_ON_SCALAR else nc.vector.tensor_copy)
 
         for g in range(2):
             gather_scales(g)
@@ -230,13 +223,8 @@ def tile_moe_ogt_relu2_sigmoid_kernel(
             for i in range(1, len(W2_PLANE_BLOCKS)):
                 if W1_LOADS[i][1] == 2 * step + 2:
                     load_w2_scales(i)
-            for eight in range(2):
-                if W1_LOADS[4 - eight][1] == 2 * step + 2:
-                    load_w2(1, eight)
             if step >= 2:
                 quantise(step - 2)
-            if step in FIRST_BLOCK_STEPS:
-                first_block(FIRST_BLOCK_STEPS.index(step))
             if step >= 1:
                 for e in (2 * step - 2, 2 * step - 1):
                     turn_and_square(e)
@@ -244,12 +232,13 @@ def tile_moe_ogt_relu2_sigmoid_kernel(
                 load_gates(step - 1 - GATE_TILE_PAIR)
         for j in range(2):
             quantise(len(QUANTISE) - 2 + j)
-            first_block(len(FIRST_BLOCK) - 2 + j)
+        for j in range(len(FIRST_BLOCK)):
+            first_block(j)
 
-        ring = [banks[0], block_banks[-2], block_banks[-1]]
+        ring = [block_banks[0], block_banks[-2], block_banks[-1]]
         result_banks = [bank for bank in banks if all(bank is not used for used in ring)]
-        wg_tile = w2_tiles[0, 1][:, 0 : 2 * N]
-        wg_plane = w2_tiles[0, 1][:, 2 * N : 3 * N]
+        wg_tile = w2_first[:, (E - 4) * 2 * P : E * 2 * P]
+        wg_plane = first_w2_plane[:, (E - 4) * P : E * P]
         out_gates = [keep.tile([P, T], F32, name="out_gate%d" % nb) for nb in range(ROW_BLOCKS)]
         part_tiles = [keep.tile([P, T], F32, name="part%d" % i) for i in range(PART_SETS * TOP)]
         pieces = [(nb, 0, T) for nb in range(ROW_BLOCKS - 1)] + [(ROW_BLOCKS - 1, 0, T - P), (ROW_BLOCKS - 1, T - P, T)]

@@ -21,9 +21,8 @@ ROW_BLOCKS = N // P
 LIST_COLS = C // 16
 FLOPS = 2 * 512 * N * T + 2 * (512 * H + H * N) * SLOTS
 
-W1_LOADS = [(0, 2), (2, 4), (4, 8), (8, 12), (12, E)]
+W1_LOADS = [(a, a + 4) for a in range(0, E, 4)]
 W1_SCALE_LOADS = [(0, 4), (4, E)]
-W2_PLANE_BLOCKS = [(0, 1), (1, 2), (2, 4)]
 GATHERS = [(0, 2), (2, 4)] + [(a, a + 3) for a in range(4, E, 3)]
 QUANTISE = [(a, a + 2) for a in range(0, E - 2, 2)] + [(E - 2, E - 1), (E - 1, E)]
 FOURS = [(a, a + 4) for a in range(0, E, 4)]
@@ -31,9 +30,8 @@ FIRST_BLOCK = FOURS[:-1] + [(E - 4, E - 1), (E - 1, E)]
 
 BOTH_ON_SCALAR = 4
 ONE_ON_SCALAR = 5
-GATE_TILE_PAIR = 2
 FIRST_BLOCK_ON_SCALAR = (2, 3)
-RELU_TILES = 2
+RELU_TILES = 3
 PRODUCT_BANKS = 3
 PART_SETS = 3
 
@@ -63,7 +61,7 @@ def tile_moe_ogt_relu2_sigmoid_kernel(
         share = (E - W1_SCALE_LOADS[1][0]) * H // 2
         nc.vector.memset(w1_planes[1][:, 0:share].bitcast(I32), 0)
         nc.gpsimd.memset(w1_planes[1][:, share : 2 * share].bitcast(I32), 0)
-        first_w2_plane = zeroed_plane("first_w2_plane", E * P, nc.gpsimd)
+        first_w2_plane = zeroed_plane("first_w2_plane", E * N // 2, nc.gpsimd)
         ident = keep.tile([P, P], F32, name="ident")
         make_identity(nc, ident[:])
 
@@ -86,35 +84,28 @@ def tile_moe_ogt_relu2_sigmoid_kernel(
         w1_tiles = [keep.tile([P, (b - a) * 2 * H], U8, name="w1_%d" % a, align_bytes=64) for a, b in W1_LOADS]
         w2_first = keep.tile([P, E * 2 * P], U8, name="w2_first", align_bytes=64)
         w2_rest = [keep.tile([P, 8 * 2 * (N - P)], U8, name="w2_rest%d" % eight, align_bytes=64) for eight in range(2)]
-        w2_planes = [first_w2_plane, w1_tiles[1], w1_tiles[2]]
+        w2_planes = [first_w2_plane, w1_tiles[0]]
         gate_pairs = [keep.tile([P, 2, T], F32, name="gates%d" % pair) for pair in range(TOP // 2)]
         gates = [gate_pairs[r // 2][:, r % 2, :] for r in range(TOP)]
-
-        def load_w2_scales(i):
-            a, b = W2_PLANE_BLOCKS[i]
-            load_scales(w2_planes[i][:], w2_scales32[:, :, a * P // 4 : b * P // 4])
-
-        def load_gates(pair):
-            nc.sync.dma_start(out=gate_pairs[pair][:], in_=gate[2 * pair : 2 * pair + 2].rearrange("r p t -> p r t"))
 
         offs_tile = keep.tile([P, SLOTS // 16], U16, name="offs_tile")
         nc.sync.dma_start(offs_tile[:], offs)
         load_scales(x_plane[:], x_scales.bitcast(I32))
         x_tile = keep.tile([P, T], I32, name="x_tile", align_bytes=64)
         nc.sync.dma_start(out=x_tile[:], in_=x_words[0].rearrange("p t d -> p (t d)").bitcast(I32))
-        for i, (a, b) in enumerate(W1_LOADS):
-            load_words(w1_tiles[i][:], w1_words32[a:b])
-            for j, (c, d) in enumerate(W1_SCALE_LOADS):
-                if c == a:
-                    load_scales(w1_planes[j][:], w1_scales32[c:d])
-        load_w2_scales(0)
+        for tile, (a, b) in zip(w1_tiles, W1_LOADS):
+            load_words(tile[:], w1_words32[a:b])
+            if a == 0:
+                for plane, (c, d) in zip(w1_planes, W1_SCALE_LOADS):
+                    load_scales(plane[:], w1_scales32[c:d])
+        load_scales(w2_planes[0][:], w2_scales32[:, :, 0 : N // 8])
         load_words(w2_first[:], w2_words32[:, :, 0 : P // 2])
         pos_tiles = []
         for r, pos in enumerate((pos1, pos2, pos3, pos4)):
             pos_tiles.append(keep.tile([P, T // 16], U16, name="pos_tile%d" % r))
             nc.sync.dma_start(pos_tiles[r][:], pos)
-        for eight in (1, 0):
-            load_words(w2_rest[eight][:], w2_words32[8 * eight : 8 * eight + 8, :, P // 2 : N // 2])
+        for pair in range(TOP // 2):
+            nc.sync.dma_start(out=gate_pairs[pair][:], in_=gate[2 * pair : 2 * pair + 2].rearrange("r p t -> p r t"))
 
         h_words = keep.tile([P, SLOTS], U32, name="h_words", align_bytes=64)
         h_plane = keep.tile([P, SLOTS], U8, name="h_plane", align_bytes=64)
@@ -127,7 +118,7 @@ def tile_moe_ogt_relu2_sigmoid_kernel(
         handed_out = []
 
         def relu_tile(pair):
-            return gate_pairs[pair - GATE_TILE_PAIR] if 0 <= pair - GATE_TILE_PAIR < TOP // 2 else relu_tiles[pair % RELU_TILES]
+            return relu_tiles[pair % RELU_TILES]
 
         def next_bank():
             handed_out.append(banks[PRODUCT_BANKS + len(handed_out) % (len(banks) - PRODUCT_BANKS)])
@@ -189,14 +180,12 @@ def tile_moe_ogt_relu2_sigmoid_kernel(
         def second_product(nb, experts, bank, copy_out):
             first = min(experts)
             for e in experts:
-                plane, in_plane = locate(W2_PLANE_BLOCKS, nb)
-                blocks = W2_PLANE_BLOCKS[plane][1] - W2_PLANE_BLOCKS[plane][0]
                 words, word_col = (w2_rest[e // 8], e % 8 * (N - P) + (nb - 1) * P) if nb else (w2_first, e * P)
-                scale_col = (e * blocks + in_plane) * P
+                plane, scale_col = w2_planes[nb // 2], (2 * e + nb % 2) * P
                 nc.tensor.matmul_mx(
                     out=bank[:, (e - first) * C : (e - first + 1) * C],
                     lhsT=words[:, 2 * word_col : 2 * (word_col + P)].bitcast(FP4X4),
-                    lhsT_scale=w2_planes[plane][:, scale_col : scale_col + P],
+                    lhsT_scale=plane[:, scale_col : scale_col + P],
                     rhs=h_words[:, e * C : (e + 1) * C].bitcast(FP8X4),
                     rhs_scale=h_plane[:, e * C : (e + 1) * C],
                     start=True, stop=True,
@@ -220,16 +209,15 @@ def tile_moe_ogt_relu2_sigmoid_kernel(
                 for g in (2 * step + 2, 2 * step + 3):
                     gather_words(g)
                     gather_scales(g)
-            for i in range(1, len(W2_PLANE_BLOCKS)):
-                if W1_LOADS[i][1] == 2 * step + 2:
-                    load_w2_scales(i)
+            if 2 * step + 2 == W1_LOADS[0][1]:
+                load_scales(w2_planes[1][:], w2_scales32[:, :, N // 8 : N // 4])
             if step >= 2:
                 quantise(step - 2)
             if step >= 1:
                 for e in (2 * step - 2, 2 * step - 1):
                     turn_and_square(e)
-            if 0 <= step - 1 - GATE_TILE_PAIR < TOP // 2:
-                load_gates(step - 1 - GATE_TILE_PAIR)
+        for eight in (1, 0):
+            load_words(w2_rest[eight][:], w2_words32[8 * eight : 8 * eight + 8, :, P // 2 : N // 2])
         for j in range(2):
             quantise(len(QUANTISE) - 2 + j)
         for j in range(len(FIRST_BLOCK)):
@@ -238,7 +226,7 @@ def tile_moe_ogt_relu2_sigmoid_kernel(
         ring = [block_banks[0], block_banks[-2], block_banks[-1]]
         result_banks = [bank for bank in banks if all(bank is not used for used in ring)]
         wg_tile = w2_first[:, (E - 4) * 2 * P : E * 2 * P]
-        wg_plane = first_w2_plane[:, (E - 4) * P : E * P]
+        wg_plane = w2_first[:, (E - 6) * 2 * P : (E - 4) * 2 * P]
         out_gates = [keep.tile([P, T], F32, name="out_gate%d" % nb) for nb in range(ROW_BLOCKS)]
         part_tiles = [keep.tile([P, T], F32, name="part%d" % i) for i in range(PART_SETS * TOP)]
         pieces = [(nb, 0, T) for nb in range(ROW_BLOCKS - 1)] + [(ROW_BLOCKS - 1, 0, T - P), (ROW_BLOCKS - 1, T - P, T)]

@@ -61,7 +61,6 @@ def tile_moe_ogt_relu2_sigmoid_kernel(
         share = (E - W1_SCALE_LOADS[1][0]) * H // 2
         nc.vector.memset(w1_planes[1][:, 0:share].bitcast(I32), 0)
         nc.gpsimd.memset(w1_planes[1][:, share : 2 * share].bitcast(I32), 0)
-        first_w2_plane = zeroed_plane("first_w2_plane", E * N // 2, nc.gpsimd)
         ident = keep.tile([P, P], F32, name="ident")
         make_identity(nc, ident[:])
 
@@ -82,9 +81,8 @@ def tile_moe_ogt_relu2_sigmoid_kernel(
         w2_scales32 = w2_scales.rearrange("e o b n -> (e o) b n").bitcast(I32)
 
         w1_tiles = [keep.tile([P, (b - a) * 2 * H], U8, name="w1_%d" % a, align_bytes=64) for a, b in W1_LOADS]
-        w2_first = keep.tile([P, E * 2 * P], U8, name="w2_first", align_bytes=64)
-        w2_rest = [keep.tile([P, 8 * 2 * (N - P)], U8, name="w2_rest%d" % eight, align_bytes=64) for eight in range(2)]
-        w2_planes = [first_w2_plane, w1_tiles[0]]
+        w2_tiles = [[keep.tile([P, 8 * N], U8, name="w2_%d_%d" % (half, eight), align_bytes=64) for eight in range(2)] for half in range(2)]
+        w2_planes = w1_tiles[0:2]
         gate_pairs = [keep.tile([P, 2, T], F32, name="gates%d" % pair) for pair in range(TOP // 2)]
         gates = [gate_pairs[r // 2][:, r % 2, :] for r in range(TOP)]
 
@@ -98,14 +96,12 @@ def tile_moe_ogt_relu2_sigmoid_kernel(
             if a == 0:
                 for plane, (c, d) in zip(w1_planes, W1_SCALE_LOADS):
                     load_scales(plane[:], w1_scales32[c:d])
-        load_scales(w2_planes[0][:], w2_scales32[:, :, 0 : N // 8])
-        load_words(w2_first[:], w2_words32[:, :, 0 : P // 2])
+        for eight in range(2):
+            load_words(w2_tiles[0][eight][:], w2_words32[8 * eight : 8 * eight + 8, :, 0 : N // 4])
         pos_tiles = []
         for r, pos in enumerate((pos1, pos2, pos3, pos4)):
             pos_tiles.append(keep.tile([P, T // 16], U16, name="pos_tile%d" % r))
             nc.sync.dma_start(pos_tiles[r][:], pos)
-        for pair in range(TOP // 2):
-            nc.sync.dma_start(out=gate_pairs[pair][:], in_=gate[2 * pair : 2 * pair + 2].rearrange("r p t -> p r t"))
 
         h_words = keep.tile([P, SLOTS], U32, name="h_words", align_bytes=64)
         h_plane = keep.tile([P, SLOTS], U8, name="h_plane", align_bytes=64)
@@ -180,7 +176,7 @@ def tile_moe_ogt_relu2_sigmoid_kernel(
         def second_product(nb, experts, bank, copy_out):
             first = min(experts)
             for e in experts:
-                words, word_col = (w2_rest[e // 8], e % 8 * (N - P) + (nb - 1) * P) if nb else (w2_first, e * P)
+                words, word_col = w2_tiles[nb // 2][e // 8], (e % 8 * 2 + nb % 2) * P
                 plane, scale_col = w2_planes[nb // 2], (2 * e + nb % 2) * P
                 nc.tensor.matmul_mx(
                     out=bank[:, (e - first) * C : (e - first + 1) * C],
@@ -209,15 +205,17 @@ def tile_moe_ogt_relu2_sigmoid_kernel(
                 for g in (2 * step + 2, 2 * step + 3):
                     gather_words(g)
                     gather_scales(g)
-            if 2 * step + 2 == W1_LOADS[0][1]:
-                load_scales(w2_planes[1][:], w2_scales32[:, :, N // 8 : N // 4])
+            for half in range(2):
+                if 2 * step + 2 == W1_LOADS[half][1]:
+                    load_scales(w2_planes[half][:], w2_scales32[:, :, half * N // 8 : (half + 1) * N // 8])
+                    nc.sync.dma_start(out=gate_pairs[half][:], in_=gate[2 * half : 2 * half + 2].rearrange("r p t -> p r t"))
             if step >= 2:
                 quantise(step - 2)
             if step >= 1:
                 for e in (2 * step - 2, 2 * step - 1):
                     turn_and_square(e)
         for eight in (1, 0):
-            load_words(w2_rest[eight][:], w2_words32[8 * eight : 8 * eight + 8, :, P // 2 : N // 2])
+            load_words(w2_tiles[1][eight][:], w2_words32[8 * eight : 8 * eight + 8, :, N // 4 : N // 2])
         for j in range(2):
             quantise(len(QUANTISE) - 2 + j)
         for j in range(len(FIRST_BLOCK)):
@@ -225,8 +223,8 @@ def tile_moe_ogt_relu2_sigmoid_kernel(
 
         ring = [block_banks[0], block_banks[-2], block_banks[-1]]
         result_banks = [bank for bank in banks if all(bank is not used for used in ring)]
-        wg_tile = w2_first[:, (E - 4) * 2 * P : E * 2 * P]
-        wg_plane = w2_first[:, (E - 6) * 2 * P : (E - 4) * 2 * P]
+        wg_tile = w2_tiles[0][1][:, 6 * N : 8 * N]
+        wg_plane = w2_tiles[0][1][:, 5 * N : 6 * N]
         out_gates = [keep.tile([P, T], F32, name="out_gate%d" % nb) for nb in range(ROW_BLOCKS)]
         part_tiles = [keep.tile([P, T], F32, name="part%d" % i) for i in range(PART_SETS * TOP)]
         pieces = [(nb, 0, T) for nb in range(ROW_BLOCKS - 1)] + [(ROW_BLOCKS - 1, 0, T - P), (ROW_BLOCKS - 1, T - P, T)]

@@ -30,7 +30,7 @@ FIRST_BLOCK = FOURS[:-1] + [(E - 4, E - 1), (E - 1, E)]
 
 BOTH_ON_SCALAR = 4
 ONE_ON_SCALAR = 5
-FIRST_BLOCK_ON_SCALAR = (2, 3)
+FIRST_BLOCK_ON_SCALAR = (0, 2, 3)
 RELU_TILES = 3
 PRODUCT_BANKS = 3
 PART_SETS = 3

@@ -29,7 +29,7 @@ FOURS = [(a, a + 4) for a in range(0, E, 4)]
 FIRST_BLOCK = FOURS[:-1] + [(E - 4, E - 1), (E - 1, E)]
 
 BOTH_ON_SCALAR = 4
-ONE_ON_SCALAR = 5
+ONE_ON_SCALAR = 6
 FIRST_BLOCK_ON_SCALAR = (0, 2, 3)
 RELU_TILES = 3
 PRODUCT_BANKS = 3

@@ -23,13 +23,13 @@ FLOPS = 2 * 512 * N * T + 2 * (512 * H + H * N) * SLOTS
 
 W1_LOADS = [(a, a + 4) for a in range(0, E, 4)]
 W1_SCALE_LOADS = [(0, 4), (4, E)]
-GATHERS = [(0, 2), (2, 4)] + [(a, a + 3) for a in range(4, E, 3)]
-QUANTISE = [(a, a + 2) for a in range(0, E - 2, 2)] + [(E - 2, E - 1), (E - 1, E)]
+PAIRS = E // 2
+WORD_SETS, SCALE_SETS = 3, 2
+QUANTISE = [(0, 4), (4, 8), (8, 12), (12, 14), (14, 15), (15, 16)]
 FOURS = [(a, a + 4) for a in range(0, E, 4)]
 FIRST_BLOCK = FOURS[:-1] + [(E - 4, E - 1), (E - 1, E)]
 
-BOTH_ON_SCALAR = 4
-ONE_ON_SCALAR = 6
+BOTH_ON_SCALAR = 1
 FIRST_BLOCK_ON_SCALAR = (0, 2, 3)
 RELU_TILES = 3
 PRODUCT_BANKS = 3
@@ -107,8 +107,8 @@ def tile_moe_ogt_relu2_sigmoid_kernel(
         h_plane = keep.tile([P, SLOTS], U8, name="h_plane", align_bytes=64)
         y = [keep.tile([P, SLOTS], F32, name="y%d" % nb) for nb in range(ROW_BLOCKS)]
         banks = [psum.tile([P, 512], F32, name="bank%d" % b) for b in range(8)]
-        slot_words = [keep.tile([P, 6 * C], U32, name="slot_words%d" % i, align_bytes=64) for i in range(2)]
-        slot_planes = [keep.tile([P, 6 * C], U8, name="slot_plane%d" % i, align_bytes=64) for i in range(2)]
+        slot_words = [keep.tile([P, 2 * C], U32, name="slot_words%d" % i, align_bytes=64) for i in range(WORD_SETS)]
+        slot_planes = [keep.tile([P, 2 * C], U8, name="slot_plane%d" % i, align_bytes=64) for i in range(SCALE_SETS)]
         relu_tiles = [keep.tile([P, 2, H], F32, name="relu%d" % i) for i in range(RELU_TILES)]
         h_tiles = [keep.tile([P, (b - a) * H], BF16, name="h%d" % a, align_bytes=64) for a, b in QUANTISE]
         handed_out = []
@@ -120,43 +120,38 @@ def tile_moe_ogt_relu2_sigmoid_kernel(
             handed_out.append(banks[PRODUCT_BANKS + len(handed_out) % (len(banks) - PRODUCT_BANKS)])
             return handed_out[-1]
 
-        def slot_columns(g):
-            a, b = GATHERS[g]
-            tile, first = (g, 2) if g < 2 else ((g - 2) // 2, 3 * (g % 2))
-            return tile, first * C, (first + b - a) * C
+        def gather_words(pair):
+            entries = offs_tile[:, 2 * pair * LIST_COLS : (2 * pair + 2) * LIST_COLS]
+            nc.vector.tensor_copy(slot_words[pair % WORD_SETS][:], x_tile[:].bitcast(U32).indirect(entries))
 
-        def gather_words(g):
-            a, b = GATHERS[g]
-            entries = offs_tile[:, a * LIST_COLS : b * LIST_COLS]
-            tile, c0, c1 = slot_columns(g)
-            nc.vector.tensor_copy(slot_words[tile][:, c0:c1], x_tile[:].bitcast(U32).indirect(entries))
+        def gather_scales(pair):
+            entries = offs_tile[:, 2 * pair * LIST_COLS : (2 * pair + 2) * LIST_COLS]
+            nc.vector.tensor_copy(slot_planes[pair % SCALE_SETS][:], x_plane[:].indirect(entries))
 
-        def gather_scales(g):
-            a, b = GATHERS[g]
-            entries = offs_tile[:, a * LIST_COLS : b * LIST_COLS]
-            tile, c0, c1 = slot_columns(g)
-            nc.vector.tensor_copy(slot_planes[tile][:, c0:c1], x_plane[:].indirect(entries))
+        def h_scales(a, b):
+            if a < 8:
+                base = a // 4 * 4 * H + 3 * H + a % 4 * C
+                return w1_tiles[-1][:, base : base + (b - a) * C]
+            return h_plane[:, a * C : b * C]
 
         def first_product(pair, half):
             bank = banks[(2 * pair + half) % PRODUCT_BANKS]
             for e in (2 * pair, 2 * pair + 1):
-                g, in_gather = locate(GATHERS, e)
                 load, in_load = locate(W1_LOADS, e)
                 plane, in_plane = locate(W1_SCALE_LOADS, e)
-                tile, c0, c1 = slot_columns(g)
-                slots = slice(c0 + in_gather * C, c0 + (in_gather + 1) * C)
+                slots = slice(e % 2 * C, (e % 2 + 1) * C)
                 word_col, scale_col = in_load * H + half * H // 2, in_plane * H + half * H // 2
                 nc.tensor.matmul_mx(
                     out=bank[:, e % 2 * H // 2 : (e % 2 + 1) * H // 2],
-                    lhsT=slot_words[tile][:, slots].bitcast(FP8X4),
-                    lhsT_scale=slot_planes[tile][:, slots],
+                    lhsT=slot_words[pair % WORD_SETS][:, slots].bitcast(FP8X4),
+                    lhsT_scale=slot_planes[pair % SCALE_SETS][:, slots],
                     rhs=w1_tiles[load][:, 2 * word_col : 2 * word_col + H].bitcast(FP4X4),
                     rhs_scale=w1_planes[plane][:, scale_col : scale_col + H // 2],
                     start=True, stop=True,
                 )
             src = bank[:].rearrange("p (e m d) -> p e d m", e=2, d=4)
             dst = relu_tile(pair)[:].rearrange("p e (d h m) -> p h e d m", d=4, h=2)[:, half]
-            if pair < BOTH_ON_SCALAR or (half == 0 and pair < ONE_ON_SCALAR):
+            if pair < BOTH_ON_SCALAR or half == 0:
                 nc.scalar.activation(dst, src, ACT.Relu)
             else:
                 nc.vector.tensor_scalar(dst, src, 0.0, None, ALU.max)
@@ -171,7 +166,7 @@ def tile_moe_ogt_relu2_sigmoid_kernel(
 
         def quantise(q):
             a, b = QUANTISE[q]
-            nc.vector.quantize_mx(out=h_words[:, a * C : b * C].bitcast(FP8X4), scales=h_plane[:, a * C : b * C], in_=h_tiles[q][:])
+            nc.vector.quantize_mx(out=h_words[:, a * C : b * C].bitcast(FP8X4), scales=h_scales(a, b), in_=h_tiles[q][:])
 
         def second_product(nb, experts, bank, copy_out):
             first = min(experts)
@@ -183,7 +178,7 @@ def tile_moe_ogt_relu2_sigmoid_kernel(
                     lhsT=words[:, 2 * word_col : 2 * (word_col + P)].bitcast(FP4X4),
                     lhsT_scale=plane[:, scale_col : scale_col + P],
                     rhs=h_words[:, e * C : (e + 1) * C].bitcast(FP8X4),
-                    rhs_scale=h_plane[:, e * C : (e + 1) * C],
+                    rhs_scale=h_scales(e, e + 1),
                     start=True, stop=True,
                 )
             copy_out(y[nb][:, first * C : (first + len(experts)) * C], bank[:, 0 : len(experts) * C])
@@ -194,30 +189,31 @@ def tile_moe_ogt_relu2_sigmoid_kernel(
             block_banks.append(banks[(E - PRODUCT_BANKS + j) % PRODUCT_BANKS] if j < PRODUCT_BANKS else next_bank())
             second_product(0, range(*FIRST_BLOCK[j]), block_banks[j], nc.scalar.copy if j in FIRST_BLOCK_ON_SCALAR else nc.vector.tensor_copy)
 
-        for g in range(2):
-            gather_scales(g)
-            gather_words(g)
-        for step in range(E // 2 + 1):
-            if step < E // 2:
+        for pair in range(SCALE_SETS):
+            gather_scales(pair)
+        for pair in range(WORD_SETS):
+            gather_words(pair)
+        for step in range(PAIRS + 1):
+            if step < PAIRS:
                 for half in range(2):
                     first_product(step, half)
-            if step < 2:
-                for g in (2 * step + 2, 2 * step + 3):
-                    gather_words(g)
-                    gather_scales(g)
+            if step + SCALE_SETS < PAIRS:
+                gather_scales(step + SCALE_SETS)
+            if step + WORD_SETS < PAIRS:
+                gather_words(step + WORD_SETS)
             for half in range(2):
                 if 2 * step + 2 == W1_LOADS[half][1]:
                     load_scales(w2_planes[half][:], w2_scales32[:, :, half * N // 8 : (half + 1) * N // 8])
                     nc.sync.dma_start(out=gate_pairs[half][:], in_=gate[2 * half : 2 * half + 2].rearrange("r p t -> p r t"))
-            if step >= 2:
-                quantise(step - 2)
+            if step >= PAIRS - 2:
+                quantise(step - PAIRS + 2)
             if step >= 1:
                 for e in (2 * step - 2, 2 * step - 1):
                     turn_and_square(e)
         for eight in (1, 0):
             load_words(w2_tiles[1][eight][:], w2_words32[8 * eight : 8 * eight + 8, :, N // 4 : N // 2])
-        for j in range(2):
-            quantise(len(QUANTISE) - 2 + j)
+        for q in range(3, len(QUANTISE)):
+            quantise(q)
         for j in range(len(FIRST_BLOCK)):
             first_block(j)
 

@@ -24,12 +24,12 @@ FLOPS = 2 * 512 * N * T + 2 * (512 * H + H * N) * SLOTS
 W1_LOADS = [(a, a + 4) for a in range(0, E, 4)]
 W1_SCALE_LOADS = [(0, 4), (4, E)]
 PAIRS = E // 2
-WORD_SETS, SCALE_SETS = 3, 2
+WORD_SETS, SCALE_SETS = 6, 2
 QUANTISE = [(0, 4), (4, 8), (8, 12), (12, 14), (14, 15), (15, 16)]
 FOURS = [(a, a + 4) for a in range(0, E, 4)]
 FIRST_BLOCK = FOURS[:-1] + [(E - 4, E - 1), (E - 1, E)]
 
-BOTH_ON_SCALAR = 1
+BOTH_ON_SCALAR = 2
 FIRST_BLOCK_ON_SCALAR = (0, 2, 3)
 RELU_TILES = 3
 PRODUCT_BANKS = 3
@@ -151,7 +151,7 @@ def tile_moe_ogt_relu2_sigmoid_kernel(
                 )
             src = bank[:].rearrange("p (e m d) -> p e d m", e=2, d=4)
             dst = relu_tile(pair)[:].rearrange("p e (d h m) -> p h e d m", d=4, h=2)[:, half]
-            if pair < BOTH_ON_SCALAR or half == 0:
+            if pair < BOTH_ON_SCALAR or (half == 0 and pair not in (5, 6)):
                 nc.scalar.activation(dst, src, ACT.Relu)
             else:
                 nc.vector.tensor_scalar(dst, src, 0.0, None, ALU.max)

@@ -32,7 +32,7 @@ FIRST_BLOCK = FOURS[:-1] + [(E - 4, E - 1), (E - 1, E)]
 BOTH_ON_SCALAR = 2
 FIRST_BLOCK_ON_SCALAR = (0, 2, 3)
 RELU_TILES = 3
-PRODUCT_BANKS = 3
+PRODUCT_BANKS = 4
 PART_SETS = 3
 
 

@@ -30,7 +30,7 @@ FOURS = [(a, a + 4) for a in range(0, E, 4)]
 FIRST_BLOCK = FOURS[:-1] + [(E - 4, E - 1), (E - 1, E)]
 
 BOTH_ON_SCALAR = 2
-FIRST_BLOCK_ON_SCALAR = (0, 2, 3)
+FIRST_BLOCK_ON_SCALAR = (0, 3)
 RELU_TILES = 3
 PRODUCT_BANKS = 4
 PART_SETS = 3
@@ -92,10 +92,13 @@ def tile_moe_ogt_relu2_sigmoid_kernel(
         x_tile = keep.tile([P, T], I32, name="x_tile", align_bytes=64)
         nc.sync.dma_start(out=x_tile[:], in_=x_words[0].rearrange("p t d -> p (t d)").bitcast(I32))
         for tile, (a, b) in zip(w1_tiles, W1_LOADS):
-            load_words(tile[:], w1_words32[a:b])
             if a == 0:
-                for plane, (c, d) in zip(w1_planes, W1_SCALE_LOADS):
-                    load_scales(plane[:], w1_scales32[c:d])
+                load_words(tile[:, 0 : 4 * H], w1_words32[0:2])
+                load_scales(w1_planes[0][:], w1_scales32[0:4])
+                load_words(tile[:, 4 * H : 8 * H], w1_words32[2:4])
+                load_scales(w1_planes[1][:], w1_scales32[4:E])
+            else:
+                load_words(tile[:], w1_words32[a:b])
         for eight in range(2):
             load_words(w2_tiles[0][eight][:], w2_words32[8 * eight : 8 * eight + 8, :, 0 : N // 4])
         pos_tiles = []
@@ -132,6 +135,9 @@ def tile_moe_ogt_relu2_sigmoid_kernel(
             if a < 8:
                 base = a // 4 * 4 * H + 3 * H + a % 4 * C
                 return w1_tiles[-1][:, base : base + (b - a) * C]
+            if a >= E - 2:
+                base = 3 * 4 * P + a % 2 * C
+                return w2_tiles[0][0][:, base : base + C]
             return h_plane[:, a * C : b * C]
 
         def first_product(pair, half):
@@ -183,10 +189,10 @@ def tile_moe_ogt_relu2_sigmoid_kernel(
                 )
             copy_out(y[nb][:, first * C : (first + len(experts)) * C], bank[:, 0 : len(experts) * C])
 
-        block_banks = []
+        block_banks = {}
 
         def first_block(j):
-            block_banks.append(banks[(E - PRODUCT_BANKS + j) % PRODUCT_BANKS] if j < PRODUCT_BANKS else next_bank())
+            block_banks[j] = banks[(E - PRODUCT_BANKS + j) % PRODUCT_BANKS] if j < PRODUCT_BANKS else next_bank()
             second_product(0, range(*FIRST_BLOCK[j]), block_banks[j], nc.scalar.copy if j in FIRST_BLOCK_ON_SCALAR else nc.vector.tensor_copy)
 
         for pair in range(SCALE_SETS):
@@ -212,12 +218,15 @@ def tile_moe_ogt_relu2_sigmoid_kernel(
                     turn_and_square(e)
         for eight in (1, 0):
             load_words(w2_tiles[1][eight][:], w2_words32[8 * eight : 8 * eight + 8, :, N // 4 : N // 2])
-        for q in range(3, len(QUANTISE)):
+        quantise(3)
+        for j in (1, 0):
+            first_block(j)
+        for q in range(4, len(QUANTISE)):
             quantise(q)
-        for j in range(len(FIRST_BLOCK)):
+        for j in range(2, len(FIRST_BLOCK)):
             first_block(j)
 
-        ring = [block_banks[0], block_banks[-2], block_banks[-1]]
+        ring = [block_banks[0], block_banks[3], block_banks[4]]
         result_banks = [bank for bank in banks if all(bank is not used for used in ring)]
         wg_tile = w2_tiles[0][1][:, 6 * N : 8 * N]
         wg_plane = w2_tiles[0][1][:, 5 * N : 6 * N]

@@ -18,10 +18,11 @@ P = 128
 T, E, C, H, N, TOP = 512, 16, 128, 512, 512, 4
 SLOTS = E * C
 ROW_BLOCKS = N // P
+TOKEN_BLOCKS = T // P
 LIST_COLS = C // 16
 FLOPS = 2 * 512 * N * T + 2 * (512 * H + H * N) * SLOTS
 
-W1_LOADS = [(a, a + 4) for a in range(0, E, 4)]
+W1_LOADS = [(0, 4), (4, 8), (8, 10), (10, 12), (12, E)]
 W1_SCALE_LOADS = [(0, 4), (4, E)]
 PAIRS = E // 2
 WORD_SETS, SCALE_SETS = 6, 2
@@ -33,7 +34,6 @@ BOTH_ON_SCALAR = 2
 FIRST_BLOCK_ON_SCALAR = (0, 3)
 RELU_TILES = 3
 PRODUCT_BANKS = 4
-PART_SETS = 3
 
 
 def locate(ranges, e):
@@ -47,7 +47,6 @@ def tile_moe_ogt_relu2_sigmoid_kernel(
     nc = tc.nc
     with ExitStack() as ctx:
         keep = ctx.enter_context(tc.tile_pool(name="keep", bufs=1))
-        work = ctx.enter_context(tc.tile_pool(name="work", bufs=1))
         psum = ctx.enter_context(tc.psum_pool(name="psum", bufs=1))
 
         def zeroed_plane(name, cols, engine):
@@ -56,6 +55,10 @@ def tile_moe_ogt_relu2_sigmoid_kernel(
             return plane
 
         x_plane = zeroed_plane("x_plane", T, nc.gpsimd)
+        preload = keep.tile([P, 16], F32, name="preload")
+        nc.gpsimd.memset(preload[:, 0:1], 0.0)
+        nc.scalar.activation(preload[:, 8:9], preload[:, 0:1], ACT.Sigmoid)
+
         w1_planes = [keep.tile([P, (b - a) * H], U8, name="w1_plane%d" % a, align_bytes=64) for a, b in W1_SCALE_LOADS]
         nc.vector.memset(w1_planes[0][:].bitcast(I32), 0)
         share = (E - W1_SCALE_LOADS[1][0]) * H // 2
@@ -80,11 +83,9 @@ def tile_moe_ogt_relu2_sigmoid_kernel(
         w1_scales32 = w1_scales.rearrange("e o b n -> (e o) b n").bitcast(I32)
         w2_scales32 = w2_scales.rearrange("e o b n -> (e o) b n").bitcast(I32)
 
-        w1_tiles = [keep.tile([P, (b - a) * 2 * H], U8, name="w1_%d" % a, align_bytes=64) for a, b in W1_LOADS]
+        w1_tiles = [keep.tile([P, (b - a) * 2 * H], U8, name="w1_%d" % a, tag="w1_%d" % a, align_bytes=64) for a, b in W1_LOADS]
         w2_tiles = [[keep.tile([P, 8 * N], U8, name="w2_%d_%d" % (half, eight), align_bytes=64) for eight in range(2)] for half in range(2)]
         w2_planes = w1_tiles[0:2]
-        gate_pairs = [keep.tile([P, 2, T], F32, name="gates%d" % pair) for pair in range(TOP // 2)]
-        gates = [gate_pairs[r // 2][:, r % 2, :] for r in range(TOP)]
 
         offs_tile = keep.tile([P, SLOTS // 16], U16, name="offs_tile")
         nc.sync.dma_start(offs_tile[:], offs)
@@ -99,12 +100,15 @@ def tile_moe_ogt_relu2_sigmoid_kernel(
                 load_scales(w1_planes[1][:], w1_scales32[4:E])
             else:
                 load_words(tile[:], w1_words32[a:b])
+
         for eight in range(2):
             load_words(w2_tiles[0][eight][:], w2_words32[8 * eight : 8 * eight + 8, :, 0 : N // 4])
         pos_tiles = []
         for r, pos in enumerate((pos1, pos2, pos3, pos4)):
             pos_tiles.append(keep.tile([P, T // 16], U16, name="pos_tile%d" % r))
             nc.sync.dma_start(pos_tiles[r][:], pos)
+        for eight in (1, 0):
+            load_words(w2_tiles[1][eight][:], w2_words32[8 * eight : 8 * eight + 8, :, N // 4 : N // 2])
 
         h_words = keep.tile([P, SLOTS], U32, name="h_words", align_bytes=64)
         h_plane = keep.tile([P, SLOTS], U8, name="h_plane", align_bytes=64)
@@ -210,14 +214,14 @@ def tile_moe_ogt_relu2_sigmoid_kernel(
             for half in range(2):
                 if 2 * step + 2 == W1_LOADS[half][1]:
                     load_scales(w2_planes[half][:], w2_scales32[:, :, half * N // 8 : (half + 1) * N // 8])
-                    nc.sync.dma_start(out=gate_pairs[half][:], in_=gate[2 * half : 2 * half + 2].rearrange("r p t -> p r t"))
             if step >= PAIRS - 2:
                 quantise(step - PAIRS + 2)
             if step >= 1:
                 for e in (2 * step - 2, 2 * step - 1):
                     turn_and_square(e)
-        for eight in (1, 0):
-            load_words(w2_tiles[1][eight][:], w2_words32[8 * eight : 8 * eight + 8, :, N // 4 : N // 2])
+        gate_tile = keep.tile([P, TOP, T], F32, name="gate_tile", tag="w1_8", align_bytes=64)
+        nc.sync.dma_start(out=gate_tile[:], in_=gate.rearrange("r p t -> p r t"))
+        gates = [gate_tile[:, r, :] for r in range(TOP)]
         quantise(3)
         for j in (1, 0):
             first_block(j)
@@ -226,62 +230,97 @@ def tile_moe_ogt_relu2_sigmoid_kernel(
         for j in range(2, len(FIRST_BLOCK)):
             first_block(j)
 
-        ring = [block_banks[0], block_banks[3], block_banks[4]]
-        result_banks = [bank for bank in banks if all(bank is not used for used in ring)]
-        wg_tile = w2_tiles[0][1][:, 6 * N : 8 * N]
-        wg_plane = w2_tiles[0][1][:, 5 * N : 6 * N]
+        wg_tile = keep.tile([P, 2 * N], U8, name="wg_tile", align_bytes=64)[:]
+        wg_plane = w1_planes[0][:, 0:N]
         out_gates = [keep.tile([P, T], F32, name="out_gate%d" % nb) for nb in range(ROW_BLOCKS)]
-        part_tiles = [keep.tile([P, T], F32, name="part%d" % i) for i in range(PART_SETS * TOP)]
-        pieces = [(nb, 0, T) for nb in range(ROW_BLOCKS - 1)] + [(ROW_BLOCKS - 1, 0, T - P), (ROW_BLOCKS - 1, T - P, T)]
+        part_tiles = [keep.tile([P, T], F32, name="part%d" % i) for i in range(ROW_BLOCKS * TOP)]
+        turned_tiles = [keep.tile([P, T], F32, name="turned%d" % i) for i in range(ROW_BLOCKS)]
+        plain_tiles = [keep.tile([P, T], F32, name="plain%d" % i) for i in range(ROW_BLOCKS)]
+        last_result = keep.tile([P, T], F32, name="last_result")
 
-        first_result = keep.tile([P, T], F32, name="first_result")
+        def later_products(nb, in_banks):
+            for (a, b), bank in zip(reversed(FOURS), in_banks):
+                second_product(nb, range(b - 1, a - 1, -1), banks[bank], nc.scalar.copy)
 
-        def output_gate(nb):
+        def output_gate(nb, bank):
             nc.tensor.matmul_mx(
-                out=result_banks[nb][:],
+                out=banks[bank][:],
                 lhsT=wg_tile[:, 2 * nb * P : 2 * (nb + 1) * P].bitcast(FP4X4),
                 lhsT_scale=wg_plane[:, nb * P : (nb + 1) * P],
                 rhs=x_tile[:].bitcast(FP8X4),
                 rhs_scale=x_plane[:],
                 start=True, stop=True,
             )
-            nc.scalar.activation(out_gates[nb][:], result_banks[nb][:], ACT.Sigmoid)
+            nc.scalar.activation(out_gates[nb][:], banks[bank][:], ACT.Sigmoid)
 
-        def combine(i):
-            nb, t0, t1 = pieces[i]
-            width = t1 - t0
-            blocks = [slice(c, c + P) for c in range(0, width, P)]
-            parts = [part_tiles[(i % PART_SETS) * TOP + r] for r in range(TOP)]
-            for r in range(TOP):
-                looked_up = y[nb][:].indirect(pos_tiles[r][:, t0 // 16 : t1 // 16])
-                nc.vector.tensor_tensor(parts[r][:, 0:width], looked_up, gates[r][:, t0:t1], ALU.mult)
-            sums = ring[i % len(ring)]
-            for r in range(TOP):
+        def add_turned(bank, tiles, t0, t1):
+            blocks = [slice(c, c + P) for c in range(t0, t1, P)]
+            for r, tile in enumerate(tiles):
                 for cols in blocks:
                     nc.tensor.matmul(
-                        sums[:, cols], parts[r][:, cols], ident[:], is_transpose=True,
-                        start=r == 0 and cols == blocks[0], stop=r == TOP - 1 and cols == blocks[-1],
+                        banks[bank][:, cols], tile[:, cols], ident[:], is_transpose=True,
+                        start=r == 0 and cols == blocks[0], stop=r == len(tiles) - 1 and cols == blocks[-1],
                     )
-            turned = work.tile([P, width], F32, name="turned", tag="turned", bufs=2)
-            nc.scalar.copy(turned[:], sums[:, 0:width])
-            for cols in blocks:
-                nc.tensor.transpose(result_banks[i][:, cols], turned[:, cols], ident[:])
 
-        def finish(i):
-            nb, t0, t1 = pieces[i]
-            result = (gates[i - 1] if i else first_result)[:, 0 : t1 - t0]
-            nc.vector.tensor_tensor(result, result_banks[i][:, 0 : t1 - t0], out_gates[nb][:, t0:t1], ALU.mult)
+        def gather_weighed(nb, t0, t1, lists):
+            for r in lists:
+                looked_up = y[nb][:].indirect(pos_tiles[r][:, t0 // 16 : t1 // 16])
+                nc.vector.tensor_tensor(part_tiles[nb * TOP + r][:, t0:t1], looked_up, gates[r][:, t0:t1], ALU.mult)
+
+        def gather_plain(nb):
+            nc.scalar.activation(plain_tiles[nb][:], y[nb][:].indirect(pos_tiles[0][:]), ACT.Copy)
+
+        def weigh(nb):
+            nc.vector.tensor_tensor(part_tiles[nb * TOP][:], plain_tiles[nb][:], gates[0], ALU.mult)
+
+        def sum_parts(nb, t0, t1, bank):
+            add_turned(bank, [part_tiles[nb * TOP + r] for r in (1, 0, 2, 3)], t0, t1)
+
+        def turn_back(nb, t0, t1, bank, result_bank):
+            nc.scalar.copy(turned_tiles[nb][:, t0:t1], banks[bank][:, t0:t1])
+            add_turned(result_bank, [turned_tiles[nb]], t0, t1)
+
+        def finish(nb, t0, t1, bank, result):
+            nc.vector.tensor_tensor(result, banks[bank][:, t0:t1], out_gates[nb][:, t0:t1], ALU.mult)
             nc.sync.dma_start(out=out[nb * P : (nb + 1) * P, t0:t1], in_=result)
 
-        for nb in range(1, ROW_BLOCKS):
-            for j, (a, b) in enumerate(reversed(FOURS)):
-                second_product(nb, range(b - 1, a - 1, -1), ring[((nb - 1) * len(FOURS) + j) % len(ring)], nc.scalar.copy)
-            if nb == 1:
-                load_words(wg_tile, wg_words.bitcast(I32))
-                load_scales(wg_plane, wg_scales.bitcast(I32))
-        for nb in range(ROW_BLOCKS):
-            output_gate(nb)
-        for i in range(len(pieces)):
-            combine(i)
-        for i in range(len(pieces)):
-            finish(i)
+        cut = T - P
+        gather_plain(0)
+        gather_weighed(0, 0, T, (1,))
+        weigh(0)
+        gather_weighed(0, 0, T, (2, 3))
+        later_products(1, (0, 3, 4, 0))
+        load_words(wg_tile, wg_words.bitcast(I32))
+        load_scales(wg_plane, wg_scales.bitcast(I32))
+        gather_plain(1)
+        gather_weighed(1, 0, T, (1,))
+        weigh(1)
+        gather_weighed(1, 0, T, (2, 3))
+        later_products(2, (3, 4, 5, 3))
+        sum_parts(0, 0, T, 0)
+        turn_back(0, 0, T, 0, 1)
+        gather_plain(2)
+        gather_weighed(2, 0, T, (1,))
+        weigh(2)
+        gather_weighed(2, 0, T, (2, 3))
+        later_products(3, (4, 5, 6, 4))
+        sum_parts(1, 0, T, 3)
+        gather_plain(3)
+        gather_weighed(3, 0, cut, (1,))
+        weigh(3)
+        gather_weighed(3, 0, cut, (2, 3))
+        gather_weighed(3, cut, T, (1, 2, 3))
+        turn_back(1, 0, T, 3, 2)
+        for nb, bank in enumerate((5, 6, 7, 0)):
+            output_gate(nb, bank)
+        sum_parts(2, 0, T, 4)
+        turn_back(2, 0, T, 4, 6)
+        sum_parts(3, 0, cut, 3)
+        sum_parts(3, cut, T, 5)
+        turn_back(3, 0, cut, 3, 4)
+        turn_back(3, cut, T, 5, 7)
+        finish(0, 0, T, 1, gates[1])
+        finish(1, 0, T, 2, gates[2])
+        finish(2, 0, T, 6, gates[3])
+        finish(3, 0, cut, 4, last_result[:, 0:cut])
+        finish(3, cut, T, 7, last_result[:, cut:T])

from contextlib import ExitStack

import concourse.mybir as mybir
from concourse.masks import make_identity

F32 = mybir.dt.float32
BF16 = mybir.dt.bfloat16
I32 = mybir.dt.int32
U32 = mybir.dt.uint32
U16 = mybir.dt.uint16
U8 = mybir.dt.uint8
FP8X4 = mybir.dt.float8_e4m3fn_x4
FP4X4 = mybir.dt.float4_e2m1fn_x4
ACT = mybir.ActivationFunctionType
ALU = mybir.AluOpType

P = 128
T, E, C, H, N, TOP = 512, 16, 128, 512, 512, 4
SLOTS = E * C
ROW_BLOCKS = N // P
TOKEN_BLOCKS = T // P
LIST_COLS = C // 16
FLOPS = 2 * 512 * N * T + 2 * (512 * H + H * N) * SLOTS

W1_LOADS = [(0, 4), (4, 8), (8, 10), (10, 12), (12, E)]
W1_SCALE_LOADS = [(0, 4), (4, E)]
PAIRS = E // 2
WORD_SETS, SCALE_SETS = 6, 2
QUANTISE = [(0, 4), (4, 8), (8, 12), (12, 14), (14, 15), (15, 16)]
FOURS = [(a, a + 4) for a in range(0, E, 4)]
FIRST_BLOCK = FOURS[:-1] + [(E - 4, E - 1), (E - 1, E)]

BOTH_ON_SCALAR = 2
FIRST_BLOCK_ON_SCALAR = (0, 3)
RELU_TILES = 3
PRODUCT_BANKS = 4


def locate(ranges, e):
    return [(i, e - a) for i, (a, b) in enumerate(ranges) if a <= e < b][0]


def tile_moe_ogt_relu2_sigmoid_kernel(
    tc, x_words, x_scales, wg_words, wg_scales, w1_words, w1_scales, w2_words, w2_scales,
    gate, offs, pos1, pos2, pos3, pos4, out,
):
    nc = tc.nc
    with ExitStack() as ctx:
        keep = ctx.enter_context(tc.tile_pool(name="keep", bufs=1))
        psum = ctx.enter_context(tc.psum_pool(name="psum", bufs=1))

        def zeroed_plane(name, cols, engine):
            plane = keep.tile([P, cols], U8, name=name, align_bytes=64)
            engine.memset(plane[:].bitcast(I32), 0)
            return plane

        x_plane = zeroed_plane("x_plane", T, nc.gpsimd)
        preload = keep.tile([P, 16], F32, name="preload")
        nc.gpsimd.memset(preload[:, 0:1], 0.0)
        nc.scalar.activation(preload[:, 8:9], preload[:, 0:1], ACT.Sigmoid)

        w1_planes = [keep.tile([P, (b - a) * H], U8, name="w1_plane%d" % a, align_bytes=64) for a, b in W1_SCALE_LOADS]
        nc.vector.memset(w1_planes[0][:].bitcast(I32), 0)
        share = (E - W1_SCALE_LOADS[1][0]) * H // 2
        nc.vector.memset(w1_planes[1][:, 0:share].bitcast(I32), 0)
        nc.gpsimd.memset(w1_planes[1][:, share : 2 * share].bitcast(I32), 0)
        ident = keep.tile([P, P], F32, name="ident")
        make_identity(nc, ident[:])

        def load_scales(plane, rows):
            src = rows.rearrange("e (q r) n -> r q e n", r=4)
            dst = plane.bitcast(I32).rearrange("p (e n) -> p e n", e=rows.shape[0])
            for r in range(4):
                nc.sync.dma_start(out=dst[r:P:32, :, :], in_=src[r])

        def load_words(tile, words):
            dst = tile.bitcast(I32).rearrange("p (e n) -> p e n", e=words.shape[0])
            nc.sync.dma_start(out=dst, in_=words.rearrange("e p n -> p e n"))


        w1_words32 = w1_words.rearrange("e o p n -> (e o) p n").bitcast(I32)
        w2_words32 = w2_words.rearrange("e o p n -> (e o) p n").bitcast(I32)
        w1_scales32 = w1_scales.rearrange("e o b n -> (e o) b n").bitcast(I32)
        w2_scales32 = w2_scales.rearrange("e o b n -> (e o) b n").bitcast(I32)

        w1_tiles = [keep.tile([P, (b - a) * 2 * H], U8, name="w1_%d" % a, tag="w1_%d" % a, align_bytes=64) for a, b in W1_LOADS]
        w2_tiles = [[keep.tile([P, 8 * N], U8, name="w2_%d_%d" % (half, eight), align_bytes=64) for eight in range(2)] for half in range(2)]
        w2_planes = w1_tiles[0:2]

        offs_tile = keep.tile([P, SLOTS // 16], U16, name="offs_tile")
        nc.sync.dma_start(offs_tile[:], offs)
        load_scales(x_plane[:], x_scales.bitcast(I32))
        x_tile = keep.tile([P, T], I32, name="x_tile", align_bytes=64)
        nc.sync.dma_start(out=x_tile[:], in_=x_words[0].rearrange("p t d -> p (t d)").bitcast(I32))
        for tile, (a, b) in zip(w1_tiles, W1_LOADS):
            if a == 0:
                load_words(tile[:, 0 : 4 * H], w1_words32[0:2])
                load_scales(w1_planes[0][:], w1_scales32[0:4])
                load_words(tile[:, 4 * H : 8 * H], w1_words32[2:4])
                load_scales(w1_planes[1][:], w1_scales32[4:E])
            else:
                load_words(tile[:], w1_words32[a:b])

        for eight in range(2):
            load_words(w2_tiles[0][eight][:], w2_words32[8 * eight : 8 * eight + 8, :, 0 : N // 4])
        pos_tiles = []
        for r, pos in enumerate((pos1, pos2, pos3, pos4)):
            pos_tiles.append(keep.tile([P, T // 16], U16, name="pos_tile%d" % r))
            nc.sync.dma_start(pos_tiles[r][:], pos)
        for eight in (1, 0):
            load_words(w2_tiles[1][eight][:], w2_words32[8 * eight : 8 * eight + 8, :, N // 4 : N // 2])

        h_words = keep.tile([P, SLOTS], U32, name="h_words", align_bytes=64)
        h_plane = keep.tile([P, SLOTS], U8, name="h_plane", align_bytes=64)
        y = [keep.tile([P, SLOTS], F32, name="y%d" % nb) for nb in range(ROW_BLOCKS)]
        banks = [psum.tile([P, 512], F32, name="bank%d" % b) for b in range(8)]
        slot_words = [keep.tile([P, 2 * C], U32, name="slot_words%d" % i, align_bytes=64) for i in range(WORD_SETS)]
        slot_planes = [keep.tile([P, 2 * C], U8, name="slot_plane%d" % i, align_bytes=64) for i in range(SCALE_SETS)]
        relu_tiles = [keep.tile([P, 2, H], F32, name="relu%d" % i) for i in range(RELU_TILES)]
        h_tiles = [keep.tile([P, (b - a) * H], BF16, name="h%d" % a, align_bytes=64) for a, b in QUANTISE]
        handed_out = []

        def relu_tile(pair):
            return relu_tiles[pair % RELU_TILES]

        def next_bank():
            handed_out.append(banks[PRODUCT_BANKS + len(handed_out) % (len(banks) - PRODUCT_BANKS)])
            return handed_out[-1]

        def gather_words(pair):
            entries = offs_tile[:, 2 * pair * LIST_COLS : (2 * pair + 2) * LIST_COLS]
            nc.vector.tensor_copy(slot_words[pair % WORD_SETS][:], x_tile[:].bitcast(U32).indirect(entries))

        def gather_scales(pair):
            entries = offs_tile[:, 2 * pair * LIST_COLS : (2 * pair + 2) * LIST_COLS]
            nc.vector.tensor_copy(slot_planes[pair % SCALE_SETS][:], x_plane[:].indirect(entries))

        def h_scales(a, b):
            if a < 8:
                base = a // 4 * 4 * H + 3 * H + a % 4 * C
                return w1_tiles[-1][:, base : base + (b - a) * C]
            if a >= E - 2:
                base = 3 * 4 * P + a % 2 * C
                return w2_tiles[0][0][:, base : base + C]
            return h_plane[:, a * C : b * C]

        def first_product(pair, half):
            bank = banks[(2 * pair + half) % PRODUCT_BANKS]
            for e in (2 * pair, 2 * pair + 1):
                load, in_load = locate(W1_LOADS, e)
                plane, in_plane = locate(W1_SCALE_LOADS, e)
                slots = slice(e % 2 * C, (e % 2 + 1) * C)
                word_col, scale_col = in_load * H + half * H // 2, in_plane * H + half * H // 2
                nc.tensor.matmul_mx(
                    out=bank[:, e % 2 * H // 2 : (e % 2 + 1) * H // 2],
                    lhsT=slot_words[pair % WORD_SETS][:, slots].bitcast(FP8X4),
                    lhsT_scale=slot_planes[pair % SCALE_SETS][:, slots],
                    rhs=w1_tiles[load][:, 2 * word_col : 2 * word_col + H].bitcast(FP4X4),
                    rhs_scale=w1_planes[plane][:, scale_col : scale_col + H // 2],
                    start=True, stop=True,
                )
            src = bank[:].rearrange("p (e m d) -> p e d m", e=2, d=4)
            dst = relu_tile(pair)[:].rearrange("p e (d h m) -> p h e d m", d=4, h=2)[:, half]
            if pair < BOTH_ON_SCALAR or (half == 0 and pair not in (5, 6)):
                nc.scalar.activation(dst, src, ACT.Relu)
            else:
                nc.vector.tensor_scalar(dst, src, 0.0, None, ALU.max)

        def turn_and_square(e):
            bank = next_bank()
            for d in range(4):
                nc.tensor.transpose(bank[:, d * C : (d + 1) * C], relu_tile(e // 2)[:, e % 2, d * P : (d + 1) * P], ident[:])
            q, in_tile = locate(QUANTISE, e)
            dst = h_tiles[q][:, in_tile * H : (in_tile + 1) * H].rearrange("p (s d) -> p s d", d=4)
            nc.scalar.activation(dst, bank[:].rearrange("p (d s) -> p s d", d=4), ACT.Square)

        def quantise(q):
            a, b = QUANTISE[q]
            nc.vector.quantize_mx(out=h_words[:, a * C : b * C].bitcast(FP8X4), scales=h_scales(a, b), in_=h_tiles[q][:])

        def second_product(nb, experts, bank, copy_out):
            first = min(experts)
            for e in experts:
                words, word_col = w2_tiles[nb // 2][e // 8], (e % 8 * 2 + nb % 2) * P
                plane, scale_col = w2_planes[nb // 2], (2 * e + nb % 2) * P
                nc.tensor.matmul_mx(
                    out=bank[:, (e - first) * C : (e - first + 1) * C],
                    lhsT=words[:, 2 * word_col : 2 * (word_col + P)].bitcast(FP4X4),
                    lhsT_scale=plane[:, scale_col : scale_col + P],
                    rhs=h_words[:, e * C : (e + 1) * C].bitcast(FP8X4),
                    rhs_scale=h_scales(e, e + 1),
                    start=True, stop=True,
                )
            copy_out(y[nb][:, first * C : (first + len(experts)) * C], bank[:, 0 : len(experts) * C])

        block_banks = {}

        def first_block(j):
            block_banks[j] = banks[(E - PRODUCT_BANKS + j) % PRODUCT_BANKS] if j < PRODUCT_BANKS else next_bank()
            second_product(0, range(*FIRST_BLOCK[j]), block_banks[j], nc.scalar.copy if j in FIRST_BLOCK_ON_SCALAR else nc.vector.tensor_copy)

        for pair in range(SCALE_SETS):
            gather_scales(pair)
        for pair in range(WORD_SETS):
            gather_words(pair)
        for step in range(PAIRS + 1):
            if step < PAIRS:
                for half in range(2):
                    first_product(step, half)
            if step + SCALE_SETS < PAIRS:
                gather_scales(step + SCALE_SETS)
            if step + WORD_SETS < PAIRS:
                gather_words(step + WORD_SETS)
            for half in range(2):
                if 2 * step + 2 == W1_LOADS[half][1]:
                    load_scales(w2_planes[half][:], w2_scales32[:, :, half * N // 8 : (half + 1) * N // 8])
            if step >= PAIRS - 2:
                quantise(step - PAIRS + 2)
            if step >= 1:
                for e in (2 * step - 2, 2 * step - 1):
                    turn_and_square(e)
        gate_tile = keep.tile([P, TOP, T], F32, name="gate_tile", tag="w1_8", align_bytes=64)
        nc.sync.dma_start(out=gate_tile[:], in_=gate.rearrange("r p t -> p r t"))
        gates = [gate_tile[:, r, :] for r in range(TOP)]
        quantise(3)
        for j in (1, 0):
            first_block(j)
        for q in range(4, len(QUANTISE)):
            quantise(q)
        for j in range(2, len(FIRST_BLOCK)):
            first_block(j)

        wg_tile = keep.tile([P, 2 * N], U8, name="wg_tile", align_bytes=64)[:]
        wg_plane = w1_planes[0][:, 0:N]
        out_gates = [keep.tile([P, T], F32, name="out_gate%d" % nb) for nb in range(ROW_BLOCKS)]
        part_tiles = [keep.tile([P, T], F32, name="part%d" % i) for i in range(ROW_BLOCKS * TOP)]
        turned_tiles = [keep.tile([P, T], F32, name="turned%d" % i) for i in range(ROW_BLOCKS)]
        plain_tiles = [keep.tile([P, T], F32, name="plain%d" % i) for i in range(ROW_BLOCKS)]
        last_result = keep.tile([P, T], F32, name="last_result")

        def later_products(nb, in_banks):
            for (a, b), bank in zip(reversed(FOURS), in_banks):
                second_product(nb, range(b - 1, a - 1, -1), banks[bank], nc.scalar.copy)

        def output_gate(nb, bank):
            nc.tensor.matmul_mx(
                out=banks[bank][:],
                lhsT=wg_tile[:, 2 * nb * P : 2 * (nb + 1) * P].bitcast(FP4X4),
                lhsT_scale=wg_plane[:, nb * P : (nb + 1) * P],
                rhs=x_tile[:].bitcast(FP8X4),
                rhs_scale=x_plane[:],
                start=True, stop=True,
            )
            nc.scalar.activation(out_gates[nb][:], banks[bank][:], ACT.Sigmoid)

        def add_turned(bank, tiles, t0, t1):
            blocks = [slice(c, c + P) for c in range(t0, t1, P)]
            for r, tile in enumerate(tiles):
                for cols in blocks:
                    nc.tensor.matmul(
                        banks[bank][:, cols], tile[:, cols], ident[:], is_transpose=True,
                        start=r == 0 and cols == blocks[0], stop=r == len(tiles) - 1 and cols == blocks[-1],
                    )

        def gather_weighed(nb, t0, t1, lists):
            for r in lists:
                looked_up = y[nb][:].indirect(pos_tiles[r][:, t0 // 16 : t1 // 16])
                nc.vector.tensor_tensor(part_tiles[nb * TOP + r][:, t0:t1], looked_up, gates[r][:, t0:t1], ALU.mult)

        def gather_plain(nb):
            nc.scalar.activation(plain_tiles[nb][:], y[nb][:].indirect(pos_tiles[0][:]), ACT.Copy)

        def weigh(nb):
            nc.vector.tensor_tensor(part_tiles[nb * TOP][:], plain_tiles[nb][:], gates[0], ALU.mult)

        def sum_parts(nb, t0, t1, bank):
            add_turned(bank, [part_tiles[nb * TOP + r] for r in (1, 0, 2, 3)], t0, t1)

        def turn_back(nb, t0, t1, bank, result_bank):
            nc.scalar.copy(turned_tiles[nb][:, t0:t1], banks[bank][:, t0:t1])
            add_turned(result_bank, [turned_tiles[nb]], t0, t1)

        def finish(nb, t0, t1, bank, result):
            nc.vector.tensor_tensor(result, banks[bank][:, t0:t1], out_gates[nb][:, t0:t1], ALU.mult)
            nc.sync.dma_start(out=out[nb * P : (nb + 1) * P, t0:t1], in_=result)

        cut = T - P
        gather_plain(0)
        gather_weighed(0, 0, T, (1,))
        weigh(0)
        gather_weighed(0, 0, T, (2, 3))
        later_products(1, (0, 3, 4, 0))
        load_words(wg_tile, wg_words.bitcast(I32))
        load_scales(wg_plane, wg_scales.bitcast(I32))
        gather_plain(1)
        gather_weighed(1, 0, T, (1,))
        weigh(1)
        gather_weighed(1, 0, T, (2, 3))
        later_products(2, (3, 4, 5, 3))
        sum_parts(0, 0, T, 0)
        turn_back(0, 0, T, 0, 1)
        gather_plain(2)
        gather_weighed(2, 0, T, (1,))
        weigh(2)
        gather_weighed(2, 0, T, (2, 3))
        later_products(3, (4, 5, 6, 4))
        sum_parts(1, 0, T, 3)
        gather_plain(3)
        gather_weighed(3, 0, cut, (1,))
        weigh(3)
        gather_weighed(3, 0, cut, (2, 3))
        gather_weighed(3, cut, T, (1, 2, 3))
        turn_back(1, 0, T, 3, 2)
        for nb, bank in enumerate((5, 6, 7, 0)):
            output_gate(nb, bank)
        sum_parts(2, 0, T, 4)
        turn_back(2, 0, T, 4, 6)
        sum_parts(3, 0, cut, 3)
        sum_parts(3, cut, T, 5)
        turn_back(3, 0, cut, 3, 4)
        turn_back(3, cut, T, 5, 7)
        finish(0, 0, T, 1, gates[1])
        finish(1, 0, T, 2, gates[2])
        finish(2, 0, T, 6, gates[3])
        finish(3, 0, cut, 4, last_result[:, 0:cut])
        finish(3, cut, T, 7, last_result[:, cut:T])
